import numpy as np, ml_dtypes
CORES = [40,41,42,43,44,45,46,47]
N = 8
import mx_ref
BF = ml_dtypes.bfloat16
def entries(a):
    return np.ascontiguousarray(a.T).reshape(-1)
def table(e):
    return np.ascontiguousarray(np.reshape(e, (-1, 16)).T).astype(np.int32)
def cols(t, e):
    v = np.concatenate([t.reshape(128, -1, 4), np.zeros((128, 1, 4), BF)], axis=1)
    return np.ascontiguousarray(v[:, e]).reshape(128, -1)
def cut(t, i, w=512):
    return t[:, w * i:w * i + w]
def pick(q, e):
    c = np.concatenate([q[0].reshape(128, -1, 4), np.zeros((128, 1, 4), np.uint8)], axis=1); s = np.concatenate([q[1], np.ones((16, 1), np.uint8)], axis=1)
    return (np.ascontiguousarray(c[:, e].reshape(128, -1)), np.ascontiguousarray(s[:, e]))
def join(*qs):
    return (np.concatenate([q[0] for q in qs], axis=1), np.concatenate([q[1] for q in qs], axis=1))
def put(q, e, v):
    c, s = q[0].reshape(128, -1, 4).copy(), q[1].copy(); c[:, e] = v[0].reshape(128, -1, 4); s[:, e] = v[1]
    return (c.reshape(128, -1), s)
def pk(c, s):
    return (np.ascontiguousarray(c), mx_ref.live(s))
def emit(q):
    return q[0], q[1]
def decode(q):
    o = []
    for b in range(4):
        e = np.zeros((128, 128, 4), np.float32); e[np.arange(128), np.arange(128), b] = 1
        o.append(mx_ref.matmul(mx_ref.quantize(e.reshape(128, 512).astype(BF)), q))
    return np.stack(o, axis=2).reshape(128, -1)
def f(rng, *shape):
    return mx_ref.flush((rng.standard_normal(shape, dtype=np.float32) * np.exp2(rng.integers(-2, 3, shape[:-1] + (1,)))).astype(BF))
def wide(rng, *shape, cols=0):
    v = rng.standard_normal(shape, dtype=np.float32) * np.exp2(rng.integers(-12, 13, shape)).astype(np.float32)
    if cols: v *= np.repeat(np.exp2(rng.integers(-cols, cols + 1, shape[:-2] + (1, shape[-1] // 4))) * (rng.random(shape[:-2] + (1, shape[-1] // 4)) > 0.0625), 4, axis=-1).astype(np.float32)
    return mx_ref.flush(v.astype(BF))
A, M, CAPP, R, O = 384, 32, 4, 3, 2
def flat(v):
    return np.concatenate([v[r] for r in range(N)], axis=1)
def ranks(v):
    return np.ascontiguousarray(v.reshape(128, N, -1).transpose(1, 0, 2))
def trim(v):
    v = np.asarray(v).astype(np.float32)
    v[np.abs(v) < np.float32(2.0 ** -16)] = 0
    return v.astype(BF)
def lists(rng):
    return np.stack([np.stack([rng.permutation(A)[:4] for i in range(M)], axis=1) for r in range(N)])
def given(rng, d, x, b, own):
    return {"d": d, "x": x, "b": b, "act": np.stack([table(v.reshape(-1)) for v in own]), "w": f(rng, N, 128, 512 * O)}
def setup_inputs(rng):
    d, own = trim(f(rng, N, 128, 4 * A)), lists(rng)
    every, x, b = flat(d), np.zeros((N, 128, 4 * M), np.float32), np.zeros((N, 128, 4 * M), np.float32)
    for r in range(N):
        for s in range(4): x[r] += np.float32(0.25) * cols(every, A * r + own[r, s]).astype(np.float32)
    x = trim(x)
    for r in range(N):
        b[r] = x[r].astype(np.float32)
        for k in range(3):
            g = rng.integers(0, N * A, M)
            if k == 0: g = np.where(rng.random(M) < 0.25, A * r + own[r, rng.integers(0, 4, M), np.arange(M)], g)
            b[r] += np.repeat(0.5 + rng.random(M), 4).astype(np.float32) * cols(every, g).astype(np.float32)
    return given(rng, d, x, trim(b), own)
def setup_inputs_crowd(rng):
    H, small = 6, np.float32(2.0 ** -10)
    rows = rng.permutation(512)[:H * N]
    hot = np.stack([A * q + rng.permutation(A)[:H] for q in range(N)])
    v = (flat(f(rng, N, 128, 4 * A)).astype(np.float32) * np.float32(0.125)).reshape(128, N * A, 4)
    v[rows // 4, :, rows % 4] = 0
    v[rows // 4, hot.reshape(-1), rows % 4] = 64
    x = f(rng, N, 128, 4 * M).astype(np.float32).reshape(N, 128, M, 4)
    x[:, rows // 4, :, rows % 4] = 0
    b, own, rows = x.copy(), np.zeros((N, 4, M), int), rows.reshape(N, H)
    busy = int(rng.integers(0, N))
    for r in range(N):
        flood = busy if r != busy else (busy + 1) % N
        even = int(rng.choice([q for q in range(N) if q != r and q != flood]))
        n = M // 8
        who = np.full(M, flood)
        who[:n] = -1
        who[n:n + CAPP + 2] = r
        who[n + CAPP + 2:n + 2 * CAPP + 2] = even
        who = rng.permutation(who)
        cold = np.setdiff1d(np.arange(A), hot[r] - A * r)
        for i in range(M):
            q, h = r if who[i] < 0 else int(who[i]), int(rng.integers(0, H))
            own[r, :, i] = rng.permutation(cold)[:4]
            if who[i] < 0: own[r, int(rng.integers(0, 4)), i] = hot[r, h] - A * r
            b[r, rows[q, h] // 4, i, rows[q, h] % 4] = 64
            k = rows[(q + int(rng.integers(1, N))) % N, int(rng.integers(0, H))]
            b[r, k // 4, i, k % 4] = 56
    return given(rng, ranks(trim(v * small)), trim((x * small).reshape(N, 128, 4 * M)), trim((b * small).reshape(N, 128, 4 * M)), own)
def setup_inputs_edge(rng):
    k = rng.integers(1, 8, (N * A, 4))
    v = np.zeros((128, N * A, 4))
    v[:64] = 2.0 ** 28
    for j in range(4):
        g = np.sort(rng.permutation(N * A)[:2])
        k[g[0], j], k[g[1], j] = 7, 8
        v[64 + 8 * j, :, 0] = k[:, j] * 2.0 ** 20
    v[96:] = rng.standard_normal((32, N * A, 4)) * 2.0 ** 20
    x = np.zeros((N, 128, M, 4))
    x[:, 96:] = rng.standard_normal((N, 32, M, 4)) * 2.0 ** 20
    b = x.copy()
    for r in range(N):
        u = np.where(rng.permutation(M) < M // 2, 2.0 ** 28, -(2.0 ** 28))
        x[r, :64] = -u[None, :, None]
        b[r, :64] = u[None, :, None]
        b[r, 64 + 8 * rng.integers(0, 4, M), np.arange(M), 0] = 2.0 ** 22
    return given(rng, ranks(trim(v)), trim(x.reshape(N, 128, 4 * M)), trim(b.reshape(N, 128, 4 * M)), lists(rng))
def setup_inputs_ties(rng):
    P = A // 8
    base = rng.standard_normal((128, P, 4))
    base[:, 0] = 0
    of = np.zeros((N, A), int)
    for q in range(N):
        first = np.arange(q, P, N)
        have = np.flatnonzero((np.arange(P) % N <= q) & (np.arange(P) > 0))
        of[q] = rng.permutation(np.concatenate([first, rng.choice(have, A - first.size)]))
    x = trim(rng.standard_normal((N, 128, M, 4)))
    b, own = x.astype(np.float32), lists(rng)
    for r in range(N):
        n = np.bincount(of[r], minlength=P)
        n[0] = 0
        p = int(np.argmax(n))
        spots = np.flatnonzero(of[r] == p)[1:]
        want, o = rng.integers(1, P, M), rng.permutation(M)
        for i in o[:M // 2]:
            want[i] = p
            own[r, :, i] = rng.permutation(spots)[:4]
        want[o[-1]] = 0
        if r == 0: own[0, :, int(o[-1])] = np.concatenate([[0], rng.permutation(np.flatnonzero(of[0] != of[0, 0]))[:3]])
        b[r] += (4 * base[:, want]).astype(np.float32)
    return given(rng, ranks(trim(base[:, of.reshape(-1)])), x.reshape(N, 128, 4 * M), trim(b.reshape(N, 128, 4 * M)), own)
def setup_inputs_spread(rng):
    return given(rng, trim(wide(rng, N, 128, 4 * A, cols=2)), trim(wide(rng, N, 128, 4 * M, cols=2)), trim(wide(rng, N, 128, 4 * M, cols=2)), lists(rng))
def check_inputs(d):
    bad = []
    for k, lo, hi in (("d", -16, 28), ("x", -16, 28), ("b", -16, 28), ("w", -30, 30)):
        v = np.abs(d[k].astype(np.float32))
        if not (np.isfinite(v).all() and ((v == 0) | (v >= 2.0 ** lo) & (v <= 2.0 ** hi)).all()): bad.append("a value of " + k)
    for r in range(N):
        a = entries(d["act"][r])
        if a.min() < 0 or a.max() >= A: bad.append("an entry of act")
        s = np.sort(a.reshape(4, M), axis=0)
        if (s[1:] == s[:-1]).any(): bad.append("two entries of act for one point are equal")
    return bad
def reference(d, x, b, act, w):
    every = mx_ref.quantize(np.ascontiguousarray(flat(d)))
    at, goal = flat(x).astype(np.float32), flat(b).astype(np.float32)
    own = np.stack([entries(act[r]).reshape(4, M).astype(np.int64) + A * r for r in range(N)])
    wq = [[mx_ref.quantize(np.ascontiguousarray(cut(w[r], o))) for o in range(O)] for r in range(N)]
    K = -(-N * M // 128)
    every_point = np.arange(M)
    y = np.zeros((N, 128, R * O * 4 * M), np.float32)
    for t in range(R):
        e = np.concatenate([(goal - at).astype(BF), np.zeros((128, 512 * K - 4 * N * M), BF)], axis=1)
        s = np.concatenate([mx_ref.matmul(mx_ref.quantize(np.ascontiguousarray(cut(e, k))), every) for k in range(K)])
        s = s[:N * M].reshape(N, M, N * A) + np.float32(0)
        far = np.argmax(s, axis=2)
        slot = np.stack([np.argmin(s[r, every_point, own[r]], axis=0) for r in range(N)])
        worst = np.stack([own[r, slot[r], every_point] for r in range(N)])
        go = np.zeros((N, M), bool)
        for r in range(N):
            used = np.zeros(N, int)
            for i in range(M):
                g = int(far[r, i])
                if (own[r, :, i] == g).any():
                    go[r, i] = True
                elif used[g // A] < CAPP:
                    used[g // A] += 1
                    go[r, i] = True
                    own[r, slot[r, i], i] = g
        v = decode(pick(every, np.concatenate([far.reshape(-1), worst.reshape(-1)]))).reshape(128, 2, N * M, 4)
        old = at.reshape(128, N * M, 4)
        new = ((v[:, 0] - v[:, 1]) * np.float32(0.25) + old).astype(BF).astype(np.float32)
        at = np.where(go.reshape(1, -1, 1), new, old).reshape(128, -1)
        for r in range(N):
            q = pick(every, own[r].reshape(-1))
            for o in range(O):
                i = (t * O + o) * 4 * M
                y[r, :, i:i + 4 * M] = mx_ref.matmul(wq[r][o], q)
    oc, osc = np.zeros((N, 128, 16 * M), np.uint8), np.zeros((N, 16, 4 * M), np.uint8)
    for r in range(N): oc[r], osc[r] = emit(pick(every, own[r].reshape(-1)))
    return {"y": y, "px": ranks(at), "oc": oc, "osc": osc, "an": own.astype(np.float32)}

@@ -1,0 +1,567 @@
+from concourse.bass import DstId, RemoteDMATransfer
+from concourse.mybir import dt, AluOpType, AxisListType, ActivationFunctionType
+
+N, A, M, CAPP, R, O = 8, 384, 32, 4, 3, 2
+G = N // 2
+QS = 1024
+HI = QS * G
+AW = HI + A
+C8, U8, F32, BF, U16, I32 = "float8_e4m3fn_x4", "uint8", "float32", "bfloat16", "uint16", "int32"
+
+SCRATCH = {}
+
+
+def _sb(name, cols, dtype):
+    SCRATCH[name] = ("sbuf", [128, cols], dtype)
+
+
+def _mx(name, cols):
+    _sb(name + "c", cols, C8)
+    _sb(name + "s", cols, U8)
+
+
+_mx("at", AW)
+_mx("fa", 160)
+_mx("ee", 1024)
+_mx("wq", 256)
+for _t in range(R):
+    _mx("qe%d" % _t, 128)
+    _mx("eg%d" % _t, 128)
+    _mx("pk%d" % _t, 96)
+    _sb("ml%d" % _t, 16, F32)
+    _sb("ys%d" % _t, 256, F32)
+for _t in range(R + 1):
+    _mx("win%d" % _t, 256)
+    _sb("xs%d" % _t, 128, BF)
+for _n, _c, _d in (
+        ("dtile", 4 * A, BF), ("wt", 1024, BF), ("bt", 128, BF), ("et", 512, BF), ("pxs", 128, F32),
+        ("v516", 516, BF), ("ua", 516, BF), ("ub", 516, BF), ("na", 516, BF), ("nb", 516, BF),
+        ("j2", 128, F32), ("d4", 128, F32), ("kp4", 128, F32), ("am", 128, F32), ("asc", 128, F32),
+        ("neg", A, F32), ("r1", A, F32), ("r2", A, F32), ("junk", 2 * A, BF),
+        ("sm", 160, F32), ("si", 16, I32), ("acti", 8, I32), ("af", 8, F32), ("ae0", 16, F32),
+        ("zer", 32, F32), ("tm", 32, F32), ("bc", 32, F32), ("kt", 32, F32), ("qq", 40, F32), ("sc16", 16, F32),
+        ("of16", 16, F32), ("i4", 4, F32),
+        ("cu", 16, U16), ("ho", 8, U16), ("fo", 2, U16), ("ao", 2, U16), ("so", 16, U16), ("aoff", 8, U16)):
+    _sb(_n, _c, _d)
+for _n in ("z", "fb", "ab", "sb", "nn"):
+    for _s in "0123":
+        if _n != "nn" or _s in "01":
+            _sb(_n + _s, 32, F32)
+for _n in ("pd0", "pd1", "pd2", "pd3", "ps1", "ps2", "pa", "py"):
+    SCRATCH[_n] = ("psum", [128, 512], F32)
+
+SEMAPHORES = ["sv", "sa", "sp", "sg", "ls", "lx", "lb", "ld", "lw", "la", "st", "aa"]
+for _t in range(R):
+    SEMAPHORES += ["ae%d" % _t, "am%d" % _t, "ac%d" % _t, "as%d" % _t]
+
+ADD, SUB, MUL, MAX, MIN = AluOpType.add, AluOpType.subtract, AluOpType.mult, AluOpType.max, AluOpType.min
+EQ, NE, GT, LT, LE = AluOpType.is_equal, AluOpType.not_equal, AluOpType.is_gt, AluOpType.is_lt, AluOpType.is_le
+AND, SHR = AluOpType.bitwise_and, AluOpType.logical_shift_right
+X = AxisListType.X
+ACT = ActivationFunctionType
+BIG = float(2 ** 20)
+WT = 1024.0
+RQ = 1.5 * 2.0 ** 33
+RJ = 1.5 * 2.0 ** 23
+TAGN = A / QS - 1.0
+
+
+def layout(T, topo, core):
+    grp = [c for c in T.cores if topo.die(c) == topo.die(core)]
+    oth = [c for c in T.cores if topo.die(c) != topo.die(core)]
+    k = grp.index(core)
+    return grp, k, oth[k]
+
+
+def shuffle_cols(k):
+    far = [s for s in range(G) if s // 2 != k // 2]
+    return {k: 12, k ^ 1: 4, far[0]: 0, far[1]: 8}
+
+
+def places(k):
+    col = shuffle_cols(k)
+    return sorted(range(G), key=lambda s: col[s])
+
+
+def bits(es):
+    m = 0
+    for e in es:
+        m |= 1 << e
+    return m
+
+
+def splits(es):
+    q = len(es) // 4
+    return ([es[:2 * q], es[2 * q:3 * q], es[3 * q:]], [es[:q], es[q:2 * q], es[2 * q:]])
+
+
+def rank_program(g, core, T, topo):
+    rank = T.rank_of(core)
+    if rank is None:
+        return
+    grp, k, mate = layout(T, topo, core)
+    qlow = min(rank, T.rank_of(mate))
+    assert (max(rank, T.rank_of(mate)) - qlow) * QS == HI
+    own0 = 0 if rank == qlow else HI
+    col = shuffle_cols(k)
+    order = places(k)
+    peers = [grp[s] for s in range(G) if s != k]
+    Q0 = slice(32 * k, 32 * k + 32)
+    ka, kb = 32 * k, 32 * k + 32
+
+    queues = {"v": g.vector, "a": g.scalar, "p": g.tensor, "g": g, "s": g.sync}
+    semof = {"v": "sv", "a": "sa", "p": "sp", "g": "sg"}
+    count = {}
+    clock = {q: {} for q in queues}
+    wr, rd = {}, {}
+
+    def need(q, toks):
+        ck = clock[q]
+        best = {}
+        for tk in toks:
+            if ck.get(tk[0], 0) < tk[1] and best.get(tk[0], (0, 0))[1] < tk[1]:
+                best[tk[0]] = tk
+        todo = sorted(best.values(), key=lambda tk: -len(tk[2]))
+        for tk in todo:
+            if ck.get(tk[0], 0) >= tk[1]:
+                continue
+            queues[q].wait_ge(T.sem[tk[0]], tk[1])
+            for s, n in tk[2].items():
+                if ck.get(s, 0) < n:
+                    ck[s] = n
+
+    def deps(q, reads, writes):
+        toks = []
+        for key in reads:
+            assert key in wr, key
+            toks += wr[key]
+            if key[0] == "P":
+                toks += [tk for tk in rd.get(key, []) if tk[3] != q]
+        for key in writes:
+            toks += wr.get(key, []) + rd.get(key, [])
+        if q == "p":
+            toks = [tk for tk in toks if tk[3] != "p"]
+        need(q, toks)
+
+    def note(tk, reads, writes):
+        for key in reads:
+            rd.setdefault(key, []).append(tk)
+        for key in writes:
+            wr[key] = [tk]
+            rd[key] = []
+
+    def op(q, fn, reads, writes, sem=None, n=1):
+        deps(q, reads, writes)
+        sem = sem or semof[q]
+        fn().then_inc(T.sem[sem], n)
+        count[sem] = count.get(sem, 0) + n
+        ck = dict(clock[q])
+        ck[sem] = count[sem]
+        note((sem, count[sem], ck, q), reads, writes)
+
+    def arrives(sem, n, keys):
+        note((sem, n, {sem: n}, "r"), [], keys)
+
+    def send(transfers, reads):
+        deps("g", reads, [])
+        g.remote_dma_fused([t[0] for t in transfers], local_sem=T.sem.ls)
+        count["ls"] = count.get("ls", 0) + sum(t[1] for t in transfers)
+
+    def xfer(src, dsts, es, sem):
+        ids = [DstId(rid=topo.addr(c)[0], pnc=topo.addr(c)[1]) for c, _ in dsts]
+        return (RemoteDMATransfer(dst_ids=ids, dma_engine_mask=bits(es), remote_sem=T.sem[sem],
+                                  srcs=[src], dsts=[v for _, v in dsts]), len(es))
+
+    V, S, P = g.vector, g.scalar, g.tensor
+
+    def ts(out, in0, s1, s2, o0, o1, r, w):
+        if o1 is None:
+            op("v", lambda: V.tensor_scalar(out, in0, s1, None, o0), r, w)
+        else:
+            op("v", lambda: V.tensor_scalar(out, in0, s1, s2, o0, o1), r, w)
+
+    def tt(out, a, b, o, r, w):
+        op("v", lambda: V.tensor_tensor(out, a, b, o), r, w)
+
+    def cp(out, a, r, w):
+        op("v", lambda: V.tensor_copy(out, a), r, w)
+
+    def red(out, a, o, r, w):
+        op("v", lambda: V.tensor_reduce(out, a, X, o), r, w)
+
+    def tr(out, a, r, w):
+        op("v", lambda: V.transpose(out, a), r, w)
+
+    def ms(out, c, w):
+        op("v", lambda: V.memset(out, c), [], w)
+
+    def scan(out, a, b, init, o0, o1, r, w):
+        op("v", lambda: V.tensor_tensor_scan(out, a, b, init, o0, o1), r, w)
+
+    def quant(name, a, b, src, r, w):
+        op("v", lambda: V.quantize_mx(T[name + "c"][:, a:b], T[name + "s"][:, a:b], src), r, w)
+
+    def pickc(dn, a, b, sn, c, d, off, r, w):
+        cp(T[dn + "c"][:, a:b].bitcast(dt.uint32), T[sn + "c"][:, c:d].bitcast(dt.uint32).indirect(off), r, w)
+
+    def picks(dn, a, b, sn, c, d, off, r, w):
+        op("a", lambda: S.activation(T[dn + "s"][:, a:b], T[sn + "s"][:, c:d].indirect(off), ACT.Copy), r, w)
+
+    def mm(bank, ln, la, rn, ra, n, start, stop, r):
+        op("p", lambda: P.matmul_mx(T[bank][:, 0:n], T[ln + "c"][:, la:la + 128], T[ln + "s"][:, la:la + 128],
+                                    T[rn + "c"][:, ra:ra + n], T[rn + "s"][:, ra:ra + n], start, stop),
+           r, ["P" + bank])
+
+    def store(q, out, src, r):
+        op(q, lambda: queues[q].dma_start(out, src), r, [], "st", 16)
+
+    def bytes_of(name, a, b):
+        return T[name + "c"][:, a:b].bitcast(dt.uint8)
+
+    cols = {}
+
+    def c_(name, w=1):
+        if name not in cols:
+            at = sum(v[1] for v in cols.values())
+            cols[name] = (at, w)
+        at, w = cols[name]
+        return T.sm[:, at:at + w]
+
+    GL, EL, AL, RL = T.cu[:, 0:2], T.cu[:, 2:4], T.cu[:, 4:5], T.cu[:, 6:7]
+
+    def turn(n, r):
+        return [lambda: tr(T[n + "1"][:], T[n + "0"][:], r, [n + "1"]),
+                lambda: cp(T[n + "2"][:], T[n + "1"][:].indirect(GL), [n + "1", "GL"], [n + "2"]),
+                lambda: tr(T[n + "3"][:], T[n + "2"][:], [n + "2"], [n + "3"])]
+
+    def spread(dst, src, r, w):
+        for a in range(4):
+            cp(dst(slice(32 * a, 32 * a + 32)), src, r, [w + str(a)])
+
+    def four(w):
+        return [w + str(a) for a in range(4)]
+
+    def weave(*chains):
+        chains = [list(c) for c in chains]
+        while any(chains):
+            for c in chains:
+                if c:
+                    c.pop(0)()
+
+    op("s", lambda: g.sync.dma_start(T.xs0[:], T.x[:]), [], four("x0."), "lx", 16)
+    op("s", lambda: g.sync.dma_start(T.bt[:], T.b[:]), [], ["bt"], "lb", 16)
+    op("a", lambda: S.dma_start(T.dtile[:], T.d[:]), [], ["dtile"], "ld", 16)
+    g.sync.dma_start(T.acti[ka:ka + 16, :], T.act[:]).then_inc(T.sem.la, 16)
+    g.sync.dma_start(T.acti[ka + 16:kb, :], T.act[:]).then_inc(T.sem.la, 16)
+    arrives("la", 32, ["acti"])
+    op("s", lambda: g.sync.dma_start(T.wt[:], T.w[:]), [], ["wt"], "lw", 16)
+
+    def iota(out, pat, base, cm, w, small=True):
+        if small:
+            op("g", lambda: g.iota(out, pat, base, cm, allow_small_or_imprecise_dtypes=True), [], w)
+        else:
+            op("g", lambda: g.iota(out, pat, base, cm), [], w)
+
+    iota(T.si[:, 0:1], [[1, 1]], 0, 1, ["pi"], False)
+    iota(T.j2[:], [[0, 4], [1, 32]], ka, -1, ["j2"])
+    iota(T.i4[:], [[1, 4]], 0, 0, ["i4"])
+    iota(T.sc16[:, 0:8], [[32, 4], [0, 2]], 128, 0, ["sc16a"])
+    iota(T.v516[:], [[1, 129], [1000, 4]], -3000, -1, ["v516"])
+
+    ms(T.et[:], 0.0, four("et."))
+    ms(T.neg[:], -1.0e29, ["neg"])
+    ms(T.zer[:], 0.0, ["zer"])
+    for n in ("fb0", "ab0", "sb0", "nn0"):
+        ms(T[n][:], 0.0, [n, n + "a", n + "b", n + "c", n + "d"])
+    ms(T.qq[:, 32:33], -(CAPP - 0.5) * WT, ["qqc"])
+    ms(T.sc16[:, 8:16], 0.0, ["sc16b"])
+    PI = T.si[:, 0:1]
+    ts(T.si[:, 1:2], PI, 31, None, AND, None, ["pi"], ["p31"])
+    ts(T.si[:, 2:3], PI, 15, None, AND, None, ["pi"], ["p15"])
+    ts(T.si[:, 3:4], PI, 3, None, AND, None, ["pi"], ["p3"])
+    ts(T.si[:, 4:5], PI, 4, 1, SHR, AND, ["pi"], ["pg"])
+    ts(T.si[:, 5:6], PI, 1, 7, SHR, AND, ["pi"], ["ph"])
+    ts(T.si[:, 6:7], PI, 1, None, AND, None, ["pi"], ["p1"])
+    tt(T.et[:, 128 * k:128 * k + 128], T.bt[:], T.xs0[:], SUB, ["bt"] + four("x0."), four("et."))
+    quant("qe0", 0, 128, T.et[:], four("et."), ["qe0"])
+
+    def send_e(t):
+        es = topo.engines(core, peers[0])
+        n = "qe%d" % t
+        send([xfer(bytes_of(n, ka, kb), [(c, bytes_of("eg%d" % t, ka, kb)) for c in peers], es, "ae%d" % t)], [n])
+        send([xfer(T[n + "s"][:, ka:kb], [(c, T["eg%ds" % t][:, ka:kb]) for c in peers], es, "ae%d" % t)], [n])
+        arrives("ae%d" % t, sum(2 * len(topo.engines(c, core)) for c in peers), ["eg%d.r" % t])
+
+    send_e(0)
+    cp(T.cu[:, 0:1], T.si[:, 1:2], ["p31"], ["GLa"])
+    cp(T.cu[:, 2:3], T.si[:, 2:3], ["p15"], ["ELa"])
+    cp(c_("pg"), T.si[:, 4:5], ["pg"], ["pgf"])
+    cp(c_("ph"), T.si[:, 5:6], ["ph"], ["phf"])
+    cp(T.cu[:, 1:2], T.si[:, 1:2], ["p31", "GLa"], ["GL"])
+    ts(T.cu[:, 3:4], T.si[:, 2:3], 16.0, None, ADD, None, ["p15", "ELa"], ["EL"])
+    quant("at", own0, own0 + A, T.dtile[:], ["dtile"], ["at.o"])
+    es = topo.engines(core, mate)
+    send([xfer(bytes_of("at", own0, own0 + A), [(mate, bytes_of("at", own0, own0 + A))], es, "aa")], ["at.o"])
+    send([xfer(T.ats[:, own0:own0 + A], [(mate, T.ats[:, own0:own0 + A])], es, "aa")], ["at.o"])
+    arrives("aa", 2 * len(topo.engines(mate, core)), ["at.r"])
+
+    ts(AL, T.si[:, 3:4], 2.0, c_("pg"), MUL, ADD, ["p3", "pgf"], ["AL"])
+    ts(RL, T.si[:, 6:7], 16.0, c_("ph"), MUL, ADD, ["p1", "phf"], ["RL"])
+    ts(c_("k1"), T.si[:, 1:2], 1.0 / 256, float(QS * qlow) + ka / 256.0, MUL, ADD, ["p31"], ["k1"])
+    spread(lambda q: T.af[q, :], T.acti[Q0, :], ["acti"], "af")
+    J0 = T.j2[:, 0:1]
+    ts(c_("ic"), J0, -1.0, None, MUL, None, ["j2"], ["ic"])
+    cp(T.aoff[:], T.af[:], four("af"), ["aoff"])
+    ts(T.ae0[:], T.af[:].indirect(AL), c_("k1"), float(QS * (rank - qlow)), ADD, ADD, four("af") + ["AL", "k1"], ["ae0"])
+    ts(c_("i128"), J0, -1.0, 128.0, MUL, ADD, ["j2"], ["i128"])
+    pickc("win0", 128, 256, "at", own0, own0 + A, T.aoff[:], ["aoff", "at.o"], ["win0.sc"])
+    picks("win0", 128, 256, "at", own0, own0 + A, T.aoff[:], ["aoff", "at.o"], ["win0.ss"])
+    ts(T.d4[:], T.j2[:], 0.0, None, EQ, None, ["j2"], ["d4"])
+    ts(T.kp4[:], T.j2[:], 0.0, None, NE, None, ["j2"], ["kp4"])
+    ts(c_("bigu"), J0, -16384.0, 16384.0, MUL, ADD, ["j2"], ["bigu"])
+    ts(T.tm[:], T.j2[:, 0:32], 0.0, -float(2 ** 30), LE, MUL, ["j2"], ["tm"])
+    quant("fa", 32, 160, T.dtile[:, 0:512], ["dtile"], ["fa.ac", "fa.as", "fa.z"])
+    ts(T.ua[:, 0:514], T.v516[:, 1:515], 0.0, 0.25, EQ, MUL, ["v516"], ["ua"])
+    ts(T.ub[:, 0:514], T.v516[:, 0:514], 0.0, 0.25, EQ, MUL, ["v516"], ["ub"])
+    op("a", lambda: S.activation(T.na[:, 0:514], T.ua[:, 0:514], ACT.Copy, scale=-1.0), ["ua"], ["na"])
+    op("a", lambda: S.activation(T.nb[:, 0:514], T.ub[:, 0:514], ACT.Copy, scale=-1.0), ["ub"], ["nb"])
+
+    def own_e(t):
+        pickc("eg%d" % t, ka, kb, "qe%d" % t, ka, kb, EL, ["EL", "qe%d" % t], ["eg%d.c" % t])
+        picks("eg%d" % t, ka, kb, "qe%d" % t, ka, kb, EL, ["EL", "qe%d" % t], ["eg%d.s" % t])
+
+    def act_e(t):
+        return (T.ae0[:, 0:4], "ae0") if t == 0 else (c_("ae%d" % t, 4), "ae%d" % t)
+
+    def a_mm(t):
+        mm("pa", "qe%d" % t, 0, "win%d" % t, 128, 128, True, True, ["qe%d" % t, "win%d.sc" % t, "win%d.ss" % t])
+
+    AS = T.asc[:, 31:128:32]
+
+    def a_chain():
+        return [
+            lambda: tt(T.am[:], T.pa[:, 0:128], T.d4[:], MUL, ["Ppa", "d4"], ["am"]),
+            lambda: scan(T.asc[:], T.kp4[:], T.am[:], 0.0, MUL, ADD, ["kp4", "am"], ["asc"]),
+            lambda: red(c_("amin"), AS, MIN, ["asc"], ["amin"]),
+            lambda: ts(c_("ta", 4), AS, c_("amin"), 8.0, GT, MUL, ["asc", "amin"], ["ta"]),
+            lambda: tt(c_("ua", 4), c_("ta", 4), T.i4[:], ADD, ["ta", "i4"], ["ua4"]),
+            lambda: red(c_("aslot"), c_("ua", 4), MIN, ["ua4"], ["aslot"])]
+
+    def best_active(t):
+        ae, key = act_e(t)
+        return [
+            lambda: red(c_("amax"), AS, MAX, ["asc"], ["amax"]),
+            lambda: ts(c_("tb", 4), AS, c_("amax"), BIG, LT, MUL, ["asc", "amax"], ["tb"]),
+            lambda: tt(c_("ub", 4), c_("tb", 4), ae, ADD, ["tb", key], ["ub4"]),
+            lambda: red(c_("amaxe"), c_("ub", 4), MIN, ["ub4"], ["amaxe"]),
+            lambda: ts(c_("amask", 4), T.i4[:], c_("aslot"), None, EQ, None, ["i4", "aslot"], ["amask"]),
+            lambda: ts(c_("apos"), c_("aslot"), 32.0, c_("i128"), MUL, ADD, ["aslot", "i128"], ["apos"])]
+
+    def a_pick(t):
+        w = "win%d" % t
+        return ([lambda: ts(T.ab0[:, 0:1], c_("aslot"), 32.0, c_("ic"), MUL, ADD, ["aslot", "ic"], ["ab0a"]),
+                 lambda: ts(T.ab0[:, 16:17], c_("aslot"), 32.0, c_("ic"), MUL, ADD, ["aslot", "ic"], ["ab0b"])]
+                + turn("ab", ["ab0", "ab0a", "ab0b"])
+                + [lambda: spread(lambda q: T.ao[q, :], T.ab3[Q0, 0:32:16], ["ab3"], "ao"),
+                   lambda: pickc("fa", 32, 64, w, 128, 256, T.ao[:], four("ao") + [w + ".sc"], ["fa.ac"]),
+                   lambda: picks("fa", 32, 64, w, 128, 256, T.ao[:], four("ao") + [w + ".ss"], ["fa.as"])])
+
+    def y_mm(t):
+        w = "win%d" % (t + 1)
+        for o, bank in enumerate(("py", "pa")):
+            mm(bank, "wq", 128 * o, w, 128, 128, True, True, ["wq", w + ".sc", w + ".ss"])
+
+    def y_out(t, q):
+        ys = T["ys%d" % t]
+        for o, bank in enumerate(("py", "pa")):
+            op("a", lambda: S.activation(ys[:, 128 * o:128 * o + 128], T[bank][:, 0:128], ACT.Copy),
+               ["P" + bank], ["ys%d.%d" % (t, o)])
+        store(q, T.y[:, 256 * t:256 * t + 256], ys[:], ["ys%d.0" % t, "ys%d.1" % t])
+
+    def slot_list(with_f):
+        n = 10 if with_f else 8
+        return ([lambda: ts(c_("ds"), c_("xx"), c_("cd"), 0.0, MAX, MIN, ["xx", "cd"], ["ds"]),
+                 lambda: ts(T.sb0[:, 0:4], c_("amask", 4), c_("ds"), c_("ic"), MUL, ADD, ["amask", "ds", "ic"], ["sb0a"]),
+                 lambda: ts(T.sb0[:, 16:20], c_("amask", 4), c_("ds"), c_("ic"), MUL, ADD, ["amask", "ds", "ic"], ["sb0b"])]
+                + turn("sb", ["sb0", "sb0a", "sb0b", "sb0c", "sb0d"])
+                + [lambda: tt(T.of16[:], T.sb3[:].indirect(RL), T.sc16[:], ADD, ["sb3", "RL", "sc16a", "sc16b"], ["of16"]),
+                   lambda: spread(lambda q: T.so[q, 0:n], T.of16[Q0, 0:n], ["of16"], "so")])
+
+    def window(t):
+        w = "win%d" % t
+        return [w + ".sc", w + ".oc", w + ".rc"], [w + ".ss", w + ".os", w + ".rs"]
+
+    def slot_pick(t):
+        w, w2 = "win%d" % t, "win%d" % (t + 1)
+        rc, rs = window(t)
+        pickc(w2, 128, 256, w, 0, 256, T.so[:, 0:8], four("so") + rc, [w2 + ".sc"])
+        picks(w2, 128, 256, w, 0, 256, T.so[:, 0:8], four("so") + rs, [w2 + ".ss"])
+
+    def renew(old, okey, diff, dkey, new, nkey):
+        return [lambda: ts(c_("m2", 4), c_("amask", 4), c_("ds"), 0.0, MUL, LT, ["amask", "ds"], ["m2"]),
+                lambda: tt(c_("dd", 4), c_("m2", 4), diff, MUL, ["m2", dkey], ["dd"]),
+                lambda: tt(new, old, c_("dd", 4), ADD, [okey, "dd"], [nkey])]
+
+    def unit(b, neg):
+        src = (("ua", "ub"), ("na", "nb"))[neg][b % 2]
+        st = 2 if b < 2 else 0
+        at = 512 * neg + 128 * b
+        return lambda: quant("ee", at, at + 128, T[src][:, st:st + 512], [src], ["ee%d" % (4 * neg + b)])
+
+    own_e(0)
+    a_mm(0)
+    weave([unit(b, 0) for b in range(4)])
+    weave(a_chain(), [unit(b, 1) for b in range(4)])
+    quant("wq", 0, 256, T.wt[:], ["wt"], ["wq"])
+
+    for t in range(R):
+        last = t == R - 1
+        ml, mk, eg, w, pk = T["ml%d" % t], "ml%d" % t, "eg%d" % t, "win%d" % t, "pk%d" % t
+        egk = [eg + ".c", eg + ".s", eg + ".r"]
+        lowk, highk = ("at.o", "at.r") if own0 == 0 else ("at.r", "at.o")
+        mm("ps1", eg, 0, "at", 0, A, True, True, egk + [lowk])
+        mm("ps2", eg, 0, "at", HI, A, True, True, egk + [highk])
+        if t > 0:
+            y_mm(t - 1)
+        M1, M2 = T.r1[:, A - 1:A], T.r2[:, A - 1:A]
+        C2 = ml[:, 4 * k + 2:4 * k + 3]
+        scan(T.r1[:], T.ps1[:, 0:A], T.neg[:], -1.0e29, MAX, MAX, ["Pps1", "neg"], ["r1"])
+        scan(T.r2[:], T.ps2[:, 0:A], T.neg[:], M1, MAX, MAX, ["Pps2", "neg", "r1"], ["r2"])
+        op("a", lambda: S.activation(T.junk[:, 0:A], T.r1[:], ACT.Sign, bias=M1, scale=-1.0, accum_out=c_("c1")),
+           ["r1"], ["c1", "junk1"])
+        op("a", lambda: S.activation(T.junk[:, A:2 * A], T.r2[:], ACT.Sign, bias=M2, scale=-1.0, accum_out=C2),
+           ["r2"], [mk + ".c", "junk2"])
+        ts(c_("gb"), M2, M1, float(HI), GT, MUL, ["r1", "r2"], ["gb"])
+        cp(ml[:, 4 * k:4 * k + 1], M2, ["r2"], [mk + ".m"])
+        ts(ml[:, 4 * k + 1:4 * k + 2], c_("gb"), c_("c1"), c_("k1"), MAX, ADD, ["gb", "c1", "k1"], [mk + ".e"])
+        ts(c_("rest"), c_("gb"), c_("c1"), None, MAX, None, ["gb", "c1"], ["rest"])
+        mine = [mk + ".m", mk + ".e", mk + ".c"]
+        mv = ml[:, 4 * k:4 * k + 3]
+        send([xfer(mv, [(c, mv) for c in peers], topo.engines(core, peers[0]), "am%d" % t)], mine)
+        arrives("am%d" % t, sum(len(topo.engines(c, core)) for c in peers), [mk + ".r"])
+        ts(T.z0[:], T.zer[:], C2, c_("rest"), ADD, ADD, ["zer", mk + ".c", "rest"], ["z0"] + four("z.") + ["zz0", "zz1"])
+        for s in range(G):
+            o = s ^ 1
+            cp(T.z0[32 * o:32 * o + 32, col[s]:32:16], T.z0[32 * s:32 * s + 32, col[s]:32:16], ["z0"], ["z.%d" % s])
+        for h in range(2):
+            a = min(col[2 * h], col[2 * h + 1])
+            cp(T.z0[64 - 64 * h:128 - 64 * h, a:32:8], T.z0[64 * h:64 * h + 64, a:32:8],
+               ["z.%d" % (2 * h), "z.%d" % (2 * h + 1)], ["zz%d" % h])
+        weave(turn("z", ["z0"] + four("z.") + ["zz0", "zz1"]))
+        cp(T.ho[:, 0:8:2], T.z3[:, 0:16:4], ["z3"], ["ho0"])
+        cp(T.ho[:, 1:8:2], T.z3[:, 16:32:4], ["z3"], ["ho1"])
+        hk = ["ho0", "ho1", "at.o", "at.r"]
+        pickc(pk, 0, 96, "at", 0, AW, T.ho[:, 0:6], hk, [pk + ".c"])
+        picks(pk, 0, 96, "at", 0, AW, T.ho[:, 0:6], hk, [pk + ".s"])
+        ec, esc = splits(topo.engines(core, peers[0]))
+        send([xfer(bytes_of(pk, 32 * i, 32 * i + 32), [(grp[order[i]], bytes_of(w, ka, kb))], ec[i], "ac%d" % t)
+              for i in range(3)], [pk + ".c"])
+        send([xfer(T[pk + "s"][:, 32 * i:32 * i + 32], [(grp[order[i]], T[w + "s"][:, ka:kb])], esc[i], "as%d" % t)
+              for i in range(3)], [pk + ".s"])
+        for j, nm, key in ((0, "ac", ".rc"), (1, "as", ".rs")):
+            arrives("%s%d" % (nm, t), sum(len(splits(topo.engines(grp[s], core))[j][places(s).index(k)])
+                                          for s in range(G) if s != k), [w + key])
+        pickc(w, ka, kb, "at", 0, AW, T.ho[:, 6:8], hk, [w + ".oc"])
+        picks(w, ka, kb, "at", 0, AW, T.ho[:, 6:8], hk, [w + ".os"])
+        weave(a_pick(t), best_active(t))
+        for b in range(4):
+            mm("pd%d" % b, "ee", 512 + 128 * b, "fa", 32, 128, True, False, ["ee%d" % (4 + b), "fa.ac", "fa.as", "fa.z"])
+        if t > 0:
+            y_out(t - 1, "s")
+        ae, aek = act_e(t)
+        if last:
+            ts(c_("k4", 4), ae, RQ, RQ, ADD, SUB, [aek], ["k4"])
+            ts(c_("j4", 4), ae, RJ, RJ, ADD, SUB, [aek], ["j4"])
+            ts(c_("k5", 4), c_("k4", 4), TAGN, None, MUL, None, ["k4"], ["k5"])
+            tt(c_("no", 4), c_("k5", 4), c_("j4", 4), ADD, ["k5", "j4"], ["no"])
+        allm = mine + [mk + ".r"]
+        SC = ml[:, 0:16:4]
+        EM = c_("em")
+        red(c_("best"), SC, MAX, allm, ["best"])
+        tt(c_("e4", 4), ml[:, 1:16:4], ml[:, 2:16:4], ADD, allm, ["e4"])
+        ts(c_("t4", 4), SC, c_("best"), BIG, LT, MUL, allm + ["best"], ["t4"])
+        tt(c_("u4", 4), c_("t4", 4), c_("e4", 4), ADD, ["t4", "e4"], ["u4"])
+        red(EM, c_("u4", 4), MIN, ["u4"], ["em"])
+        ts(c_("hh"), EM, c_("amaxe"), c_("bigu"), EQ, MUL, ["em", "amaxe", "bigu"], ["hh"])
+        ts(c_("key"), EM, RQ, RQ, ADD, SUB, ["em"], ["key"])
+        ts(T.bc[:], T.tm[:], c_("key"), c_("hh"), ADD, ADD, ["tm", "key", "hh"], ["bc"])
+        tt(c_("kp"), c_("key"), c_("hh"), ADD, ["key", "hh"], ["kp"])
+        tr(T.kt[:], T.bc[:], ["bc"], ["kt"])
+        ts(c_("jr"), EM, RJ, RJ, ADD, SUB, ["em"], ["jr"])
+        ts(T.qq[:, 0:32], T.kt[:], c_("kp"), WT, EQ, MUL, ["kt", "kp"], ["qq"])
+        ts(c_("cpv"), EM, c_("jr"), 256.0, SUB, MUL, ["em", "jr"], ["cpv"])
+        red(c_("xx"), T.qq[:, 0:33], ADD, ["qq", "qqc"], ["xx"])
+        rc, rs = window(t)
+
+        def fpos(out, key):
+            ts(out, c_("xx"), c_("cpv"), c_("apos"), MAX, MIN, ["xx", "cpv", "apos"], [key])
+
+        def gap():
+            ts(c_("cd"), c_("cpv"), c_("apos"), c_("hh"), SUB, ADD, ["cpv", "apos", "hh"], ["cd"])
+
+        if not last:
+            fpos(T.fb0[:, 0:1], "fb0a")
+            fpos(T.fb0[:, 16:17], "fb0b")
+            weave(turn("fb", ["fb0", "fb0a", "fb0b"]))
+            spread(lambda q: T.fo[q, :], T.fb3[Q0, 0:32:16], ["fb3"], "fo")
+            fo, fk = T.fo[:], four("fo")
+        else:
+            gap()
+            sl = slot_list(True)
+            weave(sl[:1], [lambda: fpos(T.sb0[:, 4:5], "sb0c")])
+            weave(sl[1:3], [lambda: fpos(T.sb0[:, 20:21], "sb0d")])
+            weave(sl[3:])
+            fo, fk = T.so[:, 8:10], four("so")
+        pickc("fa", 0, 32, w, 0, 256, fo, fk + rc, ["fa.fc"])
+        picks("fa", 0, 32, w, 0, 256, fo, fk + rs, ["fa.fs"])
+        for b in range(4):
+            mm("pd%d" % b, "ee", 128 * b, "fa", 0, 128, False, True,
+               ["ee%d" % b, "fa.fc", "fa.fs", "fa.ac", "fa.as", "fa.z"])
+        xo, xn = T["xs%d" % t], T["xs%d" % (t + 1)]
+
+        def x_new(b):
+            tt(xn[:, b:128:4], T["pd%d" % b][:, 0:32], xo[:, b:128:4], ADD, ["Ppd%d" % b, "x%d.%d" % (t, b)],
+               ["x%d.%d" % (t + 1, b)])
+
+        def e_new(b):
+            tt(T.et[:, 128 * k + b:128 * k + 128:4], T.bt[:, b:128:4], xn[:, b:128:4], SUB,
+               ["bt", "x%d.%d" % (t + 1, b)], ["et.%d" % b])
+
+        if not last:
+            gap()
+            ts(c_("de", 4), ae, -1.0, EM, MUL, ADD, [aek, "em"], ["de"])
+            x_new(0)
+            for b in range(1, 4):
+                x_new(b)
+                e_new(b - 1)
+            e_new(3)
+            quant("qe%d" % (t + 1), 0, 128, T.et[:], four("et."), ["qe%d" % (t + 1)])
+            send_e(t + 1)
+            own_e(t + 1)
+            sl = slot_list(False)
+            weave(sl[:1])
+            weave(sl[1:], renew(ae, aek, c_("de", 4), "de", act_e(t + 1)[0], act_e(t + 1)[1]))
+            slot_pick(t)
+            a_mm(t + 1)
+            weave(a_chain())
+        else:
+            wl = "win%d" % R
+            slot_pick(t)
+            y_mm(t)
+            store("s", T.oc[:], bytes_of(wl, 128, 256), [wl + ".sc"])
+            for a in range(4):
+                store("s" if a < 2 else "a", T.osc[4 * a:4 * a + 4, :], T[wl + "s"][32 * a:32 * a + 4, 128:256], [wl + ".ss"])
+            ts(c_("fn"), c_("key"), TAGN, c_("jr"), MUL, ADD, ["key", "jr"], ["fn"])
+            rn = renew(c_("no", 4), "no", c_("de", 4), "de", T.nn0[:, 0:4], "nn0a")
+            rn[0]()
+            ts(c_("de", 4), c_("no", 4), -1.0, c_("fn"), MUL, ADD, ["no", "fn"], ["de"])
+            weave([lambda b=b: x_new(b) for b in range(4)], rn[1:])
+            cp(T.pxs[:], xn[:], four("x%d." % R), ["pxs"])
+            tr(T.nn1[:], T.nn0[:], ["nn0", "nn0a"], ["nn1"])
+            store("s", T.px[:], T.pxs[:], ["pxs"])
+            store("s", T.an[:], T.nn1[ka:ka + 4, :], ["nn1"])
+            y_out(t, "a")
+
+    for s in ("sv", "sa", "sp", "sg", "ls"):
+        g.wait_ge(T.sem[s], count[s])
+    g.sync.wait_ge(T.sem.st, count["st"])

@@ -40,10 +40,10 @@ for _n, _c, _d in (
         ("neg", A, F32), ("r1", A, F32), ("r2", A, F32), ("junk", 2 * A, BF),
         ("sm", 160, F32), ("si", 16, I32), ("acti", 8, I32), ("af", 8, F32), ("ae0", 16, F32),
         ("zer", 32, F32), ("tm", 32, F32), ("bc", 32, F32), ("kt", 32, F32), ("qq", 40, F32), ("sc16", 16, F32),
-        ("of16", 16, F32), ("i4", 4, F32),
-        ("cu", 16, U16), ("ho", 8, U16), ("fo", 2, U16), ("ao", 2, U16), ("so", 16, U16), ("aoff", 8, U16)):
+        ("sc8", 8, F32), ("of16", 16, F32), ("i8", 8, F32),
+        ("cu", 16, U16), ("ho", 16, U16), ("so", 16, U16), ("aoff", 8, U16)):
     _sb(_n, _c, _d)
-for _n in ("z", "fb", "ab", "sb", "nn"):
+for _n in ("z", "sb", "nn"):
     for _s in "0123":
         if _n != "nn" or _s in "01":
             _sb(_n + _s, 32, F32)
@@ -230,9 +230,9 @@ def rank_program(g, core, T, topo):
     GL, EL, AL, RL = T.cu[:, 0:2], T.cu[:, 2:4], T.cu[:, 4:5], T.cu[:, 6:7]
 
     def turn(n, r):
-        return [lambda: tr(T[n + "1"][:], T[n + "0"][:], r, [n + "1"]),
-                lambda: cp(T[n + "2"][:], T[n + "1"][:].indirect(GL), [n + "1", "GL"], [n + "2"]),
-                lambda: tr(T[n + "3"][:], T[n + "2"][:], [n + "2"], [n + "3"])]
+        tr(T[n + "1"][:], T[n + "0"][:], r, [n + "1"])
+        cp(T[n + "2"][:], T[n + "1"][:].indirect(GL), [n + "1", "GL"], [n + "2"])
+        tr(T[n + "3"][:], T[n + "2"][:], [n + "2"], [n + "3"])
 
     def spread(dst, src, r, w):
         for a in range(4):
@@ -264,14 +264,14 @@ def rank_program(g, core, T, topo):
 
     iota(T.si[:, 0:1], [[1, 1]], 0, 1, ["pi"], False)
     iota(T.j2[:], [[0, 4], [1, 32]], ka, -1, ["j2"])
-    iota(T.i4[:], [[1, 4]], 0, 0, ["i4"])
-    iota(T.sc16[:, 0:8], [[32, 4], [0, 2]], 128, 0, ["sc16a"])
+    iota(T.i8[:], [[0, 2], [1, 4]], 0, 0, ["i8"])
+    iota(T.sc8[:], [[32, 4], [16, 2]], 128, 0, ["sc8"])
     iota(T.v516[:], [[1, 129], [1000, 4]], -3000, -1, ["v516"])
 
     ms(T.et[:], 0.0, four("et."))
     ms(T.neg[:], -1.0e29, ["neg"])
     ms(T.zer[:], 0.0, ["zer"])
-    for n in ("fb0", "ab0", "sb0", "nn0"):
+    for n in ("sb0", "nn0"):
         ms(T[n][:], 0.0, [n, n + "a", n + "b", n + "c", n + "d"])
     ms(T.qq[:, 32:33], -(CAPP - 0.5) * WT, ["qqc"])
     ms(T.sc16[:, 8:16], 0.0, ["sc16b"])
@@ -280,8 +280,9 @@ def rank_program(g, core, T, topo):
     ts(T.si[:, 2:3], PI, 15, None, AND, None, ["pi"], ["p15"])
     ts(T.si[:, 3:4], PI, 3, None, AND, None, ["pi"], ["p3"])
     ts(T.si[:, 4:5], PI, 4, 1, SHR, AND, ["pi"], ["pg"])
-    ts(T.si[:, 5:6], PI, 1, 7, SHR, AND, ["pi"], ["ph"])
+    ts(T.si[:, 5:6], PI, 1, 3, SHR, AND, ["pi"], ["ph"])
     ts(T.si[:, 6:7], PI, 1, None, AND, None, ["pi"], ["p1"])
+    ts(T.si[:, 7:8], PI, 3, 1, SHR, AND, ["pi"], ["p8"])
     tt(T.et[:, 128 * k:128 * k + 128], T.bt[:], T.xs0[:], SUB, ["bt"] + four("x0."), four("et."))
     quant("qe0", 0, 128, T.et[:], four("et."), ["qe0"])
 
@@ -296,7 +297,8 @@ def rank_program(g, core, T, topo):
     cp(T.cu[:, 0:1], T.si[:, 1:2], ["p31"], ["GLa"])
     cp(T.cu[:, 2:3], T.si[:, 2:3], ["p15"], ["ELa"])
     cp(c_("pg"), T.si[:, 4:5], ["pg"], ["pgf"])
-    cp(c_("ph"), T.si[:, 5:6], ["ph"], ["phf"])
+    cp(c_("p8"), T.si[:, 7:8], ["p8"], ["p8f"])
+    cp(c_("p15"), T.si[:, 2:3], ["p15"], ["p15f"])
     cp(T.cu[:, 1:2], T.si[:, 1:2], ["p31", "GLa"], ["GL"])
     ts(T.cu[:, 3:4], T.si[:, 2:3], 16.0, None, ADD, None, ["p15", "ELa"], ["EL"])
     quant("at", own0, own0 + A, T.dtile[:], ["dtile"], ["at.o"])
@@ -306,11 +308,11 @@ def rank_program(g, core, T, topo):
     arrives("aa", 2 * len(topo.engines(mate, core)), ["at.r"])
 
     ts(AL, T.si[:, 3:4], 2.0, c_("pg"), MUL, ADD, ["p3", "pgf"], ["AL"])
-    ts(RL, T.si[:, 6:7], 16.0, c_("ph"), MUL, ADD, ["p1", "phf"], ["RL"])
+    ts(c_("rl"), T.si[:, 5:6], 4.0, c_("p8"), MUL, ADD, ["ph", "p8f"], ["rl"])
     ts(c_("k1"), T.si[:, 1:2], 1.0 / 256, float(QS * qlow) + ka / 256.0, MUL, ADD, ["p31"], ["k1"])
     spread(lambda q: T.af[q, :], T.acti[Q0, :], ["acti"], "af")
     J0 = T.j2[:, 0:1]
-    ts(c_("ic"), J0, -1.0, None, MUL, None, ["j2"], ["ic"])
+    ts(RL, T.si[:, 6:7], 16.0, c_("rl"), MUL, ADD, ["p1", "rl"], ["RL"])
     cp(T.aoff[:], T.af[:], four("af"), ["aoff"])
     ts(T.ae0[:], T.af[:].indirect(AL), c_("k1"), float(QS * (rank - qlow)), ADD, ADD, four("af") + ["AL", "k1"], ["ae0"])
     ts(c_("i128"), J0, -1.0, 128.0, MUL, ADD, ["j2"], ["i128"])
@@ -320,7 +322,8 @@ def rank_program(g, core, T, topo):
     ts(T.kp4[:], T.j2[:], 0.0, None, NE, None, ["j2"], ["kp4"])
     ts(c_("bigu"), J0, -16384.0, 16384.0, MUL, ADD, ["j2"], ["bigu"])
     ts(T.tm[:], T.j2[:, 0:32], 0.0, -float(2 ** 30), LE, MUL, ["j2"], ["tm"])
-    quant("fa", 32, 160, T.dtile[:, 0:512], ["dtile"], ["fa.ac", "fa.as", "fa.z"])
+    ts(T.sc16[:, 0:8], T.sc8[:], c_("p15"), None, ADD, None, ["sc8", "p15f"], ["sc16a"])
+    quant("fa", 32, 160, T.dtile[:, 0:512], ["dtile"], ["fa.c", "fa.s", "fa.z"])
     ts(T.ua[:, 0:514], T.v516[:, 1:515], 0.0, 0.25, EQ, MUL, ["v516"], ["ua"])
     ts(T.ub[:, 0:514], T.v516[:, 0:514], 0.0, 0.25, EQ, MUL, ["v516"], ["ub"])
     op("a", lambda: S.activation(T.na[:, 0:514], T.ua[:, 0:514], ACT.Copy, scale=-1.0), ["ua"], ["na"])
@@ -338,14 +341,20 @@ def rank_program(g, core, T, topo):
 
     AS = T.asc[:, 31:128:32]
 
-    def a_chain():
+    def a_scores():
         return [
             lambda: tt(T.am[:], T.pa[:, 0:128], T.d4[:], MUL, ["Ppa", "d4"], ["am"]),
-            lambda: scan(T.asc[:], T.kp4[:], T.am[:], 0.0, MUL, ADD, ["kp4", "am"], ["asc"]),
+            lambda: scan(T.asc[:], T.kp4[:], T.am[:], 0.0, MUL, ADD, ["kp4", "am"], ["asc"])]
+
+    def a_chain():
+        return [
             lambda: red(c_("amin"), AS, MIN, ["asc"], ["amin"]),
             lambda: ts(c_("ta", 4), AS, c_("amin"), 8.0, GT, MUL, ["asc", "amin"], ["ta"]),
-            lambda: tt(c_("ua", 4), c_("ta", 4), T.i4[:], ADD, ["ta", "i4"], ["ua4"]),
-            lambda: red(c_("aslot"), c_("ua", 4), MIN, ["ua4"], ["aslot"])]
+            lambda: tt(c_("ua", 4), c_("ta", 4), T.i8[:, 0:4], ADD, ["ta", "i8"], ["ua4"]),
+            lambda: red(c_("aslot"), c_("ua", 4), MIN, ["ua4"], ["aslot"]),
+            lambda: ts(c_("apos"), c_("aslot"), 32.0, c_("i128"), MUL, ADD, ["aslot", "i128"], ["apos"]),
+            lambda: ts(c_("nm", 8), T.i8[:], c_("aslot"), BIG, NE, MUL, ["i8", "aslot"], ["nm"]),
+            lambda: ts(T.sb0[:, 5:32:16], T.zer[:, 0:2], c_("apos"), None, ADD, None, ["zer", "apos"], ["sb0d"])]
 
     def best_active(t):
         ae, key = act_e(t)
@@ -353,18 +362,7 @@ def rank_program(g, core, T, topo):
             lambda: red(c_("amax"), AS, MAX, ["asc"], ["amax"]),
             lambda: ts(c_("tb", 4), AS, c_("amax"), BIG, LT, MUL, ["asc", "amax"], ["tb"]),
             lambda: tt(c_("ub", 4), c_("tb", 4), ae, ADD, ["tb", key], ["ub4"]),
-            lambda: red(c_("amaxe"), c_("ub", 4), MIN, ["ub4"], ["amaxe"]),
-            lambda: ts(c_("amask", 4), T.i4[:], c_("aslot"), None, EQ, None, ["i4", "aslot"], ["amask"]),
-            lambda: ts(c_("apos"), c_("aslot"), 32.0, c_("i128"), MUL, ADD, ["aslot", "i128"], ["apos"])]
-
-    def a_pick(t):
-        w = "win%d" % t
-        return ([lambda: ts(T.ab0[:, 0:1], c_("aslot"), 32.0, c_("ic"), MUL, ADD, ["aslot", "ic"], ["ab0a"]),
-                 lambda: ts(T.ab0[:, 16:17], c_("aslot"), 32.0, c_("ic"), MUL, ADD, ["aslot", "ic"], ["ab0b"])]
-                + turn("ab", ["ab0", "ab0a", "ab0b"])
-                + [lambda: spread(lambda q: T.ao[q, :], T.ab3[Q0, 0:32:16], ["ab3"], "ao"),
-                   lambda: pickc("fa", 32, 64, w, 128, 256, T.ao[:], four("ao") + [w + ".sc"], ["fa.ac"]),
-                   lambda: picks("fa", 32, 64, w, 128, 256, T.ao[:], four("ao") + [w + ".ss"], ["fa.as"])])
+            lambda: red(c_("amaxe"), c_("ub", 4), MIN, ["ub4"], ["amaxe"])]
 
     def y_mm(t):
         w = "win%d" % (t + 1)
@@ -378,15 +376,6 @@ def rank_program(g, core, T, topo):
                ["P" + bank], ["ys%d.%d" % (t, o)])
         store(q, T.y[:, 256 * t:256 * t + 256], ys[:], ["ys%d.0" % t, "ys%d.1" % t])
 
-    def slot_list(with_f):
-        n = 10 if with_f else 8
-        return ([lambda: ts(c_("ds"), c_("xx"), c_("cd"), 0.0, MAX, MIN, ["xx", "cd"], ["ds"]),
-                 lambda: ts(T.sb0[:, 0:4], c_("amask", 4), c_("ds"), c_("ic"), MUL, ADD, ["amask", "ds", "ic"], ["sb0a"]),
-                 lambda: ts(T.sb0[:, 16:20], c_("amask", 4), c_("ds"), c_("ic"), MUL, ADD, ["amask", "ds", "ic"], ["sb0b"])]
-                + turn("sb", ["sb0", "sb0a", "sb0b", "sb0c", "sb0d"])
-                + [lambda: tt(T.of16[:], T.sb3[:].indirect(RL), T.sc16[:], ADD, ["sb3", "RL", "sc16a", "sc16b"], ["of16"]),
-                   lambda: spread(lambda q: T.so[q, 0:n], T.of16[Q0, 0:n], ["of16"], "so")])
-
     def window(t):
         w = "win%d" % t
         return [w + ".sc", w + ".oc", w + ".rc"], [w + ".ss", w + ".os", w + ".rs"]
@@ -398,7 +387,7 @@ def rank_program(g, core, T, topo):
         picks(w2, 128, 256, w, 0, 256, T.so[:, 0:8], four("so") + rs, [w2 + ".ss"])
 
     def renew(old, okey, diff, dkey, new, nkey):
-        return [lambda: ts(c_("m2", 4), c_("amask", 4), c_("ds"), 0.0, MUL, LT, ["amask", "ds"], ["m2"]),
+        return [lambda: ts(c_("m2", 4), T.sb0[:, 0:16:4], 0.0, None, LT, None, ["sb0a"], ["m2"]),
                 lambda: tt(c_("dd", 4), c_("m2", 4), diff, MUL, ["m2", dkey], ["dd"]),
                 lambda: tt(new, old, c_("dd", 4), ADD, [okey, "dd"], [nkey])]
 
@@ -411,7 +400,7 @@ def rank_program(g, core, T, topo):
     own_e(0)
     a_mm(0)
     weave([unit(b, 0) for b in range(4)])
-    weave(a_chain(), [unit(b, 1) for b in range(4)])
+    weave(a_scores() + a_chain(), [unit(b, 1) for b in range(2)] + best_active(0) + [unit(b, 1) for b in range(2, 4)])
     quant("wq", 0, 256, T.wt[:], ["wt"], ["wq"])
 
     for t in range(R):
@@ -447,10 +436,9 @@ def rank_program(g, core, T, topo):
             a = min(col[2 * h], col[2 * h + 1])
             cp(T.z0[64 - 64 * h:128 - 64 * h, a:32:8], T.z0[64 * h:64 * h + 64, a:32:8],
                ["z.%d" % (2 * h), "z.%d" % (2 * h + 1)], ["zz%d" % h])
-        weave(turn("z", ["z0"] + four("z.") + ["zz0", "zz1"]))
-        cp(T.ho[:, 0:8:2], T.z3[:, 0:16:4], ["z3"], ["ho0"])
-        cp(T.ho[:, 1:8:2], T.z3[:, 16:32:4], ["z3"], ["ho1"])
-        hk = ["ho0", "ho1", "at.o", "at.r"]
+        turn("z", ["z0"] + four("z.") + ["zz0", "zz1"])
+        cp(T.ho[:], T.z3[:].indirect(RL), ["z3", "RL"], ["ho"])
+        hk = ["ho", "at.o", "at.r"]
         pickc(pk, 0, 96, "at", 0, AW, T.ho[:, 0:6], hk, [pk + ".c"])
         picks(pk, 0, 96, "at", 0, AW, T.ho[:, 0:6], hk, [pk + ".s"])
         ec, esc = splits(topo.engines(core, peers[0]))
@@ -463,17 +451,9 @@ def rank_program(g, core, T, topo):
                                           for s in range(G) if s != k), [w + key])
         pickc(w, ka, kb, "at", 0, AW, T.ho[:, 6:8], hk, [w + ".oc"])
         picks(w, ka, kb, "at", 0, AW, T.ho[:, 6:8], hk, [w + ".os"])
-        weave(a_pick(t), best_active(t))
-        for b in range(4):
-            mm("pd%d" % b, "ee", 512 + 128 * b, "fa", 32, 128, True, False, ["ee%d" % (4 + b), "fa.ac", "fa.as", "fa.z"])
         if t > 0:
             y_out(t - 1, "s")
         ae, aek = act_e(t)
-        if last:
-            ts(c_("k4", 4), ae, RQ, RQ, ADD, SUB, [aek], ["k4"])
-            ts(c_("j4", 4), ae, RJ, RJ, ADD, SUB, [aek], ["j4"])
-            ts(c_("k5", 4), c_("k4", 4), TAGN, None, MUL, None, ["k4"], ["k5"])
-            tt(c_("no", 4), c_("k5", 4), c_("j4", 4), ADD, ["k5", "j4"], ["no"])
         allm = mine + [mk + ".r"]
         SC = ml[:, 0:16:4]
         EM = c_("em")
@@ -484,39 +464,28 @@ def rank_program(g, core, T, topo):
         red(EM, c_("u4", 4), MIN, ["u4"], ["em"])
         ts(c_("hh"), EM, c_("amaxe"), c_("bigu"), EQ, MUL, ["em", "amaxe", "bigu"], ["hh"])
         ts(c_("key"), EM, RQ, RQ, ADD, SUB, ["em"], ["key"])
-        ts(T.bc[:], T.tm[:], c_("key"), c_("hh"), ADD, ADD, ["tm", "key", "hh"], ["bc"])
-        tt(c_("kp"), c_("key"), c_("hh"), ADD, ["key", "hh"], ["kp"])
-        tr(T.kt[:], T.bc[:], ["bc"], ["kt"])
         ts(c_("jr"), EM, RJ, RJ, ADD, SUB, ["em"], ["jr"])
-        ts(T.qq[:, 0:32], T.kt[:], c_("kp"), WT, EQ, MUL, ["kt", "kp"], ["qq"])
+        ts(T.bc[:], T.tm[:], c_("key"), c_("hh"), ADD, ADD, ["tm", "key", "hh"], ["bc"])
         ts(c_("cpv"), EM, c_("jr"), 256.0, SUB, MUL, ["em", "jr"], ["cpv"])
+        tr(T.kt[:], T.bc[:], ["bc"], ["kt"])
+        tt(c_("kp"), c_("key"), c_("hh"), ADD, ["key", "hh"], ["kp"])
+        ts(c_("cd"), c_("cpv"), c_("apos"), c_("hh"), SUB, ADD, ["cpv", "apos", "hh"], ["cd"])
+        ts(T.qq[:, 0:32], T.kt[:], c_("kp"), WT, EQ, MUL, ["kt", "kp"], ["qq"])
+        ts(c_("ca", 8), c_("nm", 8), c_("cd"), None, ADD, None, ["nm", "cd"], ["ca"])
         red(c_("xx"), T.qq[:, 0:33], ADD, ["qq", "qqc"], ["xx"])
+        ts(T.sb0[:, 0:32:4], c_("ca", 8), c_("xx"), 0.0, MAX, MIN, ["ca", "xx"], ["sb0a"])
+        ts(T.sb0[:, 1:2], c_("xx"), c_("cpv"), c_("apos"), MAX, MIN, ["xx", "cpv", "apos"], ["sb0b"])
+        ts(T.sb0[:, 17:18], c_("xx"), c_("cpv"), c_("apos"), MAX, MIN, ["xx", "cpv", "apos"], ["sb0c"])
+        turn("sb", ["sb0", "sb0a", "sb0b", "sb0c", "sb0d"])
+        tt(T.of16[:], T.sb3[:].indirect(RL), T.sc16[:], ADD, ["sb3", "RL", "sc16a", "sc16b"], ["of16"])
+        spread(lambda q: T.so[q, 0:12], T.of16[Q0, 0:12], ["of16"], "so")
         rc, rs = window(t)
-
-        def fpos(out, key):
-            ts(out, c_("xx"), c_("cpv"), c_("apos"), MAX, MIN, ["xx", "cpv", "apos"], [key])
-
-        def gap():
-            ts(c_("cd"), c_("cpv"), c_("apos"), c_("hh"), SUB, ADD, ["cpv", "apos", "hh"], ["cd"])
-
-        if not last:
-            fpos(T.fb0[:, 0:1], "fb0a")
-            fpos(T.fb0[:, 16:17], "fb0b")
-            weave(turn("fb", ["fb0", "fb0a", "fb0b"]))
-            spread(lambda q: T.fo[q, :], T.fb3[Q0, 0:32:16], ["fb3"], "fo")
-            fo, fk = T.fo[:], four("fo")
-        else:
-            gap()
-            sl = slot_list(True)
-            weave(sl[:1], [lambda: fpos(T.sb0[:, 4:5], "sb0c")])
-            weave(sl[1:3], [lambda: fpos(T.sb0[:, 20:21], "sb0d")])
-            weave(sl[3:])
-            fo, fk = T.so[:, 8:10], four("so")
-        pickc("fa", 0, 32, w, 0, 256, fo, fk + rc, ["fa.fc"])
-        picks("fa", 0, 32, w, 0, 256, fo, fk + rs, ["fa.fs"])
+        pickc("fa", 0, 64, w, 0, 256, T.so[:, 8:12], four("so") + rc, ["fa.c"])
+        picks("fa", 0, 64, w, 0, 256, T.so[:, 8:12], four("so") + rs, ["fa.s"])
         for b in range(4):
-            mm("pd%d" % b, "ee", 128 * b, "fa", 0, 128, False, True,
-               ["ee%d" % b, "fa.fc", "fa.fs", "fa.ac", "fa.as", "fa.z"])
+            mm("pd%d" % b, "ee", 128 * b, "fa", 0, 128, True, False, ["ee%d" % b, "fa.c", "fa.s", "fa.z"])
+            mm("pd%d" % b, "ee", 512 + 128 * b, "fa", 32, 128, False, True, ["ee%d" % (4 + b), "fa.c", "fa.s", "fa.z"])
+        slot_pick(t)
         xo, xn = T["xs%d" % t], T["xs%d" % (t + 1)]
 
         def x_new(b):
@@ -528,8 +497,6 @@ def rank_program(g, core, T, topo):
                ["bt", "x%d.%d" % (t + 1, b)], ["et.%d" % b])
 
         if not last:
-            gap()
-            ts(c_("de", 4), ae, -1.0, EM, MUL, ADD, [aek, "em"], ["de"])
             x_new(0)
             for b in range(1, 4):
                 x_new(b)
@@ -537,16 +504,19 @@ def rank_program(g, core, T, topo):
             e_new(3)
             quant("qe%d" % (t + 1), 0, 128, T.et[:], four("et."), ["qe%d" % (t + 1)])
             send_e(t + 1)
-            own_e(t + 1)
-            sl = slot_list(False)
-            weave(sl[:1])
-            weave(sl[1:], renew(ae, aek, c_("de", 4), "de", act_e(t + 1)[0], act_e(t + 1)[1]))
-            slot_pick(t)
             a_mm(t + 1)
-            weave(a_chain())
+            own_e(t + 1)
+            ts(c_("de", 4), ae, -1.0, EM, MUL, ADD, [aek, "em"], ["de"])
+            nx, nk = act_e(t + 1)
+            weave(a_scores(), renew(ae, aek, c_("de", 4), "de", nx, nk))
+            weave(a_chain(), best_active(t + 1))
+            if t + 1 == R - 1:
+                ts(c_("k4", 4), nx, RQ, RQ, ADD, SUB, [nk], ["k4"])
+                ts(c_("j4", 4), nx, RJ, RJ, ADD, SUB, [nk], ["j4"])
+                ts(c_("k5", 4), c_("k4", 4), TAGN, None, MUL, None, ["k4"], ["k5"])
+                tt(c_("no", 4), c_("k5", 4), c_("j4", 4), ADD, ["k5", "j4"], ["no"])
         else:
             wl = "win%d" % R
-            slot_pick(t)
             y_mm(t)
             store("s", T.oc[:], bytes_of(wl, 128, 256), [wl + ".sc"])
             for a in range(4):

@@ -35,15 +35,15 @@ for _t in range(R + 1):
     _sb("xs%d" % _t, 128, BF)
 for _n, _c, _d in (
         ("dtile", 4 * A, BF), ("wt", 1024, BF), ("bt", 128, BF), ("et", 512, BF), ("pxs", 128, F32),
-        ("v516", 516, BF), ("ua", 516, BF), ("ub", 516, BF), ("na", 516, BF), ("nb", 516, BF),
-        ("j2", 128, F32), ("d4", 128, F32), ("kp4", 128, F32), ("am", 128, F32), ("asc", 128, F32),
+        ("v516", 516, BF), ("av", 516, BF), ("ua", 516, BF), ("ub", 516, BF), ("na", 516, BF), ("nb", 516, BF),
+        ("j2", 128, F32), ("aj", 128, F32), ("d4", 128, F32), ("kp4", 128, F32), ("am", 128, F32), ("asc", 128, F32),
         ("neg", A, F32), ("r1", A, F32), ("r2", A, F32), ("junk", 2 * A, BF),
         ("sm", 160, F32), ("si", 16, I32), ("acti", 8, I32), ("af", 8, F32), ("ae0", 16, F32),
         ("zer", 32, F32), ("tm", 32, F32), ("bc", 32, F32), ("kt", 32, F32), ("qq", 40, F32), ("sc16", 16, F32),
         ("sc8", 8, F32), ("of16", 16, F32), ("i8", 8, F32),
-        ("cu", 16, U16), ("ho", 16, U16), ("so", 16, U16), ("aoff", 8, U16)):
+        ("cu", 16, U16), ("ho", 16, U16), ("so", 16, U16), ("fo", 2, U16), ("ao", 2, U16), ("aoff", 8, U16)):
     _sb(_n, _c, _d)
-for _n in ("z", "sb", "nn"):
+for _n in ("z", "sb", "fb", "ab", "nn"):
     for _s in "0123":
         if _n != "nn" or _s in "01":
             _sb(_n + _s, 32, F32)
@@ -198,6 +198,9 @@ def rank_program(g, core, T, topo):
     def scan(out, a, b, init, o0, o1, r, w):
         op("v", lambda: V.tensor_tensor_scan(out, a, b, init, o0, o1), r, w)
 
+    def av(out, a, func, scale, bias, r, w):
+        op("a", lambda: S.activation(out, a, func, bias=bias, scale=scale), r, w)
+
     def quant(name, a, b, src, r, w):
         op("v", lambda: V.quantize_mx(T[name + "c"][:, a:b], T[name + "s"][:, a:b], src), r, w)
 
@@ -230,13 +233,12 @@ def rank_program(g, core, T, topo):
     GL, EL, AL, RL = T.cu[:, 0:2], T.cu[:, 2:4], T.cu[:, 4:5], T.cu[:, 6:7]
 
     def turn(n, r):
-        tr(T[n + "1"][:], T[n + "0"][:], r, [n + "1"])
-        cp(T[n + "2"][:], T[n + "1"][:].indirect(GL), [n + "1", "GL"], [n + "2"])
-        tr(T[n + "3"][:], T[n + "2"][:], [n + "2"], [n + "3"])
+        return [lambda: tr(T[n + "1"][:], T[n + "0"][:], r, [n + "1"]),
+                lambda: cp(T[n + "2"][:], T[n + "1"][:].indirect(GL), [n + "1", "GL"], [n + "2"]),
+                lambda: tr(T[n + "3"][:], T[n + "2"][:], [n + "2"], [n + "3"])]
 
     def spread(dst, src, r, w):
-        for a in range(4):
-            cp(dst(slice(32 * a, 32 * a + 32)), src, r, [w + str(a)])
+        return [lambda a=a: cp(dst(slice(32 * a, 32 * a + 32)), src, r, [w + str(a)]) for a in range(4)]
 
     def four(w):
         return [w + str(a) for a in range(4)]
@@ -254,7 +256,7 @@ def rank_program(g, core, T, topo):
     g.sync.dma_start(T.acti[ka:ka + 16, :], T.act[:]).then_inc(T.sem.la, 16)
     g.sync.dma_start(T.acti[ka + 16:kb, :], T.act[:]).then_inc(T.sem.la, 16)
     arrives("la", 32, ["acti"])
-    op("s", lambda: g.sync.dma_start(T.wt[:], T.w[:]), [], ["wt"], "lw", 16)
+    op("s", lambda: g.sync.dma_start(T.wt[:], T.w[:]), ["dtile"], ["wt"], "lw", 16)
 
     def iota(out, pat, base, cm, w, small=True):
         if small:
@@ -263,16 +265,29 @@ def rank_program(g, core, T, topo):
             op("g", lambda: g.iota(out, pat, base, cm), [], w)
 
     iota(T.si[:, 0:1], [[1, 1]], 0, 1, ["pi"], False)
+    iota(T.v516[:], [[1, 129], [1000, 4]], -3000, -1, ["v516"])
     iota(T.j2[:], [[0, 4], [1, 32]], ka, -1, ["j2"])
     iota(T.i8[:], [[0, 2], [1, 4]], 0, 0, ["i8"])
     iota(T.sc8[:], [[32, 4], [16, 2]], 128, 0, ["sc8"])
-    iota(T.v516[:], [[1, 129], [1000, 4]], -3000, -1, ["v516"])
+
+    J0 = T.j2[:, 0:1]
+    av(T.av[:], T.v516[:], ACT.Abs, 1.0, 0.0, ["v516"], ["av"])
+    av(T.ua[:, 0:514], T.av[:, 1:515], ACT.Relu, -1.0, 0.25, ["av"], ["ua"])
+    av(T.ub[:, 0:514], T.av[:, 0:514], ACT.Relu, -1.0, 0.25, ["av"], ["ub"])
+    av(T.aj[:], T.j2[:], ACT.Abs, 1.0, 0.0, ["j2"], ["aj"])
+    av(T.na[:, 0:514], T.ua[:, 0:514], ACT.Identity, -1.0, 0.0, ["ua"], ["na"])
+    av(T.nb[:, 0:514], T.ub[:, 0:514], ACT.Identity, -1.0, 0.0, ["ub"], ["nb"])
+    av(T.d4[:], T.aj[:], ACT.Relu, -1.0, 1.0, ["aj"], ["d4"])
+    av(T.kp4[:], T.aj[:], ACT.Sign, 1.0, 0.0, ["aj"], ["kp4"])
+    av(c_("i128"), J0, ACT.Identity, -1.0, 128.0, ["j2"], ["i128"])
+    av(c_("ic"), J0, ACT.Identity, -1.0, 0.0, ["j2"], ["ic"])
+    av(T.tm[:], T.j2[:, 0:32], ACT.Relu, -BIG, BIG, ["j2"], ["tm"])
+    av(c_("bigu"), J0, ACT.Identity, -16384.0, 16384.0, ["j2"], ["bigu"])
 
     ms(T.et[:], 0.0, four("et."))
-    ms(T.neg[:], -1.0e29, ["neg"])
     ms(T.zer[:], 0.0, ["zer"])
-    for n in ("sb0", "nn0"):
-        ms(T[n][:], 0.0, [n, n + "a", n + "b", n + "c", n + "d"])
+    for n in ("sb0", "fb0", "ab0", "nn0"):
+        ms(T[n][:], 0.0, [n, n + "a"])
     ms(T.qq[:, 32:33], -(CAPP - 0.5) * WT, ["qqc"])
     ms(T.sc16[:, 8:16], 0.0, ["sc16b"])
     PI = T.si[:, 0:1]
@@ -283,51 +298,34 @@ def rank_program(g, core, T, topo):
     ts(T.si[:, 5:6], PI, 1, 3, SHR, AND, ["pi"], ["ph"])
     ts(T.si[:, 6:7], PI, 1, None, AND, None, ["pi"], ["p1"])
     ts(T.si[:, 7:8], PI, 3, 1, SHR, AND, ["pi"], ["p8"])
+    cp(T.cu[:, 0:1], T.si[:, 1:2], ["p31"], ["GLa"])
+    cp(T.cu[:, 2:3], T.si[:, 2:3], ["p15"], ["ELa"])
+    cp(c_("pg"), T.si[:, 4:5], ["pg"], ["pgf"])
+    cp(c_("p8"), T.si[:, 7:8], ["p8"], ["p8f"])
+    cp(c_("p15"), T.si[:, 2:3], ["p15"], ["p15f"])
     tt(T.et[:, 128 * k:128 * k + 128], T.bt[:], T.xs0[:], SUB, ["bt"] + four("x0."), four("et."))
     quant("qe0", 0, 128, T.et[:], four("et."), ["qe0"])
 
     def send_e(t):
         es = topo.engines(core, peers[0])
         n = "qe%d" % t
-        send([xfer(bytes_of(n, ka, kb), [(c, bytes_of("eg%d" % t, ka, kb)) for c in peers], es, "ae%d" % t)], [n])
-        send([xfer(T[n + "s"][:, ka:kb], [(c, T["eg%ds" % t][:, ka:kb]) for c in peers], es, "ae%d" % t)], [n])
-        arrives("ae%d" % t, sum(2 * len(topo.engines(c, core)) for c in peers), ["eg%d.r" % t])
+        h = len(es) // 2
+        e1, e2 = (es[:h], es[h:]) if t == 0 else (es, es)
+        send([xfer(bytes_of(n, ka, kb), [(c, bytes_of("eg%d" % t, ka, kb)) for c in peers], e1, "ae%d" % t)], [n])
+        send([xfer(T[n + "s"][:, ka:kb], [(c, T["eg%ds" % t][:, ka:kb]) for c in peers], e2, "ae%d" % t)], [n])
+        arrives("ae%d" % t, (len(e1) + len(e2)) * len(peers), ["eg%d.r" % t])
 
     send_e(0)
-    cp(T.cu[:, 0:1], T.si[:, 1:2], ["p31"], ["GLa"])
-    cp(T.cu[:, 2:3], T.si[:, 2:3], ["p15"], ["ELa"])
-    cp(c_("pg"), T.si[:, 4:5], ["pg"], ["pgf"])
-    cp(c_("p8"), T.si[:, 7:8], ["p8"], ["p8f"])
-    cp(c_("p15"), T.si[:, 2:3], ["p15"], ["p15f"])
     cp(T.cu[:, 1:2], T.si[:, 1:2], ["p31", "GLa"], ["GL"])
     ts(T.cu[:, 3:4], T.si[:, 2:3], 16.0, None, ADD, None, ["p15", "ELa"], ["EL"])
+    ts(AL, T.si[:, 3:4], 2.0, c_("pg"), MUL, ADD, ["p3", "pgf"], ["AL"])
+    ts(c_("rl"), T.si[:, 5:6], 4.0, c_("p8"), MUL, ADD, ["ph", "p8f"], ["rl"])
+    ts(c_("k1"), T.si[:, 1:2], 1.0 / 256, float(QS * qlow) + ka / 256.0, MUL, ADD, ["p31"], ["k1"])
     quant("at", own0, own0 + A, T.dtile[:], ["dtile"], ["at.o"])
     es = topo.engines(core, mate)
     send([xfer(bytes_of("at", own0, own0 + A), [(mate, bytes_of("at", own0, own0 + A))], es, "aa")], ["at.o"])
     send([xfer(T.ats[:, own0:own0 + A], [(mate, T.ats[:, own0:own0 + A])], es, "aa")], ["at.o"])
     arrives("aa", 2 * len(topo.engines(mate, core)), ["at.r"])
-
-    ts(AL, T.si[:, 3:4], 2.0, c_("pg"), MUL, ADD, ["p3", "pgf"], ["AL"])
-    ts(c_("rl"), T.si[:, 5:6], 4.0, c_("p8"), MUL, ADD, ["ph", "p8f"], ["rl"])
-    ts(c_("k1"), T.si[:, 1:2], 1.0 / 256, float(QS * qlow) + ka / 256.0, MUL, ADD, ["p31"], ["k1"])
-    spread(lambda q: T.af[q, :], T.acti[Q0, :], ["acti"], "af")
-    J0 = T.j2[:, 0:1]
-    ts(RL, T.si[:, 6:7], 16.0, c_("rl"), MUL, ADD, ["p1", "rl"], ["RL"])
-    cp(T.aoff[:], T.af[:], four("af"), ["aoff"])
-    ts(T.ae0[:], T.af[:].indirect(AL), c_("k1"), float(QS * (rank - qlow)), ADD, ADD, four("af") + ["AL", "k1"], ["ae0"])
-    ts(c_("i128"), J0, -1.0, 128.0, MUL, ADD, ["j2"], ["i128"])
-    pickc("win0", 128, 256, "at", own0, own0 + A, T.aoff[:], ["aoff", "at.o"], ["win0.sc"])
-    picks("win0", 128, 256, "at", own0, own0 + A, T.aoff[:], ["aoff", "at.o"], ["win0.ss"])
-    ts(T.d4[:], T.j2[:], 0.0, None, EQ, None, ["j2"], ["d4"])
-    ts(T.kp4[:], T.j2[:], 0.0, None, NE, None, ["j2"], ["kp4"])
-    ts(c_("bigu"), J0, -16384.0, 16384.0, MUL, ADD, ["j2"], ["bigu"])
-    ts(T.tm[:], T.j2[:, 0:32], 0.0, -float(2 ** 30), LE, MUL, ["j2"], ["tm"])
-    ts(T.sc16[:, 0:8], T.sc8[:], c_("p15"), None, ADD, None, ["sc8", "p15f"], ["sc16a"])
-    quant("fa", 32, 160, T.dtile[:, 0:512], ["dtile"], ["fa.c", "fa.s", "fa.z"])
-    ts(T.ua[:, 0:514], T.v516[:, 1:515], 0.0, 0.25, EQ, MUL, ["v516"], ["ua"])
-    ts(T.ub[:, 0:514], T.v516[:, 0:514], 0.0, 0.25, EQ, MUL, ["v516"], ["ub"])
-    op("a", lambda: S.activation(T.na[:, 0:514], T.ua[:, 0:514], ACT.Copy, scale=-1.0), ["ua"], ["na"])
-    op("a", lambda: S.activation(T.nb[:, 0:514], T.ub[:, 0:514], ACT.Copy, scale=-1.0), ["ub"], ["nb"])
 
     def own_e(t):
         pickc("eg%d" % t, ka, kb, "qe%d" % t, ka, kb, EL, ["EL", "qe%d" % t], ["eg%d.c" % t])
@@ -352,9 +350,12 @@ def rank_program(g, core, T, topo):
             lambda: ts(c_("ta", 4), AS, c_("amin"), 8.0, GT, MUL, ["asc", "amin"], ["ta"]),
             lambda: tt(c_("ua", 4), c_("ta", 4), T.i8[:, 0:4], ADD, ["ta", "i8"], ["ua4"]),
             lambda: red(c_("aslot"), c_("ua", 4), MIN, ["ua4"], ["aslot"]),
-            lambda: ts(c_("apos"), c_("aslot"), 32.0, c_("i128"), MUL, ADD, ["aslot", "i128"], ["apos"]),
             lambda: ts(c_("nm", 8), T.i8[:], c_("aslot"), BIG, NE, MUL, ["i8", "aslot"], ["nm"]),
-            lambda: ts(T.sb0[:, 5:32:16], T.zer[:, 0:2], c_("apos"), None, ADD, None, ["zer", "apos"], ["sb0d"])]
+            lambda: av(c_("apr"), c_("aslot"), ACT.Identity, 32.0, c_("ic"), ["aslot", "ic"], ["apr"]),
+            lambda: av(c_("apos"), c_("aslot"), ACT.Identity, 32.0, c_("i128"), ["aslot", "i128"], ["apos"]),
+            lambda: av(T.ab0[:, 0:32:16], T.zer[:, 0:2], ACT.Identity, 1.0, c_("apr"), ["zer", "apr"], ["ab0a"]),
+            lambda: av(c_("napos"), c_("apos"), ACT.Identity, -1.0, 0.0, ["apos"], ["napos"]),
+            lambda: av(c_("nma", 8), c_("nm", 8), ACT.Identity, 1.0, c_("napos"), ["nm", "napos"], ["nma"])]
 
     def best_active(t):
         ae, key = act_e(t)
@@ -397,11 +398,19 @@ def rank_program(g, core, T, topo):
         at = 512 * neg + 128 * b
         return lambda: quant("ee", at, at + 128, T[src][:, st:st + 512], [src], ["ee%d" % (4 * neg + b)])
 
+    weave(spread(lambda q: T.af[q, :], T.acti[Q0, :], ["acti"], "af"))
+    ts(RL, T.si[:, 6:7], 16.0, c_("rl"), MUL, ADD, ["p1", "rl"], ["RL"])
+    cp(T.aoff[:], T.af[:], four("af"), ["aoff"])
+    ts(T.ae0[:], T.af[:].indirect(AL), c_("k1"), float(QS * (rank - qlow)), ADD, ADD, four("af") + ["AL", "k1"], ["ae0"])
+    pickc("win0", 128, 256, "at", own0, own0 + A, T.aoff[:], ["aoff", "at.o"], ["win0.sc"])
+    picks("win0", 128, 256, "at", own0, own0 + A, T.aoff[:], ["aoff", "at.o"], ["win0.ss"])
     own_e(0)
     a_mm(0)
+    ms(T.neg[:], -1.0e29, ["neg"])
     weave([unit(b, 0) for b in range(4)])
     weave(a_scores() + a_chain(), [unit(b, 1) for b in range(2)] + best_active(0) + [unit(b, 1) for b in range(2, 4)])
-    quant("wq", 0, 256, T.wt[:], ["wt"], ["wq"])
+    ts(T.sc16[:, 0:8], T.sc8[:], c_("p15"), None, ADD, None, ["sc8", "p15f"], ["sc16a"])
+    quant("fa", 32, 160, T.dtile[:, 0:512], ["dtile"], ["fa.ac", "fa.as", "fa.z"])
 
     for t in range(R):
         last = t == R - 1
@@ -436,8 +445,10 @@ def rank_program(g, core, T, topo):
             a = min(col[2 * h], col[2 * h + 1])
             cp(T.z0[64 - 64 * h:128 - 64 * h, a:32:8], T.z0[64 * h:64 * h + 64, a:32:8],
                ["z.%d" % (2 * h), "z.%d" % (2 * h + 1)], ["zz%d" % h])
-        turn("z", ["z0"] + four("z.") + ["zz0", "zz1"])
+        weave(turn("z", ["z0"] + four("z.") + ["zz0", "zz1"]), turn("ab", ["ab0", "ab0a"]))
         cp(T.ho[:], T.z3[:].indirect(RL), ["z3", "RL"], ["ho"])
+        apk = spread(lambda q: T.ao[q, :], T.ab3[Q0, 0:32:16], ["ab3"], "ao")
+        apk[0]()
         hk = ["ho", "at.o", "at.r"]
         pickc(pk, 0, 96, "at", 0, AW, T.ho[:, 0:6], hk, [pk + ".c"])
         picks(pk, 0, 96, "at", 0, AW, T.ho[:, 0:6], hk, [pk + ".s"])
@@ -454,38 +465,55 @@ def rank_program(g, core, T, topo):
         if t > 0:
             y_out(t - 1, "s")
         ae, aek = act_e(t)
+
+        def a_side():
+            pickc("fa", 32, 64, w, 128, 256, T.ao[:], four("ao") + [w + ".sc"], ["fa.ac"])
+            picks("fa", 32, 64, w, 128, 256, T.ao[:], four("ao") + [w + ".ss"], ["fa.as"])
+            for b in range(4):
+                mm("pd%d" % b, "ee", 512 + 128 * b, "fa", 32, 128, True, False, ["ee%d" % (4 + b), "fa.ac", "fa.as", "fa.z"])
+
         allm = mine + [mk + ".r"]
         SC = ml[:, 0:16:4]
         EM = c_("em")
+        apk[1]()
         red(c_("best"), SC, MAX, allm, ["best"])
         tt(c_("e4", 4), ml[:, 1:16:4], ml[:, 2:16:4], ADD, allm, ["e4"])
         ts(c_("t4", 4), SC, c_("best"), BIG, LT, MUL, allm + ["best"], ["t4"])
+        apk[2]()
         tt(c_("u4", 4), c_("t4", 4), c_("e4", 4), ADD, ["t4", "e4"], ["u4"])
+        apk[3]()
         red(EM, c_("u4", 4), MIN, ["u4"], ["em"])
+        a_side()
+        av(c_("em256"), EM, ACT.Identity, 256.0, 0.0, ["em"], ["em256"])
         ts(c_("hh"), EM, c_("amaxe"), c_("bigu"), EQ, MUL, ["em", "amaxe", "bigu"], ["hh"])
         ts(c_("key"), EM, RQ, RQ, ADD, SUB, ["em"], ["key"])
         ts(c_("jr"), EM, RJ, RJ, ADD, SUB, ["em"], ["jr"])
         ts(T.bc[:], T.tm[:], c_("key"), c_("hh"), ADD, ADD, ["tm", "key", "hh"], ["bc"])
-        ts(c_("cpv"), EM, c_("jr"), 256.0, SUB, MUL, ["em", "jr"], ["cpv"])
-        tr(T.kt[:], T.bc[:], ["bc"], ["kt"])
         tt(c_("kp"), c_("key"), c_("hh"), ADD, ["key", "hh"], ["kp"])
-        ts(c_("cd"), c_("cpv"), c_("apos"), c_("hh"), SUB, ADD, ["cpv", "apos", "hh"], ["cd"])
+        av(c_("cpv"), c_("jr"), ACT.Identity, -256.0, c_("em256"), ["jr", "em256"], ["cpv"])
+        av(c_("cd"), c_("hh"), ACT.Identity, 1.0, c_("cpv"), ["hh", "cpv"], ["cd"])
+        av(c_("cp2", 2), T.zer[:, 0:2], ACT.Identity, 1.0, c_("cpv"), ["zer", "cpv"], ["cp2"])
+        av(c_("ca", 8), c_("nma", 8), ACT.Identity, 1.0, c_("cd"), ["nma", "cd"], ["ca"])
+        if last:
+            av(c_("fn"), c_("key"), ACT.Identity, TAGN, c_("jr"), ["key", "jr"], ["fn"])
+            av(c_("de", 4), c_("no", 4), ACT.Identity, -1.0, c_("fn"), ["no", "fn"], ["de"])
+        else:
+            av(c_("de", 4), ae, ACT.Identity, -1.0, EM, [aek, "em"], ["de"])
+        tr(T.kt[:], T.bc[:], ["bc"], ["kt"])
         ts(T.qq[:, 0:32], T.kt[:], c_("kp"), WT, EQ, MUL, ["kt", "kp"], ["qq"])
-        ts(c_("ca", 8), c_("nm", 8), c_("cd"), None, ADD, None, ["nm", "cd"], ["ca"])
         red(c_("xx"), T.qq[:, 0:33], ADD, ["qq", "qqc"], ["xx"])
+        ts(T.fb0[:, 0:32:16], c_("cp2", 2), c_("xx"), c_("apos"), MAX, MIN, ["xx", "cp2", "apos"], ["fb0a"])
         ts(T.sb0[:, 0:32:4], c_("ca", 8), c_("xx"), 0.0, MAX, MIN, ["ca", "xx"], ["sb0a"])
-        ts(T.sb0[:, 1:2], c_("xx"), c_("cpv"), c_("apos"), MAX, MIN, ["xx", "cpv", "apos"], ["sb0b"])
-        ts(T.sb0[:, 17:18], c_("xx"), c_("cpv"), c_("apos"), MAX, MIN, ["xx", "cpv", "apos"], ["sb0c"])
-        turn("sb", ["sb0", "sb0a", "sb0b", "sb0c", "sb0d"])
+        weave(turn("fb", ["fb0", "fb0a"]), turn("sb", ["sb0", "sb0a"]))
+        weave(spread(lambda q: T.fo[q, :], T.fb3[Q0, 0:32:16], ["fb3"], "fo"))
         tt(T.of16[:], T.sb3[:].indirect(RL), T.sc16[:], ADD, ["sb3", "RL", "sc16a", "sc16b"], ["of16"])
-        spread(lambda q: T.so[q, 0:12], T.of16[Q0, 0:12], ["of16"], "so")
         rc, rs = window(t)
-        pickc("fa", 0, 64, w, 0, 256, T.so[:, 8:12], four("so") + rc, ["fa.c"])
-        picks("fa", 0, 64, w, 0, 256, T.so[:, 8:12], four("so") + rs, ["fa.s"])
+        pickc("fa", 0, 32, w, 0, 256, T.fo[:], four("fo") + rc, ["fa.fc"])
+        picks("fa", 0, 32, w, 0, 256, T.fo[:], four("fo") + rs, ["fa.fs"])
         for b in range(4):
-            mm("pd%d" % b, "ee", 128 * b, "fa", 0, 128, True, False, ["ee%d" % b, "fa.c", "fa.s", "fa.z"])
-            mm("pd%d" % b, "ee", 512 + 128 * b, "fa", 32, 128, False, True, ["ee%d" % (4 + b), "fa.c", "fa.s", "fa.z"])
-        slot_pick(t)
+            mm("pd%d" % b, "ee", 128 * b, "fa", 0, 128, False, True,
+               ["ee%d" % b, "fa.fc", "fa.fs", "fa.ac", "fa.as", "fa.z"])
+        weave(spread(lambda q: T.so[q, 0:8], T.of16[Q0, 0:8], ["of16"], "so"))
         xo, xn = T["xs%d" % t], T["xs%d" % (t + 1)]
 
         def x_new(b):
@@ -498,18 +526,23 @@ def rank_program(g, core, T, topo):
 
         if not last:
             x_new(0)
-            for b in range(1, 4):
-                x_new(b)
-                e_new(b - 1)
+            x_new(1)
+            e_new(0)
+            x_new(2)
+            x_new(3)
+            e_new(1)
+            e_new(2)
             e_new(3)
             quant("qe%d" % (t + 1), 0, 128, T.et[:], four("et."), ["qe%d" % (t + 1)])
             send_e(t + 1)
+            slot_pick(t)
             a_mm(t + 1)
             own_e(t + 1)
-            ts(c_("de", 4), ae, -1.0, EM, MUL, ADD, [aek, "em"], ["de"])
             nx, nk = act_e(t + 1)
             weave(a_scores(), renew(ae, aek, c_("de", 4), "de", nx, nk))
             weave(a_chain(), best_active(t + 1))
+            if t == 0:
+                quant("wq", 0, 256, T.wt[:], ["wt"], ["wq"])
             if t + 1 == R - 1:
                 ts(c_("k4", 4), nx, RQ, RQ, ADD, SUB, [nk], ["k4"])
                 ts(c_("j4", 4), nx, RJ, RJ, ADD, SUB, [nk], ["j4"])
@@ -517,16 +550,17 @@ def rank_program(g, core, T, topo):
                 tt(c_("no", 4), c_("k5", 4), c_("j4", 4), ADD, ["k5", "j4"], ["no"])
         else:
             wl = "win%d" % R
+            rn = renew(c_("no", 4), "no", c_("de", 4), "de", T.nn0[:, 0:4], "nn0a")
+            rn[0]()
+            slot_pick(t)
             y_mm(t)
             store("s", T.oc[:], bytes_of(wl, 128, 256), [wl + ".sc"])
             for a in range(4):
                 store("s" if a < 2 else "a", T.osc[4 * a:4 * a + 4, :], T[wl + "s"][32 * a:32 * a + 4, 128:256], [wl + ".ss"])
-            ts(c_("fn"), c_("key"), TAGN, c_("jr"), MUL, ADD, ["key", "jr"], ["fn"])
-            rn = renew(c_("no", 4), "no", c_("de", 4), "de", T.nn0[:, 0:4], "nn0a")
-            rn[0]()
-            ts(c_("de", 4), c_("no", 4), -1.0, c_("fn"), MUL, ADD, ["no", "fn"], ["de"])
-            weave([lambda b=b: x_new(b) for b in range(4)], rn[1:])
+            weave([lambda b=b: x_new(b) for b in range(4)])
+            rn[1]()
             cp(T.pxs[:], xn[:], four("x%d." % R), ["pxs"])
+            rn[2]()
             tr(T.nn1[:], T.nn0[:], ["nn0", "nn0a"], ["nn1"])
             store("s", T.px[:], T.pxs[:], ["pxs"])
             store("s", T.an[:], T.nn1[ka:ka + 4, :], ["nn1"])

@@ -4,7 +4,7 @@ from concourse.mybir import dt, AluOpType, AxisListType, ActivationFunctionType
 N, A, M, CAPP, R, O = 8, 384, 32, 4, 3, 2
 G = N // 2
 QS = 1024
-HI = QS * G
+HI = QS
 AW = HI + A
 C8, U8, F32, BF, U16, I32 = "float8_e4m3fn_x4", "uint8", "float32", "bfloat16", "uint16", "int32"
 
@@ -37,16 +37,17 @@ for _n, _c, _d in (
         ("dtile", 4 * A, BF), ("wt", 1024, BF), ("bt", 128, BF), ("et", 512, BF), ("pxs", 128, F32),
         ("v516", 516, BF), ("av", 516, BF), ("ua", 516, BF), ("ub", 516, BF), ("na", 516, BF), ("nb", 516, BF),
         ("j2", 128, F32), ("aj", 128, F32), ("d4", 128, F32), ("kp4", 128, F32), ("am", 128, F32), ("asc", 128, F32),
-        ("neg", A, F32), ("r1", A, F32), ("r2", A, F32), ("junk", 2 * A, BF),
-        ("sm", 160, F32), ("si", 16, I32), ("acti", 8, I32), ("af", 8, F32), ("ae0", 16, F32),
-        ("zer", 32, F32), ("tm", 32, F32), ("bc", 32, F32), ("kt", 32, F32), ("qq", 40, F32), ("sc16", 16, F32),
-        ("sc8", 8, F32), ("of16", 16, F32), ("i8", 8, F32),
+        ("neg", A, F32), ("r21", 2 * A, F32), ("junk", 2 * A, BF),
+        ("sm", 200, F32), ("si", 16, I32), ("acti", 8, I32), ("af", 8, F32), ("ae0", 16, F32),
+        ("zer", 32, F32), ("tm", 32, F32), ("kt", 32, F32), ("kp", 32, F32), ("qq", 40, F32), ("sc16", 16, F32),
+        ("nbw", 40, F32), ("khw", 40, F32), ("plw", 40, F32), ("kho", 64, F32), ("cpo", 64, F32), ("gb", 32, F32),
+        ("ms1", 32, F32), ("ms2", 32, F32), ("msel", 32, F32),
+        ("sc8", 8, F32), ("of16", 16, F32), ("i8", 8, F32), ("v8", 8, F32),
         ("cu", 16, U16), ("ho", 16, U16), ("so", 16, U16), ("fo", 2, U16), ("ao", 2, U16), ("aoff", 8, U16)):
     _sb(_n, _c, _d)
-for _n in ("z", "sb", "fb", "ab", "nn"):
-    for _s in "0123":
-        if _n != "nn" or _s in "01":
-            _sb(_n + _s, 32, F32)
+for _n, _k in (("z", 4), ("sb", 4), ("fb", 3), ("ab", 4), ("nn", 2)):
+    for _s in range(_k):
+        _sb(_n + str(_s), 32, F32)
 for _n in ("pd0", "pd1", "pd2", "pd3", "ps1", "ps2", "pa", "py"):
     SCRATCH[_n] = ("psum", [128, 512], F32)
 
@@ -60,17 +61,10 @@ AND, SHR = AluOpType.bitwise_and, AluOpType.logical_shift_right
 X = AxisListType.X
 ACT = ActivationFunctionType
 BIG = float(2 ** 20)
-WT = 1024.0
+PU = 1024.0
 RQ = 1.5 * 2.0 ** 33
 RJ = 1.5 * 2.0 ** 23
 TAGN = A / QS - 1.0
-
-
-def layout(T, topo, core):
-    grp = [c for c in T.cores if topo.die(c) == topo.die(core)]
-    oth = [c for c in T.cores if topo.die(c) != topo.die(core)]
-    k = grp.index(core)
-    return grp, k, oth[k]
 
 
 def shuffle_cols(k):
@@ -99,9 +93,8 @@ def rank_program(g, core, T, topo):
     rank = T.rank_of(core)
     if rank is None:
         return
-    grp, k, mate = layout(T, topo, core)
-    qlow = min(rank, T.rank_of(mate))
-    assert (max(rank, T.rank_of(mate)) - qlow) * QS == HI
+    grp, k, mate = list(T.cores[rank % 2::2]), rank // 2, T.cores[rank ^ 1]
+    qlow = 2 * k
     own0 = 0 if rank == qlow else HI
     col = shuffle_cols(k)
     order = places(k)
@@ -223,12 +216,12 @@ def rank_program(g, core, T, topo):
 
     cols = {}
 
-    def c_(name, w=1):
+    def c_(name, w=1, rows=slice(0, 128)):
         if name not in cols:
             at = sum(v[1] for v in cols.values())
             cols[name] = (at, w)
         at, w = cols[name]
-        return T.sm[:, at:at + w]
+        return T.sm[rows, at:at + w]
 
     GL, EL, AL, RL = T.cu[:, 0:2], T.cu[:, 2:4], T.cu[:, 4:5], T.cu[:, 6:7]
 
@@ -237,8 +230,11 @@ def rank_program(g, core, T, topo):
                 lambda: cp(T[n + "2"][:], T[n + "1"][:].indirect(GL), [n + "1", "GL"], [n + "2"]),
                 lambda: tr(T[n + "3"][:], T[n + "2"][:], [n + "2"], [n + "3"])]
 
+    def quad(a):
+        return slice(32 * a, 32 * a + 32)
+
     def spread(dst, src, r, w):
-        return [lambda a=a: cp(dst(slice(32 * a, 32 * a + 32)), src, r, [w + str(a)]) for a in range(4)]
+        return [lambda a=a: cp(dst(quad(a)), src, r, [w + str(a)]) for a in range(4)]
 
     def four(w):
         return [w + str(a) for a in range(4)]
@@ -269,6 +265,7 @@ def rank_program(g, core, T, topo):
     iota(T.j2[:], [[0, 4], [1, 32]], ka, -1, ["j2"])
     iota(T.i8[:], [[0, 2], [1, 4]], 0, 0, ["i8"])
     iota(T.sc8[:], [[32, 4], [16, 2]], 128, 0, ["sc8"])
+    iota(T.v8[:], [[-(16 * QS + 1), G], [-8 * QS, 2]], 8 * QS * (N - 1) + G - 1, 0, ["v8"])
 
     J0 = T.j2[:, 0:1]
     av(T.av[:], T.v516[:], ACT.Abs, 1.0, 0.0, ["v516"], ["av"])
@@ -279,16 +276,17 @@ def rank_program(g, core, T, topo):
     av(T.nb[:, 0:514], T.ub[:, 0:514], ACT.Identity, -1.0, 0.0, ["ub"], ["nb"])
     av(T.d4[:], T.aj[:], ACT.Relu, -1.0, 1.0, ["aj"], ["d4"])
     av(T.kp4[:], T.aj[:], ACT.Sign, 1.0, 0.0, ["aj"], ["kp4"])
-    av(c_("i128"), J0, ACT.Identity, -1.0, 128.0, ["j2"], ["i128"])
+    av(c_("ni128"), J0, ACT.Identity, 1.0 / PU, -128.0 / PU, ["j2"], ["ni128"])
     av(c_("ic"), J0, ACT.Identity, -1.0, 0.0, ["j2"], ["ic"])
-    av(T.tm[:], T.j2[:, 0:32], ACT.Relu, -BIG, BIG, ["j2"], ["tm"])
-    av(c_("bigu"), J0, ACT.Identity, -16384.0, 16384.0, ["j2"], ["bigu"])
+    av(T.tm[:], T.j2[:, 0:32], ACT.Relu, BIG, BIG, ["j2"], ["tm"])
+    av(T.ms1[:], T.aj[:, 0:32], ACT.Abs, 1.0, -8.0, ["aj"], ["ms1"])
+    av(T.ms2[:], T.ms1[:], ACT.Abs, 1.0, -8.0, ["ms1"], ["ms2"])
+    av(T.msel[:], T.ms2[:], ACT.Sign, 1.0, 0.0, ["ms2"], ["msel"])
 
     ms(T.et[:], 0.0, four("et."))
     ms(T.zer[:], 0.0, ["zer"])
-    for n in ("sb0", "fb0", "ab0", "nn0"):
+    for n in ("sb0", "ab0", "nn0"):
         ms(T[n][:], 0.0, [n, n + "a"])
-    ms(T.qq[:, 32:33], -(CAPP - 0.5) * WT, ["qqc"])
     ms(T.sc16[:, 8:16], 0.0, ["sc16b"])
     PI = T.si[:, 0:1]
     ts(T.si[:, 1:2], PI, 31, None, AND, None, ["pi"], ["p31"])
@@ -302,9 +300,12 @@ def rank_program(g, core, T, topo):
     cp(T.cu[:, 2:3], T.si[:, 2:3], ["p15"], ["ELa"])
     cp(c_("pg"), T.si[:, 4:5], ["pg"], ["pgf"])
     cp(c_("p8"), T.si[:, 7:8], ["p8"], ["p8f"])
-    cp(c_("p15"), T.si[:, 2:3], ["p15"], ["p15f"])
+    ts(c_("off"), T.si[:, 2:3], -1.0, 15.0, MUL, ADD, ["p15"], ["off"])
     tt(T.et[:, 128 * k:128 * k + 128], T.bt[:], T.xs0[:], SUB, ["bt"] + four("x0."), four("et."))
     quant("qe0", 0, 128, T.et[:], four("et."), ["qe0"])
+    OFF = c_("off")
+    av(c_("i128"), c_("ni128"), ACT.Identity, -1.0, OFF, ["ni128", "off"], ["i128"])
+    av(T.qq[:, 32:33], OFF, ACT.Identity, 1.0, -(CAPP - 0.5), ["off"], ["qqc"])
 
     def send_e(t):
         es = topo.engines(core, peers[0])
@@ -320,7 +321,8 @@ def rank_program(g, core, T, topo):
     ts(T.cu[:, 3:4], T.si[:, 2:3], 16.0, None, ADD, None, ["p15", "ELa"], ["EL"])
     ts(AL, T.si[:, 3:4], 2.0, c_("pg"), MUL, ADD, ["p3", "pgf"], ["AL"])
     ts(c_("rl"), T.si[:, 5:6], 4.0, c_("p8"), MUL, ADD, ["ph", "p8f"], ["rl"])
-    ts(c_("k1"), T.si[:, 1:2], 1.0 / 256, float(QS * qlow) + ka / 256.0, MUL, ADD, ["p31"], ["k1"])
+    ts(c_("k0"), T.si[:, 1:2], 1.0 / 256, None, MUL, None, ["p31"], ["k0"])
+    ts(c_("soc"), T.si[:, 2:3], 1.0 + 1.0 / PU, -15.0, MUL, ADD, ["p15"], ["soc"])
     quant("at", own0, own0 + A, T.dtile[:], ["dtile"], ["at.o"])
     es = topo.engines(core, mate)
     send([xfer(bytes_of("at", own0, own0 + A), [(mate, bytes_of("at", own0, own0 + A))], es, "aa")], ["at.o"])
@@ -338,6 +340,7 @@ def rank_program(g, core, T, topo):
         mm("pa", "qe%d" % t, 0, "win%d" % t, 128, 128, True, True, ["qe%d" % t, "win%d.sc" % t, "win%d.ss" % t])
 
     AS = T.asc[:, 31:128:32]
+    K8 = c_("k8", 8)
 
     def a_scores():
         return [
@@ -352,9 +355,9 @@ def rank_program(g, core, T, topo):
             lambda: red(c_("aslot"), c_("ua", 4), MIN, ["ua4"], ["aslot"]),
             lambda: ts(c_("nm", 8), T.i8[:], c_("aslot"), BIG, NE, MUL, ["i8", "aslot"], ["nm"]),
             lambda: av(c_("apr"), c_("aslot"), ACT.Identity, 32.0, c_("ic"), ["aslot", "ic"], ["apr"]),
-            lambda: av(c_("apos"), c_("aslot"), ACT.Identity, 32.0, c_("i128"), ["aslot", "i128"], ["apos"]),
+            lambda: av(c_("apos"), c_("aslot"), ACT.Identity, 32.0 / PU, c_("i128"), ["aslot", "i128"], ["apos"]),
             lambda: av(T.ab0[:, 0:32:16], T.zer[:, 0:2], ACT.Identity, 1.0, c_("apr"), ["zer", "apr"], ["ab0a"]),
-            lambda: av(c_("napos"), c_("apos"), ACT.Identity, -1.0, 0.0, ["apos"], ["napos"]),
+            lambda: av(c_("napos"), c_("aslot"), ACT.Identity, -32.0 / PU, c_("ni128"), ["aslot", "ni128"], ["napos"]),
             lambda: av(c_("nma", 8), c_("nm", 8), ACT.Identity, 1.0, c_("napos"), ["nm", "napos"], ["nma"])]
 
     def best_active(t):
@@ -363,7 +366,8 @@ def rank_program(g, core, T, topo):
             lambda: red(c_("amax"), AS, MAX, ["asc"], ["amax"]),
             lambda: ts(c_("tb", 4), AS, c_("amax"), BIG, LT, MUL, ["asc", "amax"], ["tb"]),
             lambda: tt(c_("ub", 4), c_("tb", 4), ae, ADD, ["tb", key], ["ub4"]),
-            lambda: red(c_("amaxe"), c_("ub", 4), MIN, ["ub4"], ["amaxe"])]
+            lambda: red(c_("amaxe"), c_("ub", 4), MIN, ["ub4"], ["amaxe"]),
+            lambda: av(c_("ak8", 8), K8, ACT.Identity, -1.0, c_("amaxe"), ["k8", "amaxe"], ["ak8"])]
 
     def y_mm(t):
         w = "win%d" % (t + 1)
@@ -388,7 +392,7 @@ def rank_program(g, core, T, topo):
         picks(w2, 128, 256, w, 0, 256, T.so[:, 0:8], four("so") + rs, [w2 + ".ss"])
 
     def renew(old, okey, diff, dkey, new, nkey):
-        return [lambda: ts(c_("m2", 4), T.sb0[:, 0:16:4], 0.0, None, LT, None, ["sb0a"], ["m2"]),
+        return [lambda: ts(c_("m2", 4), T.sb0[:, 0:16:4], OFF, None, LT, None, ["sb0a", "off"], ["m2"]),
                 lambda: tt(c_("dd", 4), c_("m2", 4), diff, MUL, ["m2", dkey], ["dd"]),
                 lambda: tt(new, old, c_("dd", 4), ADD, [okey, "dd"], [nkey])]
 
@@ -401,43 +405,63 @@ def rank_program(g, core, T, topo):
     weave(spread(lambda q: T.af[q, :], T.acti[Q0, :], ["acti"], "af"))
     ts(RL, T.si[:, 6:7], 16.0, c_("rl"), MUL, ADD, ["p1", "rl"], ["RL"])
     cp(T.aoff[:], T.af[:], four("af"), ["aoff"])
-    ts(T.ae0[:], T.af[:].indirect(AL), c_("k1"), float(QS * (rank - qlow)), ADD, ADD, four("af") + ["AL", "k1"], ["ae0"])
+    ts(T.ae0[:], T.af[:].indirect(AL), c_("k0"), float(QS * rank) + ka / 256.0, ADD, ADD,
+       four("af") + ["AL", "k0"], ["ae0"])
     pickc("win0", 128, 256, "at", own0, own0 + A, T.aoff[:], ["aoff", "at.o"], ["win0.sc"])
     picks("win0", 128, 256, "at", own0, own0 + A, T.aoff[:], ["aoff", "at.o"], ["win0.ss"])
     own_e(0)
     a_mm(0)
+    ts(K8, T.v8[:], 0.125, c_("k0"), MUL, ADD, ["v8", "k0"], ["k8"])
     ms(T.neg[:], -1.0e29, ["neg"])
+    ts(c_("key8", 8), K8, RQ, RQ, ADD, SUB, ["k8"], ["key8"])
+    ms(T.nbw[:, 8:40], 1.0, ["nbc"])
+    ms(T.khw[:, 8:40], 0.0, ["khc"])
+    tt(c_("pl8", 8), K8, c_("key8", 8), SUB, ["k8", "key8"], ["pl8"])
+    ms(T.plw[:, 8:40], 0.0, ["plc"])
     weave([unit(b, 0) for b in range(4)])
+    av(T.plw[:, 0:8], c_("pl8", 8), ACT.Identity, 256.0 / PU, OFF, ["pl8", "off"], ["plw"])
     weave(a_scores() + a_chain(), [unit(b, 1) for b in range(2)] + best_active(0) + [unit(b, 1) for b in range(2, 4)])
-    ts(T.sc16[:, 0:8], T.sc8[:], c_("p15"), None, ADD, None, ["sc8", "p15f"], ["sc16a"])
+    ts(T.sc16[:, 0:8], T.sc8[:], 1.0 / PU, c_("soc"), MUL, ADD, ["sc8", "soc"], ["sc16a"])
     quant("fa", 32, 160, T.dtile[:, 0:512], ["dtile"], ["fa.ac", "fa.as", "fa.z"])
 
     for t in range(R):
         last = t == R - 1
         ml, mk, eg, w, pk = T["ml%d" % t], "ml%d" % t, "eg%d" % t, "win%d" % t, "pk%d" % t
         egk = [eg + ".c", eg + ".s", eg + ".r"]
-        lowk, highk = ("at.o", "at.r") if own0 == 0 else ("at.r", "at.o")
-        mm("ps1", eg, 0, "at", 0, A, True, True, egk + [lowk])
-        mm("ps2", eg, 0, "at", HI, A, True, True, egk + [highk])
+        halves = [("ps1", 0, "r1", A), ("ps2", HI, "r2", 0)]
+        if own0:
+            halves.reverse()
+        for (bank, a0, _, _), key in zip(halves, ("at.o", "at.r")):
+            mm(bank, eg, 0, "at", a0, A, True, True, egk + [key])
         if t > 0:
             y_mm(t - 1)
-        M1, M2 = T.r1[:, A - 1:A], T.r2[:, A - 1:A]
-        C2 = ml[:, 4 * k + 2:4 * k + 3]
-        scan(T.r1[:], T.ps1[:, 0:A], T.neg[:], -1.0e29, MAX, MAX, ["Pps1", "neg"], ["r1"])
-        scan(T.r2[:], T.ps2[:, 0:A], T.neg[:], M1, MAX, MAX, ["Pps2", "neg", "r1"], ["r2"])
-        op("a", lambda: S.activation(T.junk[:, 0:A], T.r1[:], ACT.Sign, bias=M1, scale=-1.0, accum_out=c_("c1")),
-           ["r1"], ["c1", "junk1"])
-        op("a", lambda: S.activation(T.junk[:, A:2 * A], T.r2[:], ACT.Sign, bias=M2, scale=-1.0, accum_out=C2),
-           ["r2"], [mk + ".c", "junk2"])
-        ts(c_("gb"), M2, M1, float(HI), GT, MUL, ["r1", "r2"], ["gb"])
-        cp(ml[:, 4 * k:4 * k + 1], M2, ["r2"], [mk + ".m"])
-        ts(ml[:, 4 * k + 1:4 * k + 2], c_("gb"), c_("c1"), c_("k1"), MAX, ADD, ["gb", "c1", "k1"], [mk + ".e"])
-        ts(c_("rest"), c_("gb"), c_("c1"), None, MAX, None, ["gb", "c1"], ["rest"])
-        mine = [mk + ".m", mk + ".e", mk + ".c"]
-        mv = ml[:, 4 * k:4 * k + 3]
+        M2, M1 = T.r21[:, A - 1:A], T.r21[:, 2 * A - 1:2 * A]
+        m0 = 4 * (G - 1 - k)
+        C2, C1 = ml[:, m0 + 1:m0 + 2], ml[:, m0 + 3:m0 + 4]
+        for bank, _, rk, r0 in halves:
+            scan(T.r21[:, r0:r0 + A], T[bank][:, 0:A], T.neg[:], -1.0e29, MAX, MAX, ["P" + bank, "neg"], [rk])
+        for _, _, rk, r0 in halves:
+            op("a", lambda: S.activation(T.junk[:, r0:r0 + A], T.r21[:, r0:r0 + A], ACT.Sign,
+                                         bias=T.r21[:, r0 + A - 1:r0 + A], scale=-1.0, accum_out=C1 if r0 else C2),
+               [rk], [mk + "." + rk, "junk" + rk])
+        c1k, c2k = mk + ".r1", mk + ".r2"
+        cp(ml[:, m0:m0 + 4:2], T.r21[:, A - 1:2 * A:A], ["r1", "r2"], [mk + ".m"])
+        mine = [mk + ".m", c1k, c2k]
+        mv = ml[:, m0:m0 + 4]
         send([xfer(mv, [(c, mv) for c in peers], topo.engines(core, peers[0]), "am%d" % t)], mine)
         arrives("am%d" % t, sum(len(topo.engines(c, core)) for c in peers), [mk + ".r"])
-        ts(T.z0[:], T.zer[:], C2, c_("rest"), ADD, ADD, ["zer", mk + ".c", "rest"], ["z0"] + four("z.") + ["zz0", "zz1"])
+        zw = ["z0"] + four("z.") + ["zz0", "zz1"]
+        if own0:
+            ts(T.gb[:], T.zer[:], M2, M1, ADD, LE, ["zer", "r1", "r2"], ["gb"])
+            ts(c_("gh"), M2, M1, None, GT, None, ["r1", "r2"], ["gh"])
+            ts(c_("rest"), C2, float(HI), c_("gh"), ADD, MUL, ["gh", c2k], ["rest"])
+            ts(T.z0[:], T.gb[:], C1, c_("rest"), MUL, ADD, ["gb", c1k, "rest"], zw)
+        else:
+            ts(T.gb[:], T.zer[:], M2, M1, ADD, GT, ["zer", "r1", "r2"], ["gb"])
+            ts(c_("gh"), M2, M1, None, LE, None, ["r1", "r2"], ["gh"])
+            ts(c_("gi"), M2, M1, float(HI), GT, MUL, ["r1", "r2"], ["gi"])
+            ts(c_("rest"), C1, c_("gh"), c_("gi"), MUL, ADD, ["gh", "gi", c1k], ["rest"])
+            ts(T.z0[:], T.gb[:], C2, c_("rest"), MUL, ADD, ["gb", c2k, "rest"], zw)
         for s in range(G):
             o = s ^ 1
             cp(T.z0[32 * o:32 * o + 32, col[s]:32:16], T.z0[32 * s:32 * s + 32, col[s]:32:16], ["z0"], ["z.%d" % s])
@@ -445,7 +469,7 @@ def rank_program(g, core, T, topo):
             a = min(col[2 * h], col[2 * h + 1])
             cp(T.z0[64 - 64 * h:128 - 64 * h, a:32:8], T.z0[64 * h:64 * h + 64, a:32:8],
                ["z.%d" % (2 * h), "z.%d" % (2 * h + 1)], ["zz%d" % h])
-        weave(turn("z", ["z0"] + four("z.") + ["zz0", "zz1"]), turn("ab", ["ab0", "ab0a"]))
+        weave(turn("z", zw), turn("ab", ["ab0", "ab0a"]))
         cp(T.ho[:], T.z3[:].indirect(RL), ["z3", "RL"], ["ho"])
         apk = spread(lambda q: T.ao[q, :], T.ab3[Q0, 0:32:16], ["ab3"], "ao")
         apk[0]()
@@ -460,11 +484,13 @@ def rank_program(g, core, T, topo):
         for j, nm, key in ((0, "ac", ".rc"), (1, "as", ".rs")):
             arrives("%s%d" % (nm, t), sum(len(splits(topo.engines(grp[s], core))[j][places(s).index(k)])
                                           for s in range(G) if s != k), [w + key])
-        pickc(w, ka, kb, "at", 0, AW, T.ho[:, 6:8], hk, [w + ".oc"])
-        picks(w, ka, kb, "at", 0, AW, T.ho[:, 6:8], hk, [w + ".os"])
         if t > 0:
             y_out(t - 1, "s")
         ae, aek = act_e(t)
+
+        def own_pick():
+            pickc(w, ka, kb, "at", 0, AW, T.ho[:, 6:8], hk, [w + ".oc"])
+            picks(w, ka, kb, "at", 0, AW, T.ho[:, 6:8], hk, [w + ".os"])
 
         def a_side():
             pickc("fa", 32, 64, w, 128, 256, T.ao[:], four("ao") + [w + ".sc"], ["fa.ac"])
@@ -473,47 +499,58 @@ def rank_program(g, core, T, topo):
                 mm("pd%d" % b, "ee", 512 + 128 * b, "fa", 32, 128, True, False, ["ee%d" % (4 + b), "fa.ac", "fa.as", "fa.z"])
 
         allm = mine + [mk + ".r"]
-        SC = ml[:, 0:16:4]
-        EM = c_("em")
+        SC, CC = ml[:, 0:16:2], ml[:, 1:16:2]
+        EM = T.sm[:, 199:200]
+        HN = T.qq[:, 33:34]
         apk[1]()
         red(c_("best"), SC, MAX, allm, ["best"])
-        tt(c_("e4", 4), ml[:, 1:16:4], ml[:, 2:16:4], ADD, allm, ["e4"])
-        ts(c_("t4", 4), SC, c_("best"), BIG, LT, MUL, allm + ["best"], ["t4"])
+        tt(c_("h8", 8), CC, c_("ak8", 8), EQ, allm + ["ak8"], ["h8"])
+        tt(c_("e8", 8), CC, K8, ADD, allm + ["k8"], ["e8"])
+        ts(T.nbw[:, 0:8], SC, c_("best"), None, LT, None, allm + ["best"], ["nbw"])
+        tt(T.khw[:, 0:8], c_("h8", 8), c_("key8", 8), ADD, ["h8", "key8"], ["khw"])
         apk[2]()
-        tt(c_("u4", 4), c_("t4", 4), c_("e4", 4), ADD, ["t4", "e4"], ["u4"])
+        scan(T.kho[:, 24:64], T.nbw[:], T.khw[:], BIG, MUL, MAX, ["nbw", "nbc", "khw", "khc"], ["kho"])
+        scan(T.sm[:, 192:200], T.nbw[:, 0:8], c_("e8", 8), BIG, MUL, MAX, ["nbw", "e8"], ["em"])
+        scan(T.cpo[:, 24:64], T.nbw[:], T.plw[:], BIG, MUL, MAX, ["nbw", "nbc", "plw", "plc"], ["cpo"])
+        tr(T.kt[:], T.kho[:, 32:64], ["kho"], ["kt"])
+        tt(T.kp[:], T.kho[:, 32:64], T.tm[:], ADD, ["kho", "tm"], ["kp"])
+        ts(HN, EM, c_("amaxe"), -64.0, EQ, MUL, ["em", "amaxe"], ["hn"])
         apk[3]()
-        red(EM, c_("u4", 4), MIN, ["u4"], ["em"])
+        tt(T.qq[:, 0:32], T.kt[:], T.kp[:], EQ, ["kt", "kp"], ["qq"])
+        ts(c_("ca", 8), c_("nma", 8), HN, T.cpo[:, 63:64], SUB, ADD, ["nma", "hn", "cpo"], ["ca"])
         a_side()
-        av(c_("em256"), EM, ACT.Identity, 256.0, 0.0, ["em"], ["em256"])
-        ts(c_("hh"), EM, c_("amaxe"), c_("bigu"), EQ, MUL, ["em", "amaxe", "bigu"], ["hh"])
-        ts(c_("key"), EM, RQ, RQ, ADD, SUB, ["em"], ["key"])
-        ts(c_("jr"), EM, RJ, RJ, ADD, SUB, ["em"], ["jr"])
-        ts(T.bc[:], T.tm[:], c_("key"), c_("hh"), ADD, ADD, ["tm", "key", "hh"], ["bc"])
-        tt(c_("kp"), c_("key"), c_("hh"), ADD, ["key", "hh"], ["kp"])
-        av(c_("cpv"), c_("jr"), ACT.Identity, -256.0, c_("em256"), ["jr", "em256"], ["cpv"])
-        av(c_("cd"), c_("hh"), ACT.Identity, 1.0, c_("cpv"), ["hh", "cpv"], ["cd"])
-        av(c_("cp2", 2), T.zer[:, 0:2], ACT.Identity, 1.0, c_("cpv"), ["zer", "cpv"], ["cp2"])
-        av(c_("ca", 8), c_("nma", 8), ACT.Identity, 1.0, c_("cd"), ["nma", "cd"], ["ca"])
+        red(c_("xx"), T.qq[:, 0:34], ADD, ["qq", "qqc", "hn"], ["xx"])
+        own_pick()
         if last:
-            av(c_("fn"), c_("key"), ACT.Identity, TAGN, c_("jr"), ["key", "jr"], ["fn"])
-            av(c_("de", 4), c_("no", 4), ACT.Identity, -1.0, c_("fn"), ["no", "fn"], ["de"])
+            ts(c_("key"), EM, RQ, RQ, ADD, SUB, ["em"], ["key"])
         else:
             av(c_("de", 4), ae, ACT.Identity, -1.0, EM, [aek, "em"], ["de"])
-        tr(T.kt[:], T.bc[:], ["bc"], ["kt"])
-        ts(T.qq[:, 0:32], T.kt[:], c_("kp"), WT, EQ, MUL, ["kt", "kp"], ["qq"])
-        red(c_("xx"), T.qq[:, 0:33], ADD, ["qq", "qqc"], ["xx"])
-        ts(T.fb0[:, 0:32:16], c_("cp2", 2), c_("xx"), c_("apos"), MAX, MIN, ["xx", "cp2", "apos"], ["fb0a"])
-        ts(T.sb0[:, 0:32:4], c_("ca", 8), c_("xx"), 0.0, MAX, MIN, ["ca", "xx"], ["sb0a"])
-        weave(turn("fb", ["fb0", "fb0a"]), turn("sb", ["sb0", "sb0a"]))
-        weave(spread(lambda q: T.fo[q, :], T.fb3[Q0, 0:32:16], ["fb3"], "fo"))
-        tt(T.of16[:], T.sb3[:].indirect(RL), T.sc16[:], ADD, ["sb3", "RL", "sc16a", "sc16b"], ["of16"])
+        ts(T.fb0[:], T.cpo[:, 32:64], c_("xx"), c_("apos"), MAX, MIN, ["xx", "cpo", "apos"], ["fb0"])
+        ts(T.sb0[:, 0:32:4], c_("ca", 8), c_("xx"), OFF, MAX, MIN, ["ca", "xx", "off"], ["sb0a"])
+        if last:
+            ts(c_("jr"), EM, RJ, RJ, ADD, SUB, ["em"], ["jr"])
+            av(c_("fn"), c_("key"), ACT.Identity, TAGN, c_("jr"), ["key", "jr"], ["fn"])
+            av(c_("de", 4), c_("no", 4), ACT.Identity, -1.0, c_("fn"), ["no", "fn"], ["de"])
+        sbt = turn("sb", ["sb0", "sb0a"])
+        tr(T.fb1[:], T.fb0[:], ["fb0"], ["fb1"])
+        sbt[0]()
+        scan(T.fb2[:], T.msel[:], T.fb1[:], 0.0, MUL, MAX, ["msel", "fb1"], ["fb2"])
+        sbt[1]()
+        for a in range(4):
+            ts(T.fo[quad(a), :], T.fb2[Q0, 15:32:16], c_("off", 1, Q0), PU, SUB, MUL, ["fb2", "off"], ["fo%d" % a])
+        sbt[2]()
         rc, rs = window(t)
         pickc("fa", 0, 32, w, 0, 256, T.fo[:], four("fo") + rc, ["fa.fc"])
         picks("fa", 0, 32, w, 0, 256, T.fo[:], four("fo") + rs, ["fa.fs"])
         for b in range(4):
             mm("pd%d" % b, "ee", 128 * b, "fa", 0, 128, False, True,
                ["ee%d" % b, "fa.fc", "fa.fs", "fa.ac", "fa.as", "fa.z"])
-        weave(spread(lambda q: T.so[q, 0:8], T.of16[Q0, 0:8], ["of16"], "so"))
+        tt(T.of16[:], T.sb3[:].indirect(RL), T.sc16[:], ADD, ["sb3", "RL", "sc16a", "sc16b"], ["of16"])
+
+        def so_out():
+            for a in range(4):
+                ts(T.so[quad(a), 0:8], T.of16[Q0, 0:8], PU, None, MUL, None, ["of16"], ["so%d" % a])
+
         xo, xn = T["xs%d" % t], T["xs%d" % (t + 1)]
 
         def x_new(b):
@@ -524,6 +561,7 @@ def rank_program(g, core, T, topo):
             tt(T.et[:, 128 * k + b:128 * k + 128:4], T.bt[:, b:128:4], xn[:, b:128:4], SUB,
                ["bt", "x%d.%d" % (t + 1, b)], ["et.%d" % b])
 
+        so_out()
         if not last:
             x_new(0)
             x_new(1)
@@ -565,6 +603,7 @@ def rank_program(g, core, T, topo):
             store("s", T.px[:], T.pxs[:], ["pxs"])
             store("s", T.an[:], T.nn1[ka:ka + 4, :], ["nn1"])
             y_out(t, "a")
+    assert sum(v[1] for v in cols.values()) <= 192
 
     for s in ("sv", "sa", "sp", "sg", "ls"):
         g.wait_ge(T.sem[s], count[s])

@@ -41,11 +41,11 @@ for _n, _c, _d in (
         ("sm", 200, F32), ("si", 16, I32), ("acti", 8, I32), ("af", 8, F32), ("ae0", 16, F32),
         ("zer", 32, F32), ("tm", 32, F32), ("kt", 32, F32), ("kp", 32, F32), ("qq", 40, F32), ("sc16", 16, F32),
         ("nbw", 40, F32), ("khw", 40, F32), ("plw", 40, F32), ("kho", 64, F32), ("cpo", 64, F32), ("gb", 32, F32),
-        ("ms1", 32, F32), ("ms2", 32, F32), ("msel", 32, F32),
+        ("j16", 32, F32), ("msel", 32, F32), ("zy", 64, F32),
         ("sc8", 8, F32), ("of16", 16, F32), ("i8", 8, F32), ("v8", 8, F32),
         ("cu", 16, U16), ("ho", 16, U16), ("so", 16, U16), ("fo", 2, U16), ("ao", 2, U16), ("aoff", 8, U16)):
     _sb(_n, _c, _d)
-for _n, _k in (("z", 4), ("sb", 4), ("fb", 3), ("ab", 4), ("nn", 2)):
+for _n, _k in (("z", 2), ("sb", 4), ("fb", 3), ("ab", 3), ("nn", 2)):
     for _s in range(_k):
         _sb(_n + str(_s), 32, F32)
 for _n in ("pd0", "pd1", "pd2", "pd3", "ps1", "ps2", "pa", "py"):
@@ -62,19 +62,14 @@ X = AxisListType.X
 ACT = ActivationFunctionType
 BIG = float(2 ** 20)
 PU = 1024.0
+ZU = 2048.0
 RQ = 1.5 * 2.0 ** 33
 RJ = 1.5 * 2.0 ** 23
 TAGN = A / QS - 1.0
 
 
-def shuffle_cols(k):
-    far = [s for s in range(G) if s // 2 != k // 2]
-    return {k: 12, k ^ 1: 4, far[0]: 0, far[1]: 8}
-
-
 def places(k):
-    col = shuffle_cols(k)
-    return sorted(range(G), key=lambda s: col[s])
+    return [s for s in range(G) if s // 2 != k // 2] + [k ^ 1, k]
 
 
 def bits(es):
@@ -96,7 +91,6 @@ def rank_program(g, core, T, topo):
     grp, k, mate = list(T.cores[rank % 2::2]), rank // 2, T.cores[rank ^ 1]
     qlow = 2 * k
     own0 = 0 if rank == qlow else HI
-    col = shuffle_cols(k)
     order = places(k)
     peers = [grp[s] for s in range(G) if s != k]
     Q0 = slice(32 * k, 32 * k + 32)
@@ -230,6 +224,9 @@ def rank_program(g, core, T, topo):
                 lambda: cp(T[n + "2"][:], T[n + "1"][:].indirect(GL), [n + "1", "GL"], [n + "2"]),
                 lambda: tr(T[n + "3"][:], T[n + "2"][:], [n + "2"], [n + "3"])]
 
+    def choose(out, src, r, w):
+        scan(out, T.msel[:], src, 0.0, MUL, MAX, ["msel"] + r, w)
+
     def quad(a):
         return slice(32 * a, 32 * a + 32)
 
@@ -263,9 +260,6 @@ def rank_program(g, core, T, topo):
     iota(T.si[:, 0:1], [[1, 1]], 0, 1, ["pi"], False)
     iota(T.v516[:], [[1, 129], [1000, 4]], -3000, -1, ["v516"])
     iota(T.j2[:], [[0, 4], [1, 32]], ka, -1, ["j2"])
-    iota(T.i8[:], [[0, 2], [1, 4]], 0, 0, ["i8"])
-    iota(T.sc8[:], [[32, 4], [16, 2]], 128, 0, ["sc8"])
-    iota(T.v8[:], [[-(16 * QS + 1), G], [-8 * QS, 2]], 8 * QS * (N - 1) + G - 1, 0, ["v8"])
 
     J0 = T.j2[:, 0:1]
     av(T.av[:], T.v516[:], ACT.Abs, 1.0, 0.0, ["v516"], ["av"])
@@ -277,15 +271,11 @@ def rank_program(g, core, T, topo):
     av(T.d4[:], T.aj[:], ACT.Relu, -1.0, 1.0, ["aj"], ["d4"])
     av(T.kp4[:], T.aj[:], ACT.Sign, 1.0, 0.0, ["aj"], ["kp4"])
     av(c_("ni128"), J0, ACT.Identity, 1.0 / PU, -128.0 / PU, ["j2"], ["ni128"])
-    av(c_("ic"), J0, ACT.Identity, -1.0, 0.0, ["j2"], ["ic"])
     av(T.tm[:], T.j2[:, 0:32], ACT.Relu, BIG, BIG, ["j2"], ["tm"])
-    av(T.ms1[:], T.aj[:, 0:32], ACT.Abs, 1.0, -8.0, ["aj"], ["ms1"])
-    av(T.ms2[:], T.ms1[:], ACT.Abs, 1.0, -8.0, ["ms1"], ["ms2"])
-    av(T.msel[:], T.ms2[:], ACT.Sign, 1.0, 0.0, ["ms2"], ["msel"])
 
     ms(T.et[:], 0.0, four("et."))
     ms(T.zer[:], 0.0, ["zer"])
-    for n in ("sb0", "ab0", "nn0"):
+    for n in ("sb0", "nn0"):
         ms(T[n][:], 0.0, [n, n + "a"])
     ms(T.sc16[:, 8:16], 0.0, ["sc16b"])
     PI = T.si[:, 0:1]
@@ -306,6 +296,9 @@ def rank_program(g, core, T, topo):
     OFF = c_("off")
     av(c_("i128"), c_("ni128"), ACT.Identity, -1.0, OFF, ["ni128", "off"], ["i128"])
     av(T.qq[:, 32:33], OFF, ACT.Identity, 1.0, -(CAPP - 0.5), ["off"], ["qqc"])
+    av(c_("off2"), OFF, ACT.Identity, ZU, 0.0, ["off"], ["off2"])
+    av(c_("off3"), OFF, ACT.Identity, ZU, float(HI - own0), ["off"], ["off3"])
+    av(c_("ic"), J0, ACT.Identity, -1.0, c_("off2"), ["j2", "off2"], ["ic"])
 
     def send_e(t):
         es = topo.engines(core, peers[0])
@@ -317,6 +310,8 @@ def rank_program(g, core, T, topo):
         arrives("ae%d" % t, (len(e1) + len(e2)) * len(peers), ["eg%d.r" % t])
 
     send_e(0)
+    iota(T.i8[:], [[0, 2], [1, 4]], 0, 0, ["i8"])
+    iota(T.v8[:], [[-(16 * QS + 1), G], [-8 * QS, 2]], 8 * QS * (N - 1) + G - 1, 0, ["v8"])
     cp(T.cu[:, 1:2], T.si[:, 1:2], ["p31", "GLa"], ["GL"])
     ts(T.cu[:, 3:4], T.si[:, 2:3], 16.0, None, ADD, None, ["p15", "ELa"], ["EL"])
     ts(AL, T.si[:, 3:4], 2.0, c_("pg"), MUL, ADD, ["p3", "pgf"], ["AL"])
@@ -328,6 +323,8 @@ def rank_program(g, core, T, topo):
     send([xfer(bytes_of("at", own0, own0 + A), [(mate, bytes_of("at", own0, own0 + A))], es, "aa")], ["at.o"])
     send([xfer(T.ats[:, own0:own0 + A], [(mate, T.ats[:, own0:own0 + A])], es, "aa")], ["at.o"])
     arrives("aa", 2 * len(topo.engines(mate, core)), ["at.r"])
+    iota(T.sc8[:], [[32, 4], [16, 2]], 128, 0, ["sc8"])
+    iota(T.j16[:], [[0, 2], [-1, 16]], 15, 0, ["j16"])
 
     def own_e(t):
         pickc("eg%d" % t, ka, kb, "qe%d" % t, ka, kb, EL, ["EL", "qe%d" % t], ["eg%d.c" % t])
@@ -356,7 +353,7 @@ def rank_program(g, core, T, topo):
             lambda: ts(c_("nm", 8), T.i8[:], c_("aslot"), BIG, NE, MUL, ["i8", "aslot"], ["nm"]),
             lambda: av(c_("apr"), c_("aslot"), ACT.Identity, 32.0, c_("ic"), ["aslot", "ic"], ["apr"]),
             lambda: av(c_("apos"), c_("aslot"), ACT.Identity, 32.0 / PU, c_("i128"), ["aslot", "i128"], ["apos"]),
-            lambda: av(T.ab0[:, 0:32:16], T.zer[:, 0:2], ACT.Identity, 1.0, c_("apr"), ["zer", "apr"], ["ab0a"]),
+            lambda: av(T.ab0[:], T.zer[:], ACT.Identity, 1.0, c_("apr"), ["zer", "apr"], ["ab0"]),
             lambda: av(c_("napos"), c_("aslot"), ACT.Identity, -32.0 / PU, c_("ni128"), ["aslot", "ni128"], ["napos"]),
             lambda: av(c_("nma", 8), c_("nm", 8), ACT.Identity, 1.0, c_("napos"), ["nm", "napos"], ["nma"])]
 
@@ -420,8 +417,9 @@ def rank_program(g, core, T, topo):
     ms(T.plw[:, 8:40], 0.0, ["plc"])
     weave([unit(b, 0) for b in range(4)])
     av(T.plw[:, 0:8], c_("pl8", 8), ACT.Identity, 256.0 / PU, OFF, ["pl8", "off"], ["plw"])
-    weave(a_scores() + a_chain(), [unit(b, 1) for b in range(2)] + best_active(0) + [unit(b, 1) for b in range(2, 4)])
+    weave(a_scores() + a_chain(), [unit(b, 1) for b in range(4)])
     ts(T.sc16[:, 0:8], T.sc8[:], 1.0 / PU, c_("soc"), MUL, ADD, ["sc8", "soc"], ["sc16a"])
+    ts(T.msel[:], T.j16[:], OFF, None, NE, None, ["j16", "off"], ["msel"])
     quant("fa", 32, 160, T.dtile[:, 0:512], ["dtile"], ["fa.ac", "fa.as", "fa.z"])
 
     for t in range(R):
@@ -445,35 +443,42 @@ def rank_program(g, core, T, topo):
                                          bias=T.r21[:, r0 + A - 1:r0 + A], scale=-1.0, accum_out=C1 if r0 else C2),
                [rk], [mk + "." + rk, "junk" + rk])
         c1k, c2k = mk + ".r1", mk + ".r2"
+        ba = best_active(t)
+        ba[0]()
         cp(ml[:, m0:m0 + 4:2], T.r21[:, A - 1:2 * A:A], ["r1", "r2"], [mk + ".m"])
         mine = [mk + ".m", c1k, c2k]
         mv = ml[:, m0:m0 + 4]
         send([xfer(mv, [(c, mv) for c in peers], topo.engines(core, peers[0]), "am%d" % t)], mine)
         arrives("am%d" % t, sum(len(topo.engines(c, core)) for c in peers), [mk + ".r"])
-        zw = ["z0"] + four("z.") + ["zz0", "zz1"]
-        if own0:
-            ts(T.gb[:], T.zer[:], M2, M1, ADD, LE, ["zer", "r1", "r2"], ["gb"])
-            ts(c_("gh"), M2, M1, None, GT, None, ["r1", "r2"], ["gh"])
-            ts(c_("rest"), C2, float(HI), c_("gh"), ADD, MUL, ["gh", c2k], ["rest"])
-            ts(T.z0[:], T.gb[:], C1, c_("rest"), MUL, ADD, ["gb", c1k, "rest"], zw)
-        else:
-            ts(T.gb[:], T.zer[:], M2, M1, ADD, GT, ["zer", "r1", "r2"], ["gb"])
-            ts(c_("gh"), M2, M1, None, LE, None, ["r1", "r2"], ["gh"])
-            ts(c_("gi"), M2, M1, float(HI), GT, MUL, ["r1", "r2"], ["gi"])
-            ts(c_("rest"), C1, c_("gh"), c_("gi"), MUL, ADD, ["gh", "gi", c1k], ["rest"])
-            ts(T.z0[:], T.gb[:], C2, c_("rest"), MUL, ADD, ["gb", c2k, "rest"], zw)
-        for s in range(G):
-            o = s ^ 1
-            cp(T.z0[32 * o:32 * o + 32, col[s]:32:16], T.z0[32 * s:32 * s + 32, col[s]:32:16], ["z0"], ["z.%d" % s])
+        CF, cfk, CL, clk = (C2, c2k, C1, c1k) if own0 else (C1, c1k, C2, c2k)
+        ts(T.gb[:], T.zer[:], M2, M1, ADD, LE if own0 else GT, ["zer", "r1", "r2"], ["gb"])
+        ts(c_("gh"), M2, M1, None, GT if own0 else LE, None, ["r1", "r2"], ["gh"])
+        ts(c_("gu"), CF, float(HI if own0 else -HI), None, ADD, None, [cfk], ["gu"])
+        ts(c_("rest"), c_("gu"), c_("gh"), c_("off3"), MUL, ADD, ["gh", "gu", "off3"], ["rest"])
+        ts(T.z0[:], T.gb[:], CL, c_("rest"), MUL, ADD, ["gb", clk, "rest"], ["z0"])
+        ba[1]()
+        tr(T.z1[:], T.z0[:], ["z0"], ["z1"])
+        ba[2]()
+        choose(T.zy[:, 0:32], T.z1[:], ["z1"], ["zya", "zc0", "zc2"])
+        choose(T.zy[:, 32:64], T.z1[:], ["z1"], ["zyb", "zc1", "zc3"])
+        ba[3]()
+        ba[4]()
         for h in range(2):
-            a = min(col[2 * h], col[2 * h + 1])
-            cp(T.z0[64 - 64 * h:128 - 64 * h, a:32:8], T.z0[64 * h:64 * h + 64, a:32:8],
-               ["z.%d" % (2 * h), "z.%d" % (2 * h + 1)], ["zz%d" % h])
-        weave(turn("z", zw), turn("ab", ["ab0", "ab0a"]))
-        cp(T.ho[:], T.z3[:].indirect(RL), ["z3", "RL"], ["ho"])
-        apk = spread(lambda q: T.ao[q, :], T.ab3[Q0, 0:32:16], ["ab3"], "ao")
-        apk[0]()
-        hk = ["ho", "at.o", "at.r"]
+            f, s = order[2 * h], order[2 * h + 1]
+            cp(T.zy[quad(s), 15:32:16], T.zy[quad(f), 15:32:16], ["zya"], ["zc%d" % (2 * h)])
+        for h in range(2):
+            f, s = order[2 * h], order[2 * h + 1]
+            cp(T.zy[quad(f), 47:64:16], T.zy[quad(s), 47:64:16], ["zyb"], ["zc%d" % (2 * h + 1)])
+        tr(T.ab1[:], T.ab0[:], ["ab0"], ["ab1"])
+        for h in range(2):
+            src = slice(64 * (order[2 * h] // 2), 64 * (order[2 * h] // 2) + 64)
+            for d in range(2):
+                ts(T.ho[64 * d:64 * d + 64, 4 * h:4 * h + 4], T.zy[src, 15:64:16], c_("off2", 1, src), None, SUB, None,
+                   ["zya", "zyb", "zc%d" % (2 * h), "zc%d" % (2 * h + 1), "off2"], ["ho%d" % (2 * h + d)])
+        choose(T.ab2[:], T.ab1[:], ["ab1"], ["ab2"])
+        apk = [lambda a=a: ts(T.ao[quad(a), :], T.ab2[Q0, 15:32:16], c_("off2", 1, Q0), None, SUB, None,
+                              ["ab2", "off2"], ["ao%d" % a]) for a in range(4)]
+        hk = four("ho") + ["at.o", "at.r"]
         pickc(pk, 0, 96, "at", 0, AW, T.ho[:, 0:6], hk, [pk + ".c"])
         picks(pk, 0, 96, "at", 0, AW, T.ho[:, 0:6], hk, [pk + ".s"])
         ec, esc = splits(topo.engines(core, peers[0]))
@@ -502,6 +507,7 @@ def rank_program(g, core, T, topo):
         SC, CC = ml[:, 0:16:2], ml[:, 1:16:2]
         EM = T.sm[:, 199:200]
         HN = T.qq[:, 33:34]
+        apk[0]()
         apk[1]()
         red(c_("best"), SC, MAX, allm, ["best"])
         tt(c_("h8", 8), CC, c_("ak8", 8), EQ, allm + ["ak8"], ["h8"])
@@ -521,31 +527,38 @@ def rank_program(g, core, T, topo):
         a_side()
         red(c_("xx"), T.qq[:, 0:34], ADD, ["qq", "qqc", "hn"], ["xx"])
         own_pick()
-        if last:
-            ts(c_("key"), EM, RQ, RQ, ADD, SUB, ["em"], ["key"])
-        else:
+        if not last:
             av(c_("de", 4), ae, ACT.Identity, -1.0, EM, [aek, "em"], ["de"])
-        ts(T.fb0[:], T.cpo[:, 32:64], c_("xx"), c_("apos"), MAX, MIN, ["xx", "cpo", "apos"], ["fb0"])
-        ts(T.sb0[:, 0:32:4], c_("ca", 8), c_("xx"), OFF, MAX, MIN, ["ca", "xx", "off"], ["sb0a"])
-        if last:
-            ts(c_("jr"), EM, RJ, RJ, ADD, SUB, ["em"], ["jr"])
-            av(c_("fn"), c_("key"), ACT.Identity, TAGN, c_("jr"), ["key", "jr"], ["fn"])
-            av(c_("de", 4), c_("no", 4), ACT.Identity, -1.0, c_("fn"), ["no", "fn"], ["de"])
         sbt = turn("sb", ["sb0", "sb0a"])
-        tr(T.fb1[:], T.fb0[:], ["fb0"], ["fb1"])
-        sbt[0]()
-        scan(T.fb2[:], T.msel[:], T.fb1[:], 0.0, MUL, MAX, ["msel", "fb1"], ["fb2"])
-        sbt[1]()
-        for a in range(4):
-            ts(T.fo[quad(a), :], T.fb2[Q0, 15:32:16], c_("off", 1, Q0), PU, SUB, MUL, ["fb2", "off"], ["fo%d" % a])
-        sbt[2]()
         rc, rs = window(t)
-        pickc("fa", 0, 32, w, 0, 256, T.fo[:], four("fo") + rc, ["fa.fc"])
-        picks("fa", 0, 32, w, 0, 256, T.fo[:], four("fo") + rs, ["fa.fs"])
-        for b in range(4):
-            mm("pd%d" % b, "ee", 128 * b, "fa", 0, 128, False, True,
-               ["ee%d" % b, "fa.fc", "fa.fs", "fa.ac", "fa.as", "fa.z"])
-        tt(T.of16[:], T.sb3[:].indirect(RL), T.sc16[:], ADD, ["sb3", "RL", "sc16a", "sc16b"], ["of16"])
+
+        def f_val():
+            ts(T.fb0[:], T.cpo[:, 32:64], c_("xx"), c_("apos"), MAX, MIN, ["xx", "cpo", "apos"], ["fb0"])
+
+        def s_val():
+            ts(T.sb0[:, 0:32:4], c_("ca", 8), c_("xx"), OFF, MAX, MIN, ["ca", "xx", "off"], ["sb0a"])
+
+        def f_tr():
+            tr(T.fb1[:], T.fb0[:], ["fb0"], ["fb1"])
+
+        def f_choose():
+            choose(T.fb2[:], T.fb1[:], ["fb1"], ["fb2"])
+
+        def f_out():
+            for a in range(4):
+                ts(T.fo[quad(a), :], T.fb2[Q0, 15:32:16], c_("off", 1, Q0), PU, SUB, MUL, ["fb2", "off"], ["fo%d" % a])
+
+        def f_pick():
+            pickc("fa", 0, 32, w, 0, 256, T.fo[:], four("fo") + rc, ["fa.fc"])
+            picks("fa", 0, 32, w, 0, 256, T.fo[:], four("fo") + rs, ["fa.fs"])
+
+        def f_mm():
+            for b in range(4):
+                mm("pd%d" % b, "ee", 128 * b, "fa", 0, 128, False, True,
+                   ["ee%d" % b, "fa.fc", "fa.fs", "fa.ac", "fa.as", "fa.z"])
+
+        def s_add():
+            tt(T.of16[:], T.sb3[:].indirect(RL), T.sc16[:], ADD, ["sb3", "RL", "sc16a", "sc16b"], ["of16"])
 
         def so_out():
             for a in range(4):
@@ -561,8 +574,8 @@ def rank_program(g, core, T, topo):
             tt(T.et[:, 128 * k + b:128 * k + 128:4], T.bt[:, b:128:4], xn[:, b:128:4], SUB,
                ["bt", "x%d.%d" % (t + 1, b)], ["et.%d" % b])
 
-        so_out()
         if not last:
+            weave([f_val, s_val, f_tr, sbt[0], f_choose, sbt[1], f_out, sbt[2], f_pick, f_mm, s_add, so_out])
             x_new(0)
             x_new(1)
             e_new(0)
@@ -578,31 +591,47 @@ def rank_program(g, core, T, topo):
             own_e(t + 1)
             nx, nk = act_e(t + 1)
             weave(a_scores(), renew(ae, aek, c_("de", 4), "de", nx, nk))
-            weave(a_chain(), best_active(t + 1))
+            side = []
             if t == 0:
-                quant("wq", 0, 256, T.wt[:], ["wt"], ["wq"])
+                side = [lambda: quant("wq", 0, 256, T.wt[:], ["wt"], ["wq"])]
             if t + 1 == R - 1:
-                ts(c_("k4", 4), nx, RQ, RQ, ADD, SUB, [nk], ["k4"])
-                ts(c_("j4", 4), nx, RJ, RJ, ADD, SUB, [nk], ["j4"])
-                ts(c_("k5", 4), c_("k4", 4), TAGN, None, MUL, None, ["k4"], ["k5"])
-                tt(c_("no", 4), c_("k5", 4), c_("j4", 4), ADD, ["k5", "j4"], ["no"])
+                side = [lambda: ts(c_("k4", 4), nx, RQ, RQ, ADD, SUB, [nk], ["k4"]),
+                        lambda: ts(c_("j4", 4), nx, RJ, RJ, ADD, SUB, [nk], ["j4"]),
+                        lambda: ts(c_("k5", 4), c_("k4", 4), TAGN, None, MUL, None, ["k4"], ["k5"]),
+                        lambda: tt(c_("no", 4), c_("k5", 4), c_("j4", 4), ADD, ["k5", "j4"], ["no"])]
+            weave(a_chain(), side)
         else:
             wl = "win%d" % R
             rn = renew(c_("no", 4), "no", c_("de", 4), "de", T.nn0[:, 0:4], "nn0a")
-            rn[0]()
+            weave([s_val, f_val, sbt[0], f_tr, sbt[1], f_choose, sbt[2]])
+            ts(c_("key"), EM, RQ, RQ, ADD, SUB, ["em"], ["key"])
+            s_add()
+            ts(c_("jr"), EM, RJ, RJ, ADD, SUB, ["em"], ["jr"])
+            so_out()
+            f_out()
             slot_pick(t)
+            f_pick()
             y_mm(t)
+            f_mm()
+            av(c_("fn"), c_("key"), ACT.Identity, TAGN, c_("jr"), ["key", "jr"], ["fn"])
+            av(c_("de", 4), c_("no", 4), ACT.Identity, -1.0, c_("fn"), ["no", "fn"], ["de"])
             store("s", T.oc[:], bytes_of(wl, 128, 256), [wl + ".sc"])
-            for a in range(4):
-                store("s" if a < 2 else "a", T.osc[4 * a:4 * a + 4, :], T[wl + "s"][32 * a:32 * a + 4, 128:256], [wl + ".ss"])
-            weave([lambda b=b: x_new(b) for b in range(4)])
+            for a in range(2):
+                store("s", T.osc[4 * a:4 * a + 4, :], T[wl + "s"][32 * a:32 * a + 4, 128:256], [wl + ".ss"])
+            rn[0]()
+            ys = T["ys%d" % t]
+            op("a", lambda: S.activation(ys[:, 0:128], T.py[:, 0:128], ACT.Copy), ["Ppy"], ["ys.0"])
+            cp(ys[:, 128:256], T.pa[:, 0:128], ["Ppa"], ["ys.1"])
+            store("a", T.y[:, 256 * t:256 * t + 256], ys[:], ["ys.0", "ys.1"])
+            for a in range(2, 4):
+                store("a", T.osc[4 * a:4 * a + 4, :], T[wl + "s"][32 * a:32 * a + 4, 128:256], [wl + ".ss"])
             rn[1]()
-            cp(T.pxs[:], xn[:], four("x%d." % R), ["pxs"])
+            weave([lambda b=b: x_new(b) for b in range(4)])
             rn[2]()
+            cp(T.pxs[:], xn[:], four("x%d." % R), ["pxs"])
             tr(T.nn1[:], T.nn0[:], ["nn0", "nn0a"], ["nn1"])
             store("s", T.px[:], T.pxs[:], ["pxs"])
             store("s", T.an[:], T.nn1[ka:ka + 4, :], ["nn1"])
-            y_out(t, "a")
     assert sum(v[1] for v in cols.values()) <= 192
 
     for s in ("sv", "sa", "sp", "sg", "ls"):

@@ -3,9 +3,9 @@ from concourse.mybir import dt, AluOpType, AxisListType, ActivationFunctionType
 
 N, A, M, CAPP, R, O = 8, 384, 32, 4, 3, 2
 G = N // 2
-QS = 1024
-HI = QS
-AW = HI + A
+HI = A
+AW = 2 * A
+NP = 1
 C8, U8, F32, BF, U16, I32 = "float8_e4m3fn_x4", "uint8", "float32", "bfloat16", "uint16", "int32"
 
 SCRATCH = {}
@@ -21,39 +21,39 @@ def _mx(name, cols):
 
 
 _mx("at", AW)
-_mx("fa", 160)
 _mx("ee", 1024)
 _mx("wq", 256)
 for _t in range(R):
     _mx("qe%d" % _t, 128)
     _mx("eg%d" % _t, 128)
     _mx("pk%d" % _t, 96)
+    _mx("fa%d" % _t, 128)
     _sb("ml%d" % _t, 16, F32)
-    _sb("ys%d" % _t, 256, F32)
+    _sb("xw%d" % _t, 1024, BF)
 for _t in range(R + 1):
     _mx("win%d" % _t, 256)
-    _sb("xs%d" % _t, 128, BF)
 for _n, _c, _d in (
-        ("dtile", 4 * A, BF), ("wt", 1024, BF), ("bt", 128, BF), ("et", 512, BF), ("pxs", 128, F32),
-        ("v516", 516, BF), ("av", 516, BF), ("ua", 516, BF), ("ub", 516, BF), ("na", 516, BF), ("nb", 516, BF),
-        ("j2", 128, F32), ("aj", 128, F32), ("d4", 128, F32), ("kp4", 128, F32), ("am", 128, F32), ("asc", 128, F32),
-        ("neg", A, F32), ("r21", 2 * A, F32), ("junk", 2 * A, BF),
-        ("sm", 200, F32), ("si", 16, I32), ("acti", 8, I32), ("af", 8, F32), ("ae0", 16, F32),
-        ("zer", 32, F32), ("tm", 32, F32), ("kt", 32, F32), ("kp", 32, F32), ("qq", 40, F32), ("sc16", 16, F32),
-        ("nbw", 40, F32), ("khw", 40, F32), ("plw", 40, F32), ("kho", 64, F32), ("cpo", 64, F32), ("gb", 32, F32),
-        ("j16", 32, F32), ("msel", 32, F32), ("zy", 64, F32),
-        ("sc8", 8, F32), ("of16", 16, F32), ("i8", 8, F32), ("v8", 8, F32),
-        ("cu", 16, U16), ("ho", 16, U16), ("so", 16, U16), ("fo", 2, U16), ("ao", 2, U16), ("aoff", 8, U16)):
+        ("dtile", 4 * A, BF), ("wt", 1024, BF), ("bt", 128, BF), ("xs", 128, BF), ("et", 512, BF), ("pxs", 128, F32),
+        ("ua", 516, BF), ("ub", 516, BF), ("na", 516, BF), ("nb", 516, BF), ("zb", A, BF), ("junk", 2 * A, BF),
+        ("jd", 128, F32), ("ad", 128, F32), ("j2", 128, F32), ("aj", 128, F32), ("d4", 128, F32), ("kp4", 128, F32),
+        ("am", 128, F32), ("asc", 128, F32), ("r21", 2 * A, F32), ("ci", 128, I32), ("cj", 128, I32), ("c4", 32, I32),
+        ("cw", 128, F32), ("cu1", 128, F32), ("caps", 128, F32), ("cap4", 32, F32), ("u4", 64, F32),
+        ("sbk", 128, F32), ("c32", 128, F32), ("n1", 128, F32), ("nmb", 128, F32),
+        ("ab0", 128, F32), ("ab1", 128, F32), ("ab2", 128, F32), ("zs0", 128, F32), ("zs1", 128, F32), ("zs2", 128, F32),
+        ("ys0", 256, F32), ("yw", 512, F32), ("yo", 256, F32),
+        ("sm", 128, F32), ("si", 16, I32), ("acti", 8, I32), ("af", 8, F32), ("ae0", 16, F32),
+        ("tm", 32, F32), ("kt", 32, F32), ("kp", 32, F32), ("qq", 66, F32), ("cpw", 66, F32), ("vv", 66, F32),
+        ("nbw", 40, F32), ("khw", 40, F32), ("kho", 40, F32), ("gb", 64, F32), ("msel", 64, F32),
+        ("z0", 64, F32), ("z1", 64, F32), ("zy", 64, F32), ("fb1", 32, F32), ("fb2", 32, F32),
+        ("nn0", 32, F32), ("nn1", 32, F32), ("k8", 8, F32), ("p8", 8, F32),
+        ("cu", 16, U16), ("ho", 8, U16), ("so", 8, U16), ("fo", 8, U16), ("ao", 8, U16), ("aoff", 8, U16)):
     _sb(_n, _c, _d)
-for _n, _k in (("z", 2), ("sb", 4), ("fb", 3), ("ab", 3), ("nn", 2)):
-    for _s in range(_k):
-        _sb(_n + str(_s), 32, F32)
 for _n in ("pd0", "pd1", "pd2", "pd3", "ps1", "ps2", "pa", "py"):
     SCRATCH[_n] = ("psum", [128, 512], F32)
 
-SEMAPHORES = ["sv", "sa", "sp", "sg", "ls", "lx", "lb", "ld", "lw", "la", "st", "aa"]
+SEMAPHORES = ["sv", "sa", "sp", "sg", "ls", "lx", "lb", "lw", "la", "st", "aa"]
 for _t in range(R):
-    SEMAPHORES += ["ae%d" % _t, "am%d" % _t, "ac%d" % _t, "as%d" % _t]
+    SEMAPHORES += ["ae%d" % _t, "am%d" % _t, "ac%d" % _t, "ld%d" % _t]
 
 ADD, SUB, MUL, MAX, MIN = AluOpType.add, AluOpType.subtract, AluOpType.mult, AluOpType.max, AluOpType.min
 EQ, NE, GT, LT, LE = AluOpType.is_equal, AluOpType.not_equal, AluOpType.is_gt, AluOpType.is_lt, AluOpType.is_le
@@ -63,9 +63,8 @@ ACT = ActivationFunctionType
 BIG = float(2 ** 20)
 PU = 1024.0
 ZU = 2048.0
-RQ = 1.5 * 2.0 ** 33
-RJ = 1.5 * 2.0 ** 23
-TAGN = A / QS - 1.0
+ISSUE, HOP, LOAD, SX, SLACK = 0.25, 1.5, 1.6, 0.03, 1.0
+CASES = ((0.12, 0.3), (0.17, 0.0), (0.2, -0.2))
 
 
 def places(k):
@@ -84,13 +83,103 @@ def splits(es):
     return ([es[:2 * q], es[2 * q:3 * q], es[3 * q:]], [es[:q], es[q:2 * q], es[2 * q:]])
 
 
+def arrange(nodes):
+    wr, rd, pred, soft = {}, {}, [], []
+    for i, (q, _, reads, writes, _, _) in enumerate(nodes):
+        ps = set()
+        soft.append(set(wr[key] for key in reads if key[0] == "#" and q != "r"))
+        for key in reads:
+            ps.add(wr[key])
+            if key[0] == "P":
+                ps.update(j for j in rd.get(key, []) if nodes[j][0] != q or len(q) > 1)
+        for key in writes:
+            ps.update(rd.get(key, []))
+            if key in wr:
+                ps.add(wr[key])
+        ps.discard(i)
+        pred.append(sorted(ps))
+        for key in reads:
+            rd.setdefault(key, []).append(i)
+        for key in writes:
+            wr[key] = i
+            rd[key] = []
+    n = len(nodes)
+    succ = [[] for _ in nodes]
+    for j in range(n):
+        for i in pred[j]:
+            succ[i].append(j)
+
+    def span(i, where, case):
+        q = nodes[i][0]
+        return nodes[i][4][where[i]] if len(q) > 1 else nodes[i][5] + (case[1] if q == "r" and nodes[i][5] else 0.0)
+
+    def lat(i, j, where, case):
+        if i in soft[j]:
+            return nodes[i][4][where[i]]
+        free = nodes[j][0] == "r" or nodes[i][0] == nodes[j][0] == "p"
+        return span(i, where, case) + (0.0 if free else case[0])
+
+    def forward(key, case):
+        start, where, seq = {}, {}, []
+        free = {q: 0.0 for q in "vapgsr"}
+        left = [len(p) for p in pred]
+        ready = {j: 0.0 for j in range(n) if not pred[j]}
+        late = -min(key)
+        while ready:
+            t, q = min((max(free[q], r), q) for j, r in ready.items() for q in nodes[j][4])
+            mine = [(key[j], j) for j in ready if q in nodes[j][4]]
+            soon = [(ku, u) for ku, u in mine if ready[u] > t + 1e-9]
+            j = None
+            for kj, c in sorted(e for e in mine if ready[e[1]] <= t + 1e-9):
+                end = t + nodes[c][4][q]
+                if all(ready[u] >= end - 1e-9 or ku >= kj or end - ku <= late - SLACK
+                       or end - ku <= ready[u] + nodes[u][4][q] - kj for ku, u in soon):
+                    j = c
+                    break
+            if j is None:
+                free[q] = min(ready[u] for _, u in soon)
+                continue
+            del ready[j]
+            start[j], where[j] = t, q
+            seq.append(j)
+            late = max(late, t - key[j])
+            if q != "r":
+                free[q] = t + nodes[j][4][q]
+            for s in succ[j]:
+                left[s] -= 1
+                if not left[s]:
+                    ready[s] = max(start[i] + lat(i, s, where, case) for i in pred[s])
+        return seq, where
+
+    def length(seq, where, case):
+        start, free, end = {}, {}, 0.0
+        for j in seq:
+            q = where[j]
+            start[j] = max([start[i] + lat(i, j, where, case) for i in pred[j]] + [free.get(q, 0.0)])
+            if q != "r":
+                free[q] = start[j] + nodes[j][4][q]
+            end = max(end, start[j] + span(j, where, case))
+        return end
+
+    best = None
+    first = {j: nodes[j][0][-1] for j in range(n)}
+    for case in CASES:
+        key = [0.0] * n
+        for i in range(n - 1, -1, -1):
+            key[i] = min([key[j] - lat(i, j, first, case) for j in succ[i]] + [-span(i, first, case)])
+        seq, where = forward(key, case)
+        cost = sum(length(seq, where, c) for c in CASES)
+        if best is None or cost < best[0]:
+            best = (cost, seq, where)
+    return [(j, best[2][j]) for j in best[1]]
+
+
 def rank_program(g, core, T, topo):
     rank = T.rank_of(core)
     if rank is None:
         return
     grp, k, mate = list(T.cores[rank % 2::2]), rank // 2, T.cores[rank ^ 1]
-    qlow = 2 * k
-    own0 = 0 if rank == qlow else HI
+    own0 = 0 if rank == 2 * k else HI
     order = places(k)
     peers = [grp[s] for s in range(G) if s != k]
     Q0 = slice(32 * k, 32 * k + 32)
@@ -98,7 +187,7 @@ def rank_program(g, core, T, topo):
 
     queues = {"v": g.vector, "a": g.scalar, "p": g.tensor, "g": g, "s": g.sync}
     semof = {"v": "sv", "a": "sa", "p": "sp", "g": "sg"}
-    count = {}
+    count, nodes = {}, []
     clock = {q: {} for q in queues}
     wr, rd = {}, {}
 
@@ -108,8 +197,7 @@ def rank_program(g, core, T, topo):
         for tk in toks:
             if ck.get(tk[0], 0) < tk[1] and best.get(tk[0], (0, 0))[1] < tk[1]:
                 best[tk[0]] = tk
-        todo = sorted(best.values(), key=lambda tk: -len(tk[2]))
-        for tk in todo:
+        for tk in sorted(best.values(), key=lambda tk: -len(tk[2])):
             if ck.get(tk[0], 0) >= tk[1]:
                 continue
             queues[q].wait_ge(T.sem[tk[0]], tk[1])
@@ -120,7 +208,8 @@ def rank_program(g, core, T, topo):
     def deps(q, reads, writes):
         toks = []
         for key in reads:
-            assert key in wr, key
+            if key[0] == "#":
+                continue
             toks += wr[key]
             if key[0] == "P":
                 toks += [tk for tk in rd.get(key, []) if tk[3] != q]
@@ -137,22 +226,29 @@ def rank_program(g, core, T, topo):
             wr[key] = [tk]
             rd[key] = []
 
-    def op(q, fn, reads, writes, sem=None, n=1):
-        deps(q, reads, writes)
-        sem = sem or semof[q]
-        fn().then_inc(T.sem[sem], n)
-        count[sem] = count.get(sem, 0) + n
-        ck = dict(clock[q])
-        ck[sem] = count[sem]
-        note((sem, count[sem], ck, q), reads, writes)
+    def op(qs, fn, reads, writes, hold, sem=None, n=1, last=None):
+        if len(qs) == 1:
+            fn, hold = {qs: fn}, {qs: hold}
 
-    def arrives(sem, n, keys):
-        note((sem, n, {sem: n}, "r"), [], keys)
+        def emit(q):
+            deps(q, reads, writes)
+            s = sem or semof[q]
+            fn[q]().then_inc(T.sem[s], n)
+            count[s] = count.get(s, 0) + n
+            ck = dict(clock[q])
+            ck[s] = count[s]
+            note((s, count[s], ck, q), reads, writes)
+        nodes.append((qs, emit, reads, writes, hold, min(hold.values()) if last is None else last))
 
-    def send(transfers, reads):
-        deps("g", reads, [])
-        g.remote_dma_fused([t[0] for t in transfers], local_sem=T.sem.ls)
-        count["ls"] = count.get("ls", 0) + sum(t[1] for t in transfers)
+    def arrives(sem, n, after, keys, last):
+        nodes.append(("r", lambda q: note((sem, n, {sem: n}, "r"), [], keys), after, keys, {"r": 0.0}, last))
+
+    def send(transfers, reads, mark):
+        def emit(q):
+            deps("g", reads, [])
+            g.remote_dma_fused([t[0] for t in transfers], local_sem=T.sem.ls)
+            count["ls"] = count.get("ls", 0) + sum(t[1] for t in transfers)
+        nodes.append(("g", emit, reads, [mark], {"g": ISSUE}, 0.01))
 
     def xfer(src, dsts, es, sem):
         ids = [DstId(rid=topo.addr(c)[0], pnc=topo.addr(c)[1]) for c, _ in dsts]
@@ -160,480 +256,357 @@ def rank_program(g, core, T, topo):
                                   srcs=[src], dsts=[v for _, v in dsts]), len(es))
 
     V, S, P = g.vector, g.scalar, g.tensor
+    ID, W0, W1, W2 = ACT.Identity, 0.064, 0.128, 0.256
 
-    def ts(out, in0, s1, s2, o0, o1, r, w):
+    def gat(n):
+        return 0.05 + n * 1.3e-3
+
+    def ts(out, in0, s1, s2, o0, o1, r, w, c=W0):
         if o1 is None:
-            op("v", lambda: V.tensor_scalar(out, in0, s1, None, o0), r, w)
+            op("v", lambda: V.tensor_scalar(out, in0, s1, None, o0), r, w, c)
         else:
-            op("v", lambda: V.tensor_scalar(out, in0, s1, s2, o0, o1), r, w)
+            op("v", lambda: V.tensor_scalar(out, in0, s1, s2, o0, o1), r, w, c)
 
-    def tt(out, a, b, o, r, w):
-        op("v", lambda: V.tensor_tensor(out, a, b, o), r, w)
+    def tt(out, a, b, o, r, w, c=W0):
+        op("v", lambda: V.tensor_tensor(out, a, b, o), r, w, c)
 
-    def cp(out, a, r, w):
-        op("v", lambda: V.tensor_copy(out, a), r, w)
+    def cp(out, a, r, w, c=W0):
+        op("v", lambda: V.tensor_copy(out, a), r, w, c)
 
     def red(out, a, o, r, w):
-        op("v", lambda: V.tensor_reduce(out, a, X, o), r, w)
+        op("v", lambda: V.tensor_reduce(out, a, X, o), r, w, W0)
 
-    def tr(out, a, r, w):
-        op("v", lambda: V.transpose(out, a), r, w)
+    def tr(out, a, r, w, c=W0):
+        op("v", lambda: V.transpose(out, a), r, w, c)
 
-    def ms(out, c, w):
-        op("v", lambda: V.memset(out, c), [], w)
+    def ms(out, v, w, c=W0):
+        op("v", lambda: V.memset(out, v), [], w, c)
 
-    def scan(out, a, b, init, o0, o1, r, w):
-        op("v", lambda: V.tensor_tensor_scan(out, a, b, init, o0, o1), r, w)
+    def scan(out, a, b, init, o0, o1, r, w, c=W0):
+        op("v", lambda: V.tensor_tensor_scan(out, a, b, init, o0, o1), r, w, c)
 
-    def av(out, a, func, scale, bias, r, w):
-        op("a", lambda: S.activation(out, a, func, bias=bias, scale=scale), r, w)
+    def av(out, a, func, scale, bias, r, w, c=W0, acc=None):
+        op("a", lambda: S.activation(out, a, func, bias=bias, scale=scale, accum_out=acc), r, w, c)
+
+    def af(out, a, scale, bias, r, w, c=W0):
+        op("va", {"v": lambda: V.tensor_scalar(out, a, scale, bias, MUL, ADD),
+                  "a": lambda: S.activation(out, a, ID, bias=bias, scale=scale)}, r, w, {"v": c, "a": c + SX})
 
     def quant(name, a, b, src, r, w):
-        op("v", lambda: V.quantize_mx(T[name + "c"][:, a:b], T[name + "s"][:, a:b], src), r, w)
+        op("v", lambda: V.quantize_mx(T[name + "c"][:, a:b], T[name + "s"][:, a:b], src), r, w, 0.015 + (b - a) * 1.05e-3)
 
-    def pickc(dn, a, b, sn, c, d, off, r, w):
-        cp(T[dn + "c"][:, a:b].bitcast(dt.uint32), T[sn + "c"][:, c:d].bitcast(dt.uint32).indirect(off), r, w)
-
-    def picks(dn, a, b, sn, c, d, off, r, w):
-        op("a", lambda: S.activation(T[dn + "s"][:, a:b], T[sn + "s"][:, c:d].indirect(off), ACT.Copy), r, w)
+    def pick(dn, a, b, sn, c, d, off, rc, rs, wc, ws):
+        cp(T[dn + "c"][:, a:b].bitcast(dt.uint32), T[sn + "c"][:, c:d].bitcast(dt.uint32).indirect(off), rc, wc, gat(b - a))
+        op("a", lambda: S.activation(T[dn + "s"][:, a:b], T[sn + "s"][:, c:d].indirect(off), ACT.Copy), rs, ws,
+           gat(b - a) + 0.015)
 
     def mm(bank, ln, la, rn, ra, n, start, stop, r):
         op("p", lambda: P.matmul_mx(T[bank][:, 0:n], T[ln + "c"][:, la:la + 128], T[ln + "s"][:, la:la + 128],
                                     T[rn + "c"][:, ra:ra + n], T[rn + "s"][:, ra:ra + n], start, stop),
-           r, ["P" + bank])
+           r, ["P" + bank], (n + 16) * 6e-4)
 
-    def store(q, out, src, r):
-        op(q, lambda: queues[q].dma_start(out, src), r, [], "st", 16)
+    def dma(q, out, src, r, w, sem, last=LOAD):
+        op(q, lambda: queues[q].dma_start(out, src), r, w, 0.05, sem, 16, last)
 
     def bytes_of(name, a, b):
         return T[name + "c"][:, a:b].bitcast(dt.uint8)
 
+    def iota(out, pat, base, cm, w, n, small=True):
+        if small:
+            op("g", lambda: g.iota(out, pat, base, cm, allow_small_or_imprecise_dtypes=True), [], w, 0.16 + 2e-3 * n)
+        else:
+            op("g", lambda: g.iota(out, pat, base, cm), [], w, 0.16 + 2e-3 * n)
+
     cols = {}
 
-    def c_(name, w=1, rows=slice(0, 128)):
+    def c_(name, w=1, rows=slice(0, 128), j=None):
         if name not in cols:
-            at = sum(v[1] for v in cols.values())
-            cols[name] = (at, w)
+            cols[name] = (sum(v[1] for v in cols.values()), w)
         at, w = cols[name]
-        return T.sm[rows, at:at + w]
-
-    GL, EL, AL, RL = T.cu[:, 0:2], T.cu[:, 2:4], T.cu[:, 4:5], T.cu[:, 6:7]
-
-    def turn(n, r):
-        return [lambda: tr(T[n + "1"][:], T[n + "0"][:], r, [n + "1"]),
-                lambda: cp(T[n + "2"][:], T[n + "1"][:].indirect(GL), [n + "1", "GL"], [n + "2"]),
-                lambda: tr(T[n + "3"][:], T[n + "2"][:], [n + "2"], [n + "3"])]
-
-    def choose(out, src, r, w):
-        scan(out, T.msel[:], src, 0.0, MUL, MAX, ["msel"] + r, w)
+        return T.sm[rows, at:at + w] if j is None else T.sm[rows, at + j:at + j + 1]
 
     def quad(a):
         return slice(32 * a, 32 * a + 32)
 
-    def spread(dst, src, r, w):
-        return [lambda a=a: cp(dst(quad(a)), src, r, [w + str(a)]) for a in range(4)]
-
     def four(w):
         return [w + str(a) for a in range(4)]
 
-    def weave(*chains):
-        chains = [list(c) for c in chains]
-        while any(chains):
-            for c in chains:
-                if c:
-                    c.pop(0)()
+    EL, AL = T.cu[:, 2:4], T.cu[:, 4:5]
 
-    op("s", lambda: g.sync.dma_start(T.xs0[:], T.x[:]), [], four("x0."), "lx", 16)
-    op("s", lambda: g.sync.dma_start(T.bt[:], T.b[:]), [], ["bt"], "lb", 16)
-    op("a", lambda: S.dma_start(T.dtile[:], T.d[:]), [], ["dtile"], "ld", 16)
-    g.sync.dma_start(T.acti[ka:ka + 16, :], T.act[:]).then_inc(T.sem.la, 16)
-    g.sync.dma_start(T.acti[ka + 16:kb, :], T.act[:]).then_inc(T.sem.la, 16)
-    arrives("la", 32, ["acti"])
-    op("s", lambda: g.sync.dma_start(T.wt[:], T.w[:]), ["dtile"], ["wt"], "lw", 16)
+    dma("s", T.xs[:], T.x[:], [], ["xs"], "lx", 1.7)
+    dma("a", T.bt[:], T.b[:], [], ["bt", "#b"], "lb", 1.7)
+    PW = A // NP
+    for j in range(NP):
+        dma("a", T.dtile[:, 4 * PW * j:4 * PW * j + 4 * PW], T.d[:, 4 * PW * j:4 * PW * j + 4 * PW], ["#b"], ["dt%d" % j],
+            "ld%d" % j, 1.7 + 1.2 * (j + 1) / NP)
+    dma("s", T.acti[ka:ka + 16, :], T.act[:], [], ["actia"], "la", 3.3)
+    dma("s", T.acti[ka + 16:kb, :], T.act[:], [], ["actib"], "la", 3.3)
+    arrives("la", 32, ["actia", "actib"], ["acti"], 0.0)
+    dma("s", T.wt[:], T.w[:], ["dt%d" % (NP - 1)], ["wt"], "lw", 2.5)
 
-    def iota(out, pat, base, cm, w, small=True):
-        if small:
-            op("g", lambda: g.iota(out, pat, base, cm, allow_small_or_imprecise_dtypes=True), [], w)
-        else:
-            op("g", lambda: g.iota(out, pat, base, cm), [], w)
-
-    iota(T.si[:, 0:1], [[1, 1]], 0, 1, ["pi"], False)
-    iota(T.v516[:], [[1, 129], [1000, 4]], -3000, -1, ["v516"])
-    iota(T.j2[:], [[0, 4], [1, 32]], ka, -1, ["j2"])
-
-    J0 = T.j2[:, 0:1]
-    av(T.av[:], T.v516[:], ACT.Abs, 1.0, 0.0, ["v516"], ["av"])
-    av(T.ua[:, 0:514], T.av[:, 1:515], ACT.Relu, -1.0, 0.25, ["av"], ["ua"])
-    av(T.ub[:, 0:514], T.av[:, 0:514], ACT.Relu, -1.0, 0.25, ["av"], ["ub"])
-    av(T.aj[:], T.j2[:], ACT.Abs, 1.0, 0.0, ["j2"], ["aj"])
-    av(T.na[:, 0:514], T.ua[:, 0:514], ACT.Identity, -1.0, 0.0, ["ua"], ["na"])
-    av(T.nb[:, 0:514], T.ub[:, 0:514], ACT.Identity, -1.0, 0.0, ["ub"], ["nb"])
-    av(T.d4[:], T.aj[:], ACT.Relu, -1.0, 1.0, ["aj"], ["d4"])
-    av(T.kp4[:], T.aj[:], ACT.Sign, 1.0, 0.0, ["aj"], ["kp4"])
-    av(c_("ni128"), J0, ACT.Identity, 1.0 / PU, -128.0 / PU, ["j2"], ["ni128"])
+    iota(T.si[:, 0:1], [[1, 1]], 0, 1, ["pi"], 1, False)
+    iota(T.jd[:], [[1, 128]], 0, -1, ["jd"], 128)
+    iota(T.j2[:], [[0, 4], [1, 32]], ka, -1, ["j2"], 128)
+    iota(T.ci[:], [[1, 128]], 0, 0, ["ci"], 128, False)
+    iota(T.k8[:], [[-A, N]], A * (N - 1), 0, ["k8"], 8)
+    iota(T.p8[:], [[-32, G], [0, 2]], 32 * (G - 1), 0, ["p8"], 8)
+    ms(T.et[:], 0.0, ["et"], W2)
+    ms(T.ua[:], 0.0, ["ua"], W2)
+    ms(T.ub[:], 0.0, ["ub"], W2)
+    ms(T.zb[:], 0.0, ["zb"], 0.19)
+    ms(T.nn0[:], 0.0, ["nn0"])
+    ms(T.nbw[:, 8:40], 1.0, ["nbc"])
+    ms(T.khw[:, 8:40], 0.0, ["khc"])
+    ms(T.qq[:, 34:66], 0.0, ["qqz"])
+    ms(T.cpw[:, 0:34], -BIG, ["cpc"])
+    ms(T.c32[:], -32.0 / PU, ["c32"], W1)
+    for s in range(4):
+        ms(T.sbk[:, 32 * s:32 * s + 32], float(s), ["sbk%d" % s])
+    av(T.ad[:], T.jd[:], ACT.Abs, 1.0, 0.0, ["jd"], ["ad"], W1)
+    av(T.ua[:, 2:514:4], T.ad[:], ACT.Relu, -1.0, 0.25, ["ad"], ["ua"], W1)
+    av(T.ub[:, 3:515:4], T.ad[:], ACT.Relu, -1.0, 0.25, ["ad"], ["ub"], W1)
+    av(T.na[:], T.ua[:], ID, -1.0, 0.0, ["ua"], ["na"], 0.52)
+    av(T.nb[:], T.ub[:], ID, -1.0, 0.0, ["ub"], ["nb"], 0.52)
+    av(T.aj[:], T.j2[:], ACT.Abs, 1.0, 0.0, ["j2"], ["aj"], W1)
+    av(T.d4[:], T.aj[:], ACT.Relu, -1.0, 1.0, ["aj"], ["d4"], W1)
+    av(T.kp4[:], T.aj[:], ACT.Sign, 1.0, 0.0, ["aj"], ["kp4"], W1)
     av(T.tm[:], T.j2[:, 0:32], ACT.Relu, BIG, BIG, ["j2"], ["tm"])
-
-    ms(T.et[:], 0.0, four("et."))
-    ms(T.zer[:], 0.0, ["zer"])
-    for n in ("sb0", "nn0"):
-        ms(T[n][:], 0.0, [n, n + "a"])
-    ms(T.sc16[:, 8:16], 0.0, ["sc16b"])
+    for neg in range(2):
+        for b in range(4):
+            src = (("ua", "ub"), ("na", "nb"))[neg][b % 2]
+            st, at = 2 if b < 2 else 0, 512 * neg + 128 * b
+            quant("ee", at, at + 128, T[src][:, st:st + 512], [src], ["ee%d" % (4 * neg + b)])
     PI = T.si[:, 0:1]
     ts(T.si[:, 1:2], PI, 31, None, AND, None, ["pi"], ["p31"])
     ts(T.si[:, 2:3], PI, 15, None, AND, None, ["pi"], ["p15"])
     ts(T.si[:, 3:4], PI, 3, None, AND, None, ["pi"], ["p3"])
     ts(T.si[:, 4:5], PI, 4, 1, SHR, AND, ["pi"], ["pg"])
-    ts(T.si[:, 5:6], PI, 1, 3, SHR, AND, ["pi"], ["ph"])
-    ts(T.si[:, 6:7], PI, 1, None, AND, None, ["pi"], ["p1"])
-    ts(T.si[:, 7:8], PI, 3, 1, SHR, AND, ["pi"], ["p8"])
-    cp(T.cu[:, 0:1], T.si[:, 1:2], ["p31"], ["GLa"])
-    cp(T.cu[:, 2:3], T.si[:, 2:3], ["p15"], ["ELa"])
-    cp(c_("pg"), T.si[:, 4:5], ["pg"], ["pgf"])
-    cp(c_("p8"), T.si[:, 7:8], ["p8"], ["p8f"])
-    ts(c_("off"), T.si[:, 2:3], -1.0, 15.0, MUL, ADD, ["p15"], ["off"])
-    tt(T.et[:, 128 * k:128 * k + 128], T.bt[:], T.xs0[:], SUB, ["bt"] + four("x0."), four("et."))
-    quant("qe0", 0, 128, T.et[:], four("et."), ["qe0"])
-    OFF = c_("off")
-    av(c_("i128"), c_("ni128"), ACT.Identity, -1.0, OFF, ["ni128", "off"], ["i128"])
-    av(T.qq[:, 32:33], OFF, ACT.Identity, 1.0, -(CAPP - 0.5), ["off"], ["qqc"])
-    av(c_("off2"), OFF, ACT.Identity, ZU, 0.0, ["off"], ["off2"])
-    av(c_("off3"), OFF, ACT.Identity, ZU, float(HI - own0), ["off"], ["off3"])
-    av(c_("ic"), J0, ACT.Identity, -1.0, c_("off2"), ["j2", "off2"], ["ic"])
+    ts(T.si[:, 5:6], PI, 2, 3, SHR, AND, ["pi"], ["pq"])
+    cp(c_("pf", 5), T.si[:, 1:6], ["p31", "p15", "p3", "pg", "pq"], ["pf"])
+    P31, P15, P3, PG, PQ = [c_("pf", j=j) for j in range(5)]
+    P15Q = c_("pf", rows=Q0, j=1)
+    cp(T.cu[:, 2:3], P15, ["pf"], ["ELa"])
+    ts(T.cu[:, 3:4], P15, 16.0, None, ADD, None, ["pf", "ELa"], ["EL"])
+    ts(AL, P3, 2.0, PG, MUL, ADD, ["pf"], ["AL"])
+    av(c_("off2"), P15, ID, -ZU, 15 * ZU, ["pf"], ["off2"])
+    av(c_("off3"), P15, ID, -ZU, 15 * ZU + HI - own0, ["pf"], ["off3"])
+    av(c_("ic"), P31, ID, 1.0 / PU, P15, ["pf"], ["ic"])
+    av(c_("ip"), P31, ID, 1.0 / PU, P3, ["pf"], ["ip"])
+    av(c_("d153"), P3, ID, -1.0, P15, ["pf"], ["d153"])
+    av(c_("thr"), P15, ID, 1.0, 0.25, ["pf"], ["thr"])
+    av(c_("c4"), P3, ID, -0.25 / PU, PQ, ["pf"], ["c4c"])
+    av(T.qq[:, 32:33], P3, ID, 1.0, -(CAPP - 0.5), ["pf"], ["qqc"])
+    av(c_("plw", 8), T.p8[:], ID, 1.0 / PU, c_("ip"), ["p8", "ip"], ["plw"])
+    ts(T.cj[:], T.ci[:], 15, None, AND, None, ["ci"], ["cj"], W1)
+    ts(T.c4[:], T.ci[:, 0:32], 3, None, AND, None, ["ci"], ["c4"])
+    ts(T.cw[:], T.ci[:], 128.0, 1.0 / PU, ADD, MUL, ["ci"], ["cw"], W1)
+    ts(T.msel[:], T.cj[:, 0:64], P15, None, NE, None, ["cj", "pf"], ["msel"])
+    ts(T.cu1[:], T.cj[:], P15, -BIG, NE, MUL, ["cj", "pf"], ["cu1"], W1)
+    ts(T.u4[:, 0:32], T.c4[:], PQ, -BIG, NE, MUL, ["c4", "pf"], ["u4a"])
+    av(T.u4[:, 32:64], T.cw[:, 0:32], ID, 1.0, PQ, ["cw", "pf"], ["u4b"])
+    tt(T.cap4[:], T.u4[:, 0:32], T.u4[:, 32:64], ADD, ["u4a", "u4b"], ["cap4"])
+    av(T.n1[:], T.cw[:], ID, 1.0, P15, ["cw", "pf"], ["n1"], W1)
+    tt(T.caps[:], T.cu1[:], T.n1[:], ADD, ["cu1", "n1"], ["caps"], W2)
 
     def send_e(t):
         es = topo.engines(core, peers[0])
-        n = "qe%d" % t
-        h = len(es) // 2
+        n, h = "qe%d" % t, len(es) // 2
         e1, e2 = (es[:h], es[h:]) if t == 0 else (es, es)
-        send([xfer(bytes_of(n, ka, kb), [(c, bytes_of("eg%d" % t, ka, kb)) for c in peers], e1, "ae%d" % t)], [n])
-        send([xfer(T[n + "s"][:, ka:kb], [(c, T["eg%ds" % t][:, ka:kb]) for c in peers], e2, "ae%d" % t)], [n])
-        arrives("ae%d" % t, (len(e1) + len(e2)) * len(peers), ["eg%d.r" % t])
+        send([xfer(bytes_of(n, ka, kb), [(c, bytes_of("eg%d" % t, ka, kb)) for c in peers], e1, "ae%d" % t)], [n],
+             "#ec%d" % t)
+        send([xfer(T[n + "s"][:, ka:kb], [(c, T["eg%ds" % t][:, ka:kb]) for c in peers], e2, "ae%d" % t)],
+             [n, "#ec%d" % t], "#es%d" % t)
+        arrives("ae%d" % t, (len(e1) + len(e2)) * len(peers), ["#es%d" % t], ["eg%d.r" % t], HOP + (1.5 if t == 0 else 0))
+        pick("eg%d" % t, ka, kb, n, ka, kb, EL, ["EL", n], ["EL", n], ["eg%d.c" % t], ["eg%d.s" % t])
 
+    def copies(t):
+        xw, key = T["xw%d" % t], "xr%d" % t
+        av(xw[:, 640:768], xw[:, 512:640], ID, 1.0, 0.0, [key + "a"], [key + "b"], W1)
+        av(xw[:, 768:1024], xw[:, 512:768], ID, 1.0, 0.0, [key + "a", key + "b"], [key + "c"], W2)
+
+    ET = T.et[:, 128 * k:128 * k + 128]
+    tt(ET, T.bt[:], T.xs[:], SUB, ["bt", "xs"], ["et"], W2)
+    quant("qe0", 0, 128, T.et[:], ["et"], ["qe0"])
     send_e(0)
-    iota(T.i8[:], [[0, 2], [1, 4]], 0, 0, ["i8"])
-    iota(T.v8[:], [[-(16 * QS + 1), G], [-8 * QS, 2]], 8 * QS * (N - 1) + G - 1, 0, ["v8"])
-    cp(T.cu[:, 1:2], T.si[:, 1:2], ["p31", "GLa"], ["GL"])
-    ts(T.cu[:, 3:4], T.si[:, 2:3], 16.0, None, ADD, None, ["p15", "ELa"], ["EL"])
-    ts(AL, T.si[:, 3:4], 2.0, c_("pg"), MUL, ADD, ["p3", "pgf"], ["AL"])
-    ts(c_("rl"), T.si[:, 5:6], 4.0, c_("p8"), MUL, ADD, ["ph", "p8f"], ["rl"])
-    ts(c_("k0"), T.si[:, 1:2], 1.0 / 256, None, MUL, None, ["p31"], ["k0"])
-    ts(c_("soc"), T.si[:, 2:3], 1.0 + 1.0 / PU, -15.0, MUL, ADD, ["p15"], ["soc"])
-    quant("at", own0, own0 + A, T.dtile[:], ["dtile"], ["at.o"])
+    av(T.xw0[:, 512:640], T.xs[:], ID, -1.0, 0.0, ["xs"], ["xr0a"], W1)
+    copies(0)
     es = topo.engines(core, mate)
-    send([xfer(bytes_of("at", own0, own0 + A), [(mate, bytes_of("at", own0, own0 + A))], es, "aa")], ["at.o"])
-    send([xfer(T.ats[:, own0:own0 + A], [(mate, T.ats[:, own0:own0 + A])], es, "aa")], ["at.o"])
-    arrives("aa", 2 * len(topo.engines(mate, core)), ["at.r"])
-    iota(T.sc8[:], [[32, 4], [16, 2]], 128, 0, ["sc8"])
-    iota(T.j16[:], [[0, 2], [-1, 16]], 15, 0, ["j16"])
+    mark = "#es0"
+    for j in range(NP):
+        a, b = own0 + PW * j, own0 + PW * j + PW
+        quant("at", a, b, T.dtile[:, 4 * PW * j:4 * PW * j + 4 * PW], ["dt%d" % j], ["at.%d" % j])
+        send([xfer(bytes_of("at", a, b), [(mate, bytes_of("at", a, b))], es, "aa")], ["at.%d" % j, mark], "#ac%d" % j)
+        send([xfer(T.ats[:, a:b], [(mate, T.ats[:, a:b])], es, "aa")], ["at.%d" % j, "#ac%d" % j], "#as%d" % j)
+        mark = "#as%d" % j
+    arrives("aa", 2 * NP * len(topo.engines(mate, core)), [mark], ["at.r"], HOP + 0.9 / NP)
+    ato = ["at.%d" % j for j in range(NP)]
 
-    def own_e(t):
-        pickc("eg%d" % t, ka, kb, "qe%d" % t, ka, kb, EL, ["EL", "qe%d" % t], ["eg%d.c" % t])
-        picks("eg%d" % t, ka, kb, "qe%d" % t, ka, kb, EL, ["EL", "qe%d" % t], ["eg%d.s" % t])
+    for a in range(4):
+        cp(T.af[quad(a), :], T.acti[Q0, :], ["acti"], ["af%d" % a])
+    cp(T.aoff[:], T.af[:], four("af"), ["aoff"])
+    ts(T.ae0[:], T.af[:].indirect(AL), float(A * rank), None, ADD, None, four("af") + ["AL"], ["ae0"], gat(16))
+    pick("win0", 128, 256, "at", own0, own0 + A, T.aoff[:], ["aoff"] + ato, ["aoff"] + ato, ["win0.sc"], ["win0.ss"])
+    quant("wq", 0, 256, T.wt[:], ["wt"], ["wq"])
 
-    def act_e(t):
-        return (T.ae0[:, 0:4], "ae0") if t == 0 else (c_("ae%d" % t, 4), "ae%d" % t)
-
-    def a_mm(t):
-        mm("pa", "qe%d" % t, 0, "win%d" % t, 128, 128, True, True, ["qe%d" % t, "win%d.sc" % t, "win%d.ss" % t])
+    def y_mm(w, a, keys):
+        for o, bank in enumerate(("py", "pa")):
+            mm(bank, "wq", 128 * o, w, a, 128, True, True, ["wq"] + keys)
 
     AS = T.asc[:, 31:128:32]
-    K8 = c_("k8", 8)
-
-    def a_scores():
-        return [
-            lambda: tt(T.am[:], T.pa[:, 0:128], T.d4[:], MUL, ["Ppa", "d4"], ["am"]),
-            lambda: scan(T.asc[:], T.kp4[:], T.am[:], 0.0, MUL, ADD, ["kp4", "am"], ["asc"])]
-
-    def a_chain():
-        return [
-            lambda: red(c_("amin"), AS, MIN, ["asc"], ["amin"]),
-            lambda: ts(c_("ta", 4), AS, c_("amin"), 8.0, GT, MUL, ["asc", "amin"], ["ta"]),
-            lambda: tt(c_("ua", 4), c_("ta", 4), T.i8[:, 0:4], ADD, ["ta", "i8"], ["ua4"]),
-            lambda: red(c_("aslot"), c_("ua", 4), MIN, ["ua4"], ["aslot"]),
-            lambda: ts(c_("nm", 8), T.i8[:], c_("aslot"), BIG, NE, MUL, ["i8", "aslot"], ["nm"]),
-            lambda: av(c_("apr"), c_("aslot"), ACT.Identity, 32.0, c_("ic"), ["aslot", "ic"], ["apr"]),
-            lambda: av(c_("apos"), c_("aslot"), ACT.Identity, 32.0 / PU, c_("i128"), ["aslot", "i128"], ["apos"]),
-            lambda: av(T.ab0[:], T.zer[:], ACT.Identity, 1.0, c_("apr"), ["zer", "apr"], ["ab0"]),
-            lambda: av(c_("napos"), c_("aslot"), ACT.Identity, -32.0 / PU, c_("ni128"), ["aslot", "ni128"], ["napos"]),
-            lambda: av(c_("nma", 8), c_("nm", 8), ACT.Identity, 1.0, c_("napos"), ["nm", "napos"], ["nma"])]
-
-    def best_active(t):
-        ae, key = act_e(t)
-        return [
-            lambda: red(c_("amax"), AS, MAX, ["asc"], ["amax"]),
-            lambda: ts(c_("tb", 4), AS, c_("amax"), BIG, LT, MUL, ["asc", "amax"], ["tb"]),
-            lambda: tt(c_("ub", 4), c_("tb", 4), ae, ADD, ["tb", key], ["ub4"]),
-            lambda: red(c_("amaxe"), c_("ub", 4), MIN, ["ub4"], ["amaxe"]),
-            lambda: av(c_("ak8", 8), K8, ACT.Identity, -1.0, c_("amaxe"), ["k8", "amaxe"], ["ak8"])]
-
-    def y_mm(t):
-        w = "win%d" % (t + 1)
-        for o, bank in enumerate(("py", "pa")):
-            mm(bank, "wq", 128 * o, w, 128, 128, True, True, ["wq", w + ".sc", w + ".ss"])
-
-    def y_out(t, q):
-        ys = T["ys%d" % t]
-        for o, bank in enumerate(("py", "pa")):
-            op("a", lambda: S.activation(ys[:, 128 * o:128 * o + 128], T[bank][:, 0:128], ACT.Copy),
-               ["P" + bank], ["ys%d.%d" % (t, o)])
-        store(q, T.y[:, 256 * t:256 * t + 256], ys[:], ["ys%d.0" % t, "ys%d.1" % t])
-
-    def window(t):
-        w = "win%d" % t
-        return [w + ".sc", w + ".oc", w + ".rc"], [w + ".ss", w + ".os", w + ".rs"]
-
-    def slot_pick(t):
-        w, w2 = "win%d" % t, "win%d" % (t + 1)
-        rc, rs = window(t)
-        pickc(w2, 128, 256, w, 0, 256, T.so[:, 0:8], four("so") + rc, [w2 + ".sc"])
-        picks(w2, 128, 256, w, 0, 256, T.so[:, 0:8], four("so") + rs, [w2 + ".ss"])
-
-    def renew(old, okey, diff, dkey, new, nkey):
-        return [lambda: ts(c_("m2", 4), T.sb0[:, 0:16:4], OFF, None, LT, None, ["sb0a", "off"], ["m2"]),
-                lambda: tt(c_("dd", 4), c_("m2", 4), diff, MUL, ["m2", dkey], ["dd"]),
-                lambda: tt(new, old, c_("dd", 4), ADD, [okey, "dd"], [nkey])]
-
-    def unit(b, neg):
-        src = (("ua", "ub"), ("na", "nb"))[neg][b % 2]
-        st = 2 if b < 2 else 0
-        at = 512 * neg + 128 * b
-        return lambda: quant("ee", at, at + 128, T[src][:, st:st + 512], [src], ["ee%d" % (4 * neg + b)])
-
-    weave(spread(lambda q: T.af[q, :], T.acti[Q0, :], ["acti"], "af"))
-    ts(RL, T.si[:, 6:7], 16.0, c_("rl"), MUL, ADD, ["p1", "rl"], ["RL"])
-    cp(T.aoff[:], T.af[:], four("af"), ["aoff"])
-    ts(T.ae0[:], T.af[:].indirect(AL), c_("k0"), float(QS * rank) + ka / 256.0, ADD, ADD,
-       four("af") + ["AL", "k0"], ["ae0"])
-    pickc("win0", 128, 256, "at", own0, own0 + A, T.aoff[:], ["aoff", "at.o"], ["win0.sc"])
-    picks("win0", 128, 256, "at", own0, own0 + A, T.aoff[:], ["aoff", "at.o"], ["win0.ss"])
-    own_e(0)
-    a_mm(0)
-    ts(K8, T.v8[:], 0.125, c_("k0"), MUL, ADD, ["v8", "k0"], ["k8"])
-    ms(T.neg[:], -1.0e29, ["neg"])
-    ts(c_("key8", 8), K8, RQ, RQ, ADD, SUB, ["k8"], ["key8"])
-    ms(T.nbw[:, 8:40], 1.0, ["nbc"])
-    ms(T.khw[:, 8:40], 0.0, ["khc"])
-    tt(c_("pl8", 8), K8, c_("key8", 8), SUB, ["k8", "key8"], ["pl8"])
-    ms(T.plw[:, 8:40], 0.0, ["plc"])
-    weave([unit(b, 0) for b in range(4)])
-    av(T.plw[:, 0:8], c_("pl8", 8), ACT.Identity, 256.0 / PU, OFF, ["pl8", "off"], ["plw"])
-    weave(a_scores() + a_chain(), [unit(b, 1) for b in range(4)])
-    ts(T.sc16[:, 0:8], T.sc8[:], 1.0 / PU, c_("soc"), MUL, ADD, ["sc8", "soc"], ["sc16a"])
-    ts(T.msel[:], T.j16[:], OFF, None, NE, None, ["j16", "off"], ["msel"])
-    quant("fa", 32, 160, T.dtile[:, 0:512], ["dtile"], ["fa.ac", "fa.as", "fa.z"])
-
     for t in range(R):
         last = t == R - 1
-        ml, mk, eg, w, pk = T["ml%d" % t], "ml%d" % t, "eg%d" % t, "win%d" % t, "pk%d" % t
-        egk = [eg + ".c", eg + ".s", eg + ".r"]
+        ml, mk, eg, w, pk, fa, xw = (T["ml%d" % t], "ml%d" % t, "eg%d" % t, "win%d" % t, "pk%d" % t, "fa%d" % t,
+                                     T["xw%d" % t])
+        ae, aek = (T.ae0[:, 0:4], "ae0") if t == 0 else (c_("ae%d" % t, 4), "ae%d" % t)
+        mm("pa", "qe%d" % t, 0, w, 128, 128, True, True, ["qe%d" % t, w + ".sc", w + ".ss"])
+        tt(T.am[:], T.pa[:, 0:128], T.d4[:], MUL, ["Ppa", "d4"], ["am"], W1)
+        scan(T.asc[:], T.kp4[:], T.am[:], 0.0, MUL, ADD, ["kp4", "am"], ["asc"], W1)
+        scan(c_("rm", 4), AS, T.zb[:, 0:4], 1.0e29, MIN, ADD, ["asc", "zb"], ["rm"])
+        NS = c_("nslot")
+        av(c_("sj", 4), c_("rm", 4), ACT.Sign, -1.0, c_("rm", j=3), ["rm"], ["nslot"], 0.084, NS)
+        av(T.ab0[:], T.c32[:], ID, NS, c_("ic"), ["c32", "nslot", "ic"], ["ab0"], W1)
+        av(T.n1[:], T.sbk[:], ACT.Abs, 1.0, NS, four("sbk") + ["nslot"], ["n1"], W1)
+        av(T.nmb[:], T.n1[:], ID, BIG, c_("d153"), ["n1", "d153"], ["nmb"], W1)
+        tr(T.ab1[:], T.ab0[:], ["ab0"], ["ab1"], W1)
+        scan(T.ab2[:], T.caps[:], T.ab1[:], 0.0, MAX, MIN, ["caps", "ab1"], ["ab2"], W1)
+        for a in range(4):
+            ts(T.ao[quad(a), :], T.ab2[Q0, 15:128:16], P15Q, PU, SUB, MUL, ["ab2", "pf"], ["ao%d" % a])
+        pick(fa, 0, 128, w, 128, 256, T.ao[:], four("ao") + [w + ".sc"], four("ao") + [w + ".ss"], [fa + "c"], [fa + "s"])
+        for b in range(4):
+            mm("pd%d" % b, "ee", 128 * b, fa, 0, 128, True, False, ["ee%d" % b, fa + "c", fa + "s"])
+        red(c_("amax"), AS, MAX, ["asc"], ["amax"])
+        ts(c_("tb", 4), AS, c_("amax"), BIG, LT, MUL, ["asc", "amax"], ["tb"])
+        tt(c_("ub", 4), c_("tb", 4), ae, ADD, ["tb", aek], ["ub4"])
+        red(c_("amaxe"), c_("ub", 4), MIN, ["ub4"], ["amaxe"])
+        av(c_("ak8", 8), T.k8[:], ID, -1.0, c_("amaxe"), ["k8", "amaxe"], ["ak8"])
+        if t > 0:
+            y_mm(w, 128, [w + ".sc", w + ".ss"])
+            for o, bank in enumerate(("py", "pa")):
+                if t == 1:
+                    av(T.ys0[:, 128 * o:128 * o + 128], T[bank][:, 0:128], ID, 1.0, 0.0, ["P" + bank], ["ys%d" % o], W1)
+                else:
+                    ys = T.yw[:, 256 * o + 128:256 * o + 256]
+                    av(ys, T[bank][:, 0:128], ID, 1.0, 0.0, ["P" + bank], ["yw%d" % o], W1)
+                    dma("s", T.y[:, 256 + 128 * o:384 + 128 * o], ys, ["yw%d" % o], [], "st")
+            if t == 1:
+                dma("s", T.y[:, 0:256], T.ys0[:], ["ys0", "ys1"], [], "st")
         halves = [("ps1", 0, "r1", A), ("ps2", HI, "r2", 0)]
         if own0:
             halves.reverse()
-        for (bank, a0, _, _), key in zip(halves, ("at.o", "at.r")):
-            mm(bank, eg, 0, "at", a0, A, True, True, egk + [key])
-        if t > 0:
-            y_mm(t - 1)
+        for (bank, a0, _, _), key in zip(halves, (ato, ["at.r"])):
+            mm(bank, eg, 0, "at", a0, A, True, True, [eg + ".c", eg + ".s", eg + ".r"] + key)
         M2, M1 = T.r21[:, A - 1:A], T.r21[:, 2 * A - 1:2 * A]
         m0 = 4 * (G - 1 - k)
         C2, C1 = ml[:, m0 + 1:m0 + 2], ml[:, m0 + 3:m0 + 4]
         for bank, _, rk, r0 in halves:
-            scan(T.r21[:, r0:r0 + A], T[bank][:, 0:A], T.neg[:], -1.0e29, MAX, MAX, ["P" + bank, "neg"], [rk])
+            scan(T.r21[:, r0:r0 + A], T[bank][:, 0:A], T.zb[:], -1.0e29, MAX, ADD, ["P" + bank, "zb"], [rk], A * 1e-3)
         for _, _, rk, r0 in halves:
-            op("a", lambda: S.activation(T.junk[:, r0:r0 + A], T.r21[:, r0:r0 + A], ACT.Sign,
-                                         bias=T.r21[:, r0 + A - 1:r0 + A], scale=-1.0, accum_out=C1 if r0 else C2),
-               [rk], [mk + "." + rk, "junk" + rk])
+            av(T.junk[:, r0:r0 + A], T.r21[:, r0:r0 + A], ACT.Sign, -1.0, T.r21[:, r0 + A - 1:r0 + A], [rk],
+               [mk + "." + rk, "junk" + rk], A * 1e-3 + 0.02, C1 if r0 else C2)
         c1k, c2k = mk + ".r1", mk + ".r2"
-        ba = best_active(t)
-        ba[0]()
         cp(ml[:, m0:m0 + 4:2], T.r21[:, A - 1:2 * A:A], ["r1", "r2"], [mk + ".m"])
         mine = [mk + ".m", c1k, c2k]
         mv = ml[:, m0:m0 + 4]
-        send([xfer(mv, [(c, mv) for c in peers], topo.engines(core, peers[0]), "am%d" % t)], mine)
-        arrives("am%d" % t, sum(len(topo.engines(c, core)) for c in peers), [mk + ".r"])
+        send([xfer(mv, [(c, mv) for c in peers], topo.engines(core, peers[0]), "am%d" % t)], mine, "#m%d" % t)
+        arrives("am%d" % t, sum(len(topo.engines(c, core)) for c in peers), ["#m%d" % t], [mk + ".r"], HOP - 0.2)
         CF, cfk, CL, clk = (C2, c2k, C1, c1k) if own0 else (C1, c1k, C2, c2k)
-        ts(T.gb[:], T.zer[:], M2, M1, ADD, LE if own0 else GT, ["zer", "r1", "r2"], ["gb"])
+        ts(T.gb[:], T.zb[:, 0:64], M2, M1, ADD, LE if own0 else GT, ["zb", "r1", "r2"], ["gb"])
         ts(c_("gh"), M2, M1, None, GT if own0 else LE, None, ["r1", "r2"], ["gh"])
         ts(c_("gu"), CF, float(HI if own0 else -HI), None, ADD, None, [cfk], ["gu"])
         ts(c_("rest"), c_("gu"), c_("gh"), c_("off3"), MUL, ADD, ["gh", "gu", "off3"], ["rest"])
         ts(T.z0[:], T.gb[:], CL, c_("rest"), MUL, ADD, ["gb", clk, "rest"], ["z0"])
-        ba[1]()
         tr(T.z1[:], T.z0[:], ["z0"], ["z1"])
-        ba[2]()
-        choose(T.zy[:, 0:32], T.z1[:], ["z1"], ["zya", "zc0", "zc2"])
-        choose(T.zy[:, 32:64], T.z1[:], ["z1"], ["zyb", "zc1", "zc3"])
-        ba[3]()
-        ba[4]()
+        scan(T.zy[:], T.msel[:], T.z1[:], 0.0, MUL, MAX, ["msel", "z1"], ["zy"] + four("zc"))
         for h in range(2):
             f, s = order[2 * h], order[2 * h + 1]
-            cp(T.zy[quad(s), 15:32:16], T.zy[quad(f), 15:32:16], ["zya"], ["zc%d" % (2 * h)])
-        for h in range(2):
-            f, s = order[2 * h], order[2 * h + 1]
-            cp(T.zy[quad(f), 47:64:16], T.zy[quad(s), 47:64:16], ["zyb"], ["zc%d" % (2 * h + 1)])
-        tr(T.ab1[:], T.ab0[:], ["ab0"], ["ab1"])
+            cp(T.zy[quad(s), 15:32:16], T.zy[quad(f), 15:32:16], ["zy"], ["zc%d" % (2 * h)])
+            cp(T.zy[quad(f), 47:64:16], T.zy[quad(s), 47:64:16], ["zy"], ["zc%d" % (2 * h + 1)])
         for h in range(2):
             src = slice(64 * (order[2 * h] // 2), 64 * (order[2 * h] // 2) + 64)
             for d in range(2):
                 ts(T.ho[64 * d:64 * d + 64, 4 * h:4 * h + 4], T.zy[src, 15:64:16], c_("off2", 1, src), None, SUB, None,
-                   ["zya", "zyb", "zc%d" % (2 * h), "zc%d" % (2 * h + 1), "off2"], ["ho%d" % (2 * h + d)])
-        choose(T.ab2[:], T.ab1[:], ["ab1"], ["ab2"])
-        apk = [lambda a=a: ts(T.ao[quad(a), :], T.ab2[Q0, 15:32:16], c_("off2", 1, Q0), None, SUB, None,
-                              ["ab2", "off2"], ["ao%d" % a]) for a in range(4)]
-        hk = four("ho") + ["at.o", "at.r"]
-        pickc(pk, 0, 96, "at", 0, AW, T.ho[:, 0:6], hk, [pk + ".c"])
-        picks(pk, 0, 96, "at", 0, AW, T.ho[:, 0:6], hk, [pk + ".s"])
+                   ["zy", "zc%d" % (2 * h), "zc%d" % (2 * h + 1), "off2"], ["ho%d" % (2 * h + d)])
+        hk = four("ho") + ato + ["at.r"]
+        pick(pk, 0, 96, "at", 0, AW, T.ho[:, 0:6], hk, hk, [pk + ".c"], [pk + ".s"])
         ec, esc = splits(topo.engines(core, peers[0]))
         send([xfer(bytes_of(pk, 32 * i, 32 * i + 32), [(grp[order[i]], bytes_of(w, ka, kb))], ec[i], "ac%d" % t)
-              for i in range(3)], [pk + ".c"])
-        send([xfer(T[pk + "s"][:, 32 * i:32 * i + 32], [(grp[order[i]], T[w + "s"][:, ka:kb])], esc[i], "as%d" % t)
-              for i in range(3)], [pk + ".s"])
-        for j, nm, key in ((0, "ac", ".rc"), (1, "as", ".rs")):
-            arrives("%s%d" % (nm, t), sum(len(splits(topo.engines(grp[s], core))[j][places(s).index(k)])
-                                          for s in range(G) if s != k), [w + key])
-        if t > 0:
-            y_out(t - 1, "s")
-        ae, aek = act_e(t)
-
-        def own_pick():
-            pickc(w, ka, kb, "at", 0, AW, T.ho[:, 6:8], hk, [w + ".oc"])
-            picks(w, ka, kb, "at", 0, AW, T.ho[:, 6:8], hk, [w + ".os"])
-
-        def a_side():
-            pickc("fa", 32, 64, w, 128, 256, T.ao[:], four("ao") + [w + ".sc"], ["fa.ac"])
-            picks("fa", 32, 64, w, 128, 256, T.ao[:], four("ao") + [w + ".ss"], ["fa.as"])
-            for b in range(4):
-                mm("pd%d" % b, "ee", 512 + 128 * b, "fa", 32, 128, True, False, ["ee%d" % (4 + b), "fa.ac", "fa.as", "fa.z"])
-
+              for i in range(3)], [pk + ".c", "#m%d" % t], "#c%d" % t)
+        send([xfer(T[pk + "s"][:, 32 * i:32 * i + 32], [(grp[order[i]], T[w + "s"][:, ka:kb])], esc[i], "ac%d" % t)
+              for i in range(3)], [pk + ".s", "#c%d" % t], "#s%d" % t)
+        arrives("ac%d" % t, sum(len(splits(topo.engines(grp[s], core))[j][places(s).index(k)])
+                                for s in range(G) if s != k for j in range(2)), ["#s%d" % t], [w + ".r"], HOP)
+        pick(w, ka, kb, "at", 0, AW, T.ho[:, 6:8], hk, hk, [w + ".oc"], [w + ".os"])
+        cand = [w + ".oc", w + ".os", w + ".r"]
+        for b in range(4):
+            mm("pd%d" % b, "ee", 512 + 128 * b, w, 0, 128, False, True, ["ee%d" % (4 + b)] + cand)
+        for b in range(4):
+            tt(xw[:, b:512:4], T["pd%d" % b][:, 0:128], xw[:, 512 + b:1024:4], ADD,
+               ["Ppd%d" % b] + ["xr%d%s" % (t, s) for s in "abc"], ["xc%d" % b], W1)
         allm = mine + [mk + ".r"]
         SC, CC = ml[:, 0:16:2], ml[:, 1:16:2]
-        EM = T.sm[:, 199:200]
         HN = T.qq[:, 33:34]
-        apk[0]()
-        apk[1]()
+        EMW, CPW = c_("emw", 8), c_("cpo", 8)
+        EM, CPO = c_("emw", j=7), c_("cpo", j=7)
         red(c_("best"), SC, MAX, allm, ["best"])
         tt(c_("h8", 8), CC, c_("ak8", 8), EQ, allm + ["ak8"], ["h8"])
-        tt(c_("e8", 8), CC, K8, ADD, allm + ["k8"], ["e8"])
+        tt(c_("e8", 8), CC, T.k8[:], ADD, allm + ["k8"], ["e8"])
         ts(T.nbw[:, 0:8], SC, c_("best"), None, LT, None, allm + ["best"], ["nbw"])
-        tt(T.khw[:, 0:8], c_("h8", 8), c_("key8", 8), ADD, ["h8", "key8"], ["khw"])
-        apk[2]()
-        scan(T.kho[:, 24:64], T.nbw[:], T.khw[:], BIG, MUL, MAX, ["nbw", "nbc", "khw", "khc"], ["kho"])
-        scan(T.sm[:, 192:200], T.nbw[:, 0:8], c_("e8", 8), BIG, MUL, MAX, ["nbw", "e8"], ["em"])
-        scan(T.cpo[:, 24:64], T.nbw[:], T.plw[:], BIG, MUL, MAX, ["nbw", "nbc", "plw", "plc"], ["cpo"])
-        tr(T.kt[:], T.kho[:, 32:64], ["kho"], ["kt"])
-        tt(T.kp[:], T.kho[:, 32:64], T.tm[:], ADD, ["kho", "tm"], ["kp"])
+        tt(T.khw[:, 0:8], c_("h8", 8), T.k8[:], ADD, ["h8", "k8"], ["khw"])
+        scan(T.kho[:], T.nbw[:], T.khw[:], BIG, MUL, MAX, ["nbw", "nbc", "khw", "khc"], ["kho"])
+        scan(EMW, T.nbw[:, 0:8], c_("e8", 8), BIG, MUL, MAX, ["nbw", "e8"], ["em"])
+        scan(CPW, T.nbw[:, 0:8], c_("plw", 8), BIG, MUL, MAX, ["nbw", "plw"], ["cpo"])
+        tr(T.kt[:], T.kho[:, 8:40], ["kho"], ["kt"])
+        av(T.kp[:], T.tm[:], ID, 1.0, T.kho[:, 39:40], ["kho", "tm"], ["kp"])
+        av(T.cpw[:, 34:66], T.zb[:, 0:32], ID, 1.0, CPO, ["zb", "cpo"], ["cpw"])
         ts(HN, EM, c_("amaxe"), -64.0, EQ, MUL, ["em", "amaxe"], ["hn"])
-        apk[3]()
         tt(T.qq[:, 0:32], T.kt[:], T.kp[:], EQ, ["kt", "kp"], ["qq"])
-        ts(c_("ca", 8), c_("nma", 8), HN, T.cpo[:, 63:64], SUB, ADD, ["nma", "hn", "cpo"], ["ca"])
-        a_side()
-        red(c_("xx"), T.qq[:, 0:34], ADD, ["qq", "qqc", "hn"], ["xx"])
-        own_pick()
+        scan(T.vv[:], T.qq[:], T.cpw[:], 0.0, ADD, MAX, ["qq", "qqc", "qqz", "hn", "cpc", "cpw"], ["vv"], 0.066)
+        tr(T.fb1[:], T.vv[:, 34:66], ["vv"], ["fb1"])
+        scan(T.fb2[:], T.cap4[:], T.fb1[:], 0.0, MAX, MIN, ["cap4", "fb1"], ["fb2"])
+        for a in range(4):
+            ts(T.fo[quad(a), :], T.fb2[Q0, 3:32:4], c_("c4", 1, Q0), 4 * PU, SUB, MUL, ["fb2", "c4c"], ["fo%d" % a])
+        xk = four("fo") + four("xc") + ["xr%da" % t]
+        XN = xw[:, 0:640].indirect(T.fo[:])
         if not last:
-            av(c_("de", 4), ae, ACT.Identity, -1.0, EM, [aek, "em"], ["de"])
-        sbt = turn("sb", ["sb0", "sb0a"])
-        rc, rs = window(t)
-
-        def f_val():
-            ts(T.fb0[:], T.cpo[:, 32:64], c_("xx"), c_("apos"), MAX, MIN, ["xx", "cpo", "apos"], ["fb0"])
-
-        def s_val():
-            ts(T.sb0[:, 0:32:4], c_("ca", 8), c_("xx"), OFF, MAX, MIN, ["ca", "xx", "off"], ["sb0a"])
-
-        def f_tr():
-            tr(T.fb1[:], T.fb0[:], ["fb0"], ["fb1"])
-
-        def f_choose():
-            choose(T.fb2[:], T.fb1[:], ["fb1"], ["fb2"])
-
-        def f_out():
-            for a in range(4):
-                ts(T.fo[quad(a), :], T.fb2[Q0, 15:32:16], c_("off", 1, Q0), PU, SUB, MUL, ["fb2", "off"], ["fo%d" % a])
-
-        def f_pick():
-            pickc("fa", 0, 32, w, 0, 256, T.fo[:], four("fo") + rc, ["fa.fc"])
-            picks("fa", 0, 32, w, 0, 256, T.fo[:], four("fo") + rs, ["fa.fs"])
-
-        def f_mm():
-            for b in range(4):
-                mm("pd%d" % b, "ee", 128 * b, "fa", 0, 128, False, True,
-                   ["ee%d" % b, "fa.fc", "fa.fs", "fa.ac", "fa.as", "fa.z"])
-
-        def s_add():
-            tt(T.of16[:], T.sb3[:].indirect(RL), T.sc16[:], ADD, ["sb3", "RL", "sc16a", "sc16b"], ["of16"])
-
-        def so_out():
-            for a in range(4):
-                ts(T.so[quad(a), 0:8], T.of16[Q0, 0:8], PU, None, MUL, None, ["of16"], ["so%d" % a])
-
-        xo, xn = T["xs%d" % t], T["xs%d" % (t + 1)]
-
-        def x_new(b):
-            tt(xn[:, b:128:4], T["pd%d" % b][:, 0:32], xo[:, b:128:4], ADD, ["Ppd%d" % b, "x%d.%d" % (t, b)],
-               ["x%d.%d" % (t + 1, b)])
-
-        def e_new(b):
-            tt(T.et[:, 128 * k + b:128 * k + 128:4], T.bt[:, b:128:4], xn[:, b:128:4], SUB,
-               ["bt", "x%d.%d" % (t + 1, b)], ["et.%d" % b])
-
-        if not last:
-            weave([f_val, s_val, f_tr, sbt[0], f_choose, sbt[1], f_out, sbt[2], f_pick, f_mm, s_add, so_out])
-            x_new(0)
-            x_new(1)
-            e_new(0)
-            x_new(2)
-            x_new(3)
-            e_new(1)
-            e_new(2)
-            e_new(3)
-            quant("qe%d" % (t + 1), 0, 128, T.et[:], four("et."), ["qe%d" % (t + 1)])
+            tt(ET, XN, T.bt[:], ADD, xk + ["bt"], ["et"], gat(128))
+            quant("qe%d" % (t + 1), 0, 128, T.et[:], ["et"], ["qe%d" % (t + 1)])
             send_e(t + 1)
-            slot_pick(t)
-            a_mm(t + 1)
-            own_e(t + 1)
-            nx, nk = act_e(t + 1)
-            weave(a_scores(), renew(ae, aek, c_("de", 4), "de", nx, nk))
-            side = []
-            if t == 0:
-                side = [lambda: quant("wq", 0, 256, T.wt[:], ["wt"], ["wq"])]
-            if t + 1 == R - 1:
-                side = [lambda: ts(c_("k4", 4), nx, RQ, RQ, ADD, SUB, [nk], ["k4"]),
-                        lambda: ts(c_("j4", 4), nx, RJ, RJ, ADD, SUB, [nk], ["j4"]),
-                        lambda: ts(c_("k5", 4), c_("k4", 4), TAGN, None, MUL, None, ["k4"], ["k5"]),
-                        lambda: tt(c_("no", 4), c_("k5", 4), c_("j4", 4), ADD, ["k5", "j4"], ["no"])]
-            weave(a_chain(), side)
+            av(T["xw%d" % (t + 1)][:, 512:640], XN, ID, 1.0, 0.0, xk, ["xr%da" % (t + 1)], gat(128))
+            copies(t + 1)
         else:
-            wl = "win%d" % R
-            rn = renew(c_("no", 4), "no", c_("de", 4), "de", T.nn0[:, 0:4], "nn0a")
-            weave([s_val, f_val, sbt[0], f_tr, sbt[1], f_choose, sbt[2]])
-            ts(c_("key"), EM, RQ, RQ, ADD, SUB, ["em"], ["key"])
-            s_add()
-            ts(c_("jr"), EM, RJ, RJ, ADD, SUB, ["em"], ["jr"])
-            so_out()
-            f_out()
-            slot_pick(t)
-            f_pick()
-            y_mm(t)
-            f_mm()
-            av(c_("fn"), c_("key"), ACT.Identity, TAGN, c_("jr"), ["key", "jr"], ["fn"])
-            av(c_("de", 4), c_("no", 4), ACT.Identity, -1.0, c_("fn"), ["no", "fn"], ["de"])
-            store("s", T.oc[:], bytes_of(wl, 128, 256), [wl + ".sc"])
-            for a in range(2):
-                store("s", T.osc[4 * a:4 * a + 4, :], T[wl + "s"][32 * a:32 * a + 4, 128:256], [wl + ".ss"])
-            rn[0]()
-            ys = T["ys%d" % t]
-            op("a", lambda: S.activation(ys[:, 0:128], T.py[:, 0:128], ACT.Copy), ["Ppy"], ["ys.0"])
-            cp(ys[:, 128:256], T.pa[:, 0:128], ["Ppa"], ["ys.1"])
-            store("a", T.y[:, 256 * t:256 * t + 256], ys[:], ["ys.0", "ys.1"])
-            for a in range(2, 4):
-                store("a", T.osc[4 * a:4 * a + 4, :], T[wl + "s"][32 * a:32 * a + 4, 128:256], [wl + ".ss"])
-            rn[1]()
-            weave([lambda b=b: x_new(b) for b in range(4)])
-            rn[2]()
-            cp(T.pxs[:], xn[:], four("x%d." % R), ["pxs"])
-            tr(T.nn1[:], T.nn0[:], ["nn0", "nn0a"], ["nn1"])
-            store("s", T.px[:], T.pxs[:], ["pxs"])
-            store("s", T.an[:], T.nn1[ka:ka + 4, :], ["nn1"])
-    assert sum(v[1] for v in cols.values()) <= 192
+            af(T.pxs[:], XN, -1.0, 0.0, xk, ["pxs"], gat(128))
+            dma("s", T.px[:], T.pxs[:], ["pxs"], [], "st")
+        w2 = "win%d" % (t + 1)
+        ts(T.zs0[:], T.nmb[:], T.vv[:, 65:66], HN, ADD, SUB, ["nmb", "vv", "hn"], ["zs0"], W1)
+        tr(T.zs1[:], T.zs0[:], ["zs0"], ["zs1"], W1)
+        scan(T.zs2[:], T.caps[:], T.zs1[:], 0.0, MAX, MIN, ["caps", "zs1"], ["zs2"], W1)
+        for a in range(4):
+            ts(T.so[quad(a), :], T.zs2[Q0, 15:128:16], P15Q, PU, SUB, MUL, ["zs2", "pf"], ["so%d" % a])
+        pick(w2, 128, 256, w, 0, 256, T.so[:], four("so") + [w + ".sc", w + ".oc", w + ".r"],
+             four("so") + [w + ".ss", w + ".os", w + ".r"], [w2 + ".sc"], [w2 + ".ss"])
+        av(c_("de", 4), ae, ID, -1.0, EM, [aek, "em"], ["de"])
+        ts(c_("m2", 4), T.zs0[:, 0:128:32], c_("thr"), None, LT, None, ["zs0", "thr"], ["m2"])
+        tt(c_("dd", 4), c_("m2", 4), c_("de", 4), MUL, ["m2", "de"], ["dd"])
+        if not last:
+            tt(c_("ae%d" % (t + 1), 4), ae, c_("dd", 4), ADD, [aek, "dd"], ["ae%d" % (t + 1)])
+        else:
+            tt(T.nn0[:, 0:4], ae, c_("dd", 4), ADD, [aek, "dd"], ["nn0"])
+            tr(T.nn1[:], T.nn0[:], ["nn0"], ["nn1"])
+            dma("s", T.an[:], T.nn1[ka:ka + 4, :], ["nn1"], [], "st")
+            dma("s", T.oc[:], bytes_of(w2, 128, 256), [w2 + ".sc"], [], "st", 1.8)
+            for a in range(4):
+                dma("sa"[a // 2], T.osc[4 * a:4 * a + 4, :], T[w2 + "s"][32 * a:32 * a + 4, 128:256], [w2 + ".ss"], [], "st")
+            y_mm(w, 0, cand)
+            for o, bank in enumerate(("py", "pa")):
+                av(T.yw[:, 256 * o:256 * o + 128], T[bank][:, 0:128], ID, 1.0, 0.0, ["P" + bank], ["yc%d" % o], W1)
+            af(T.yo[:, 0:128], T.yw[:, 0:256].indirect(T.so[:]), 1.0, 0.0, four("so") + ["yc0", "yw0"], ["yo0"], gat(128))
+            av(T.yo[:, 128:256], T.yw[:, 256:512].indirect(T.so[:]), ID, 1.0, 0.0, four("so") + ["yc1", "yw1"], ["yo1"],
+               gat(128))
+            dma("a", T.y[:, 512:768], T.yo[:], ["yo0", "yo1"], [], "st", 2.0)
+    assert sum(v[1] for v in cols.values()) <= 128
 
+    for j, q in arrange(nodes):
+        nodes[j][1](q)
     for s in ("sv", "sa", "sp", "sg", "ls"):
         g.wait_ge(T.sem[s], count[s])
     g.sync.wait_ge(T.sem.st, count["st"])

@@ -5,7 +5,8 @@ N, A, M, CAPP, R, O = 8, 384, 32, 4, 3, 2
 G = N // 2
 HI = A
 AW = 2 * A
-NP = 1
+NP = 3
+PW = A // NP
 C8, U8, F32, BF, U16, I32 = "float8_e4m3fn_x4", "uint8", "float32", "bfloat16", "uint16", "int32"
 
 SCRATCH = {}
@@ -63,8 +64,9 @@ ACT = ActivationFunctionType
 BIG = float(2 ** 20)
 PU = 1024.0
 ZU = 2048.0
-ISSUE, HOP, LOAD, SX, SLACK = 0.25, 1.5, 1.6, 0.03, 1.0
-CASES = ((0.12, 0.3), (0.17, 0.0), (0.2, -0.2))
+ISSUE, HOP, LOAD, SX, SLACK = 0.25, 1.3, 1.6, 0.03, 1.0
+CASES = ((0.17, 0.0), (0.14, 0.3), (0.2, -0.15))
+DONE, TURNS, MOVES, SHAKE = {}, 200, 8, 0.5
 
 
 def places(k):
@@ -161,17 +163,27 @@ def arrange(nodes):
             end = max(end, start[j] + span(j, where, case))
         return end
 
-    best = None
-    first = {j: nodes[j][0][-1] for j in range(n)}
-    for case in CASES:
+    shape = tuple(tuple(p) for p in pred)
+    if shape not in DONE:
+        first = {j: nodes[j][0][-1] for j in range(n)}
+        case = CASES[0]
         key = [0.0] * n
         for i in range(n - 1, -1, -1):
             key[i] = min([key[j] - lat(i, j, first, case) for j in succ[i]] + [-span(i, first, case)])
-        seq, where = forward(key, case)
-        cost = sum(length(seq, where, c) for c in CASES)
-        if best is None or cost < best[0]:
-            best = (cost, seq, where)
-    return [(j, best[2][j]) for j in best[1]]
+        best, seed = None, 1
+        for turn in range(TURNS):
+            trial = list(best[3] if best else key)
+            for _ in range(MOVES if turn else 0):
+                seed = (seed * 1103515245 + 12345) % 2147483648
+                j = (seed >> 8) % n
+                seed = (seed * 1103515245 + 12345) % 2147483648
+                trial[j] += SHAKE * (seed / 1073741824.0 - 1.0)
+            seq, where = forward(trial, case)
+            cost = sum(length(seq, where, c) for c in CASES)
+            if best is None or cost <= best[0]:
+                best = (cost, seq, where, trial)
+        DONE[shape] = [(j, best[2][j]) for j in best[1]]
+    return DONE[shape]
 
 
 def rank_program(g, core, T, topo):
@@ -214,7 +226,8 @@ def rank_program(g, core, T, topo):
             if key[0] == "P":
                 toks += [tk for tk in rd.get(key, []) if tk[3] != q]
         for key in writes:
-            toks += wr.get(key, []) + rd.get(key, [])
+            if key[0] != "#":
+                toks += wr.get(key, []) + rd.get(key, [])
         if q == "p":
             toks = [tk for tk in toks if tk[3] != "p"]
         need(q, toks)
@@ -292,6 +305,10 @@ def rank_program(g, core, T, topo):
         op("va", {"v": lambda: V.tensor_scalar(out, a, scale, bias, MUL, ADD),
                   "a": lambda: S.activation(out, a, ID, bias=bias, scale=scale)}, r, w, {"v": c, "a": c + SX})
 
+    def move(out, a, r, w, c=W0):
+        op("va", {"v": lambda: V.tensor_copy(out, a), "a": lambda: S.activation(out, a, ACT.Copy)}, r, w,
+           {"v": c, "a": c + SX})
+
     def quant(name, a, b, src, r, w):
         op("v", lambda: V.quantize_mx(T[name + "c"][:, a:b], T[name + "s"][:, a:b], src), r, w, 0.015 + (b - a) * 1.05e-3)
 
@@ -300,10 +317,10 @@ def rank_program(g, core, T, topo):
         op("a", lambda: S.activation(T[dn + "s"][:, a:b], T[sn + "s"][:, c:d].indirect(off), ACT.Copy), rs, ws,
            gat(b - a) + 0.015)
 
-    def mm(bank, ln, la, rn, ra, n, start, stop, r):
+    def mm(bank, ln, la, rn, ra, n, start, stop, r, w=()):
         op("p", lambda: P.matmul_mx(T[bank][:, 0:n], T[ln + "c"][:, la:la + 128], T[ln + "s"][:, la:la + 128],
                                     T[rn + "c"][:, ra:ra + n], T[rn + "s"][:, ra:ra + n], start, stop),
-           r, ["P" + bank], (n + 16) * 6e-4)
+           r, ["P" + bank] + list(w), (n + 16) * 6e-4)
 
     def dma(q, out, src, r, w, sem, last=LOAD):
         op(q, lambda: queues[q].dma_start(out, src), r, w, 0.05, sem, 16, last)
@@ -333,16 +350,14 @@ def rank_program(g, core, T, topo):
 
     EL, AL = T.cu[:, 2:4], T.cu[:, 4:5]
 
-    dma("s", T.xs[:], T.x[:], [], ["xs"], "lx", 1.7)
-    dma("a", T.bt[:], T.b[:], [], ["bt", "#b"], "lb", 1.7)
-    PW = A // NP
-    for j in range(NP):
-        dma("a", T.dtile[:, 4 * PW * j:4 * PW * j + 4 * PW], T.d[:, 4 * PW * j:4 * PW * j + 4 * PW], ["#b"], ["dt%d" % j],
-            "ld%d" % j, 1.7 + 1.2 * (j + 1) / NP)
-    dma("s", T.acti[ka:ka + 16, :], T.act[:], [], ["actia"], "la", 3.3)
-    dma("s", T.acti[ka + 16:kb, :], T.act[:], [], ["actib"], "la", 3.3)
+    for j, last in enumerate((1.75, 2.3, 3.0)):
+        dma("a", T.dtile[:, 4 * PW * j:4 * PW * j + 4 * PW], T.d[:, 4 * PW * j:4 * PW * j + 4 * PW],
+            ["#d%d" % (j - 1)] * (j > 0), ["dt%d" % j, "#d%d" % j], "ld%d" % j, last)
+    dma("s", T.xs[:], T.x[:], [], ["xs", "#x"], "lx", 1.95)
+    dma("s", T.bt[:], T.b[:], ["#x"], ["bt", "#b"], "lb", 2.5)
+    dma("s", T.acti[ka:ka + 16, :], T.act[:], ["#b"], ["actia"], "la", 3.1)
+    dma("s", T.acti[ka + 16:kb, :], T.act[:], ["#b"], ["actib"], "la", 3.1)
     arrives("la", 32, ["actia", "actib"], ["acti"], 0.0)
-    dma("s", T.wt[:], T.w[:], ["dt%d" % (NP - 1)], ["wt"], "lw", 2.5)
 
     iota(T.si[:, 0:1], [[1, 1]], 0, 1, ["pi"], 1, False)
     iota(T.jd[:], [[1, 128]], 0, -1, ["jd"], 128)
@@ -408,15 +423,16 @@ def rank_program(g, core, T, topo):
     av(T.n1[:], T.cw[:], ID, 1.0, P15, ["cw", "pf"], ["n1"], W1)
     tt(T.caps[:], T.cu1[:], T.n1[:], ADD, ["cu1", "n1"], ["caps"], W2)
 
-    def send_e(t):
+    def send_e(t, after):
         es = topo.engines(core, peers[0])
-        n, h = "qe%d" % t, len(es) // 2
-        e1, e2 = (es[:h], es[h:]) if t == 0 else (es, es)
-        send([xfer(bytes_of(n, ka, kb), [(c, bytes_of("eg%d" % t, ka, kb)) for c in peers], e1, "ae%d" % t)], [n],
-             "#ec%d" % t)
-        send([xfer(T[n + "s"][:, ka:kb], [(c, T["eg%ds" % t][:, ka:kb]) for c in peers], e2, "ae%d" % t)],
-             [n, "#ec%d" % t], "#es%d" % t)
-        arrives("ae%d" % t, (len(e1) + len(e2)) * len(peers), ["#es%d" % t], ["eg%d.r" % t], HOP + (1.5 if t == 0 else 0))
+        n = "qe%d" % t
+        calls = [xfer(bytes_of(n, ka, kb), [(c, bytes_of("eg%d" % t, ka, kb)) for c in peers], es, "ae%d" % t),
+                 xfer(T[n + "s"][:, ka:kb], [(c, T["eg%ds" % t][:, ka:kb]) for c in peers], es, "ae%d" % t)]
+        if t == 0:
+            calls.reverse()
+        send(calls[:1], [n] + after, "#ea%d" % t)
+        send(calls[1:], [n, "#ea%d" % t], "#eb%d" % t)
+        arrives("ae%d" % t, 2 * len(es) * len(peers), ["#eb%d" % t], ["eg%d.r" % t], HOP + (1.0 if t == 0 else 0))
         pick("eg%d" % t, ka, kb, n, ka, kb, EL, ["EL", n], ["EL", n], ["eg%d.c" % t], ["eg%d.s" % t])
 
     def copies(t):
@@ -427,25 +443,30 @@ def rank_program(g, core, T, topo):
     ET = T.et[:, 128 * k:128 * k + 128]
     tt(ET, T.bt[:], T.xs[:], SUB, ["bt", "xs"], ["et"], W2)
     quant("qe0", 0, 128, T.et[:], ["et"], ["qe0"])
-    send_e(0)
     av(T.xw0[:, 512:640], T.xs[:], ID, -1.0, 0.0, ["xs"], ["xr0a"], W1)
     copies(0)
     es = topo.engines(core, mate)
-    mark = "#es0"
-    for j in range(NP):
-        a, b = own0 + PW * j, own0 + PW * j + PW
-        quant("at", a, b, T.dtile[:, 4 * PW * j:4 * PW * j + 4 * PW], ["dt%d" % j], ["at.%d" % j])
-        send([xfer(bytes_of("at", a, b), [(mate, bytes_of("at", a, b))], es, "aa")], ["at.%d" % j, mark], "#ac%d" % j)
-        send([xfer(T.ats[:, a:b], [(mate, T.ats[:, a:b])], es, "aa")], ["at.%d" % j, "#ac%d" % j], "#as%d" % j)
-        mark = "#as%d" % j
-    arrives("aa", 2 * NP * len(topo.engines(mate, core)), [mark], ["at.r"], HOP + 0.9 / NP)
+    half = len(es) // 2
     ato = ["at.%d" % j for j in range(NP)]
+
+    def piece(j, engines, after):
+        a, b = own0 + PW * j, own0 + PW * j + PW
+        quant("at", a, b, T.dtile[:, 4 * PW * j:4 * PW * j + 4 * PW], ["dt%d" % j] + ato[j - 1:j], [ato[j]])
+        send([xfer(bytes_of("at", a, b), [(mate, bytes_of("at", a, b))], engines, "aa")], [ato[j]] + after, "#a%d" % j)
+
+    piece(0, es[:half], [])
+    piece(1, es[half:], ["#a0"])
+    send_e(0, ["#a1"])
+    piece(2, es, ["#eb0"])
+    send([xfer(T.ats[:, own0:own0 + A], [(mate, T.ats[:, own0:own0 + A])], es, "aa")], ato + ["#a2"], "#as")
+    arrives("aa", 3 * len(es), ["#as"], ["at.r"], 1.7)
 
     for a in range(4):
         cp(T.af[quad(a), :], T.acti[Q0, :], ["acti"], ["af%d" % a])
     cp(T.aoff[:], T.af[:], four("af"), ["aoff"])
     ts(T.ae0[:], T.af[:].indirect(AL), float(A * rank), None, ADD, None, four("af") + ["AL"], ["ae0"], gat(16))
     pick("win0", 128, 256, "at", own0, own0 + A, T.aoff[:], ["aoff"] + ato, ["aoff"] + ato, ["win0.sc"], ["win0.ss"])
+    dma("s", T.wt[:], T.w[:], ["at.r"], ["wt"], "lw", 2.5)
     quant("wq", 0, 256, T.wt[:], ["wt"], ["wq"])
 
     def y_mm(w, a, keys):
@@ -508,25 +529,25 @@ def rank_program(g, core, T, topo):
         mine = [mk + ".m", c1k, c2k]
         mv = ml[:, m0:m0 + 4]
         send([xfer(mv, [(c, mv) for c in peers], topo.engines(core, peers[0]), "am%d" % t)], mine, "#m%d" % t)
-        arrives("am%d" % t, sum(len(topo.engines(c, core)) for c in peers), ["#m%d" % t], [mk + ".r"], HOP - 0.2)
+        arrives("am%d" % t, sum(len(topo.engines(c, core)) for c in peers), ["#m%d" % t], [mk + ".r"], HOP - 0.15)
         CF, cfk, CL, clk = (C2, c2k, C1, c1k) if own0 else (C1, c1k, C2, c2k)
         ts(T.gb[:], T.zb[:, 0:64], M2, M1, ADD, LE if own0 else GT, ["zb", "r1", "r2"], ["gb"])
         ts(c_("gh"), M2, M1, None, GT if own0 else LE, None, ["r1", "r2"], ["gh"])
-        ts(c_("gu"), CF, float(HI if own0 else -HI), None, ADD, None, [cfk], ["gu"])
-        ts(c_("rest"), c_("gu"), c_("gh"), c_("off3"), MUL, ADD, ["gh", "gu", "off3"], ["rest"])
+        ts(c_("gu"), c_("gh"), float(HI if own0 else -HI), c_("off3"), MUL, ADD, ["gh", "off3"], ["gu"])
+        ts(c_("rest"), CF, c_("gh"), c_("gu"), MUL, ADD, ["gh", "gu", cfk], ["rest"])
         ts(T.z0[:], T.gb[:], CL, c_("rest"), MUL, ADD, ["gb", clk, "rest"], ["z0"])
         tr(T.z1[:], T.z0[:], ["z0"], ["z1"])
         scan(T.zy[:], T.msel[:], T.z1[:], 0.0, MUL, MAX, ["msel", "z1"], ["zy"] + four("zc"))
         for h in range(2):
             f, s = order[2 * h], order[2 * h + 1]
-            cp(T.zy[quad(s), 15:32:16], T.zy[quad(f), 15:32:16], ["zy"], ["zc%d" % (2 * h)])
-            cp(T.zy[quad(f), 47:64:16], T.zy[quad(s), 47:64:16], ["zy"], ["zc%d" % (2 * h + 1)])
-        for h in range(2):
+            move(T.zy[quad(s), 15:32:16], T.zy[quad(f), 15:32:16], ["zy"], ["zc%d" % (2 * h)])
+            move(T.zy[quad(f), 47:64:16], T.zy[quad(s), 47:64:16], ["zy"], ["zc%d" % (2 * h + 1)])
+        for h, a, b, zk in ((0, 0, 4, ["zc0", "zc1"]), (1, 0, 2, ["zc2"]), (1, 2, 4, ["zc3"])):
             src = slice(64 * (order[2 * h] // 2), 64 * (order[2 * h] // 2) + 64)
             for d in range(2):
-                ts(T.ho[64 * d:64 * d + 64, 4 * h:4 * h + 4], T.zy[src, 15:64:16], c_("off2", 1, src), None, SUB, None,
-                   ["zy", "zc%d" % (2 * h), "zc%d" % (2 * h + 1), "off2"], ["ho%d" % (2 * h + d)])
-        hk = four("ho") + ato + ["at.r"]
+                ts(T.ho[64 * d:64 * d + 64, 4 * h + a:4 * h + b], T.zy[src, 15 + 16 * a:16 * b:16], c_("off2", 1, src), None,
+                   SUB, None, ["zy", "off2"] + zk, ["ho%d%d%d" % (h, a, d)])
+        hk = ["ho000", "ho001", "ho100", "ho101", "at.r"] + ato
         pick(pk, 0, 96, "at", 0, AW, T.ho[:, 0:6], hk, hk, [pk + ".c"], [pk + ".s"])
         ec, esc = splits(topo.engines(core, peers[0]))
         send([xfer(bytes_of(pk, 32 * i, 32 * i + 32), [(grp[order[i]], bytes_of(w, ka, kb))], ec[i], "ac%d" % t)
@@ -535,10 +556,12 @@ def rank_program(g, core, T, topo):
               for i in range(3)], [pk + ".s", "#c%d" % t], "#s%d" % t)
         arrives("ac%d" % t, sum(len(splits(topo.engines(grp[s], core))[j][places(s).index(k)])
                                 for s in range(G) if s != k for j in range(2)), ["#s%d" % t], [w + ".r"], HOP)
+        hk = ["ho120", "ho121", "at.r"] + ato
         pick(w, ka, kb, "at", 0, AW, T.ho[:, 6:8], hk, hk, [w + ".oc"], [w + ".os"])
         cand = [w + ".oc", w + ".os", w + ".r"]
         for b in range(4):
-            mm("pd%d" % b, "ee", 512 + 128 * b, w, 0, 128, False, True, ["ee%d" % (4 + b)] + cand)
+            mm("pd%d" % b, "ee", 512 + 128 * b, w, 0, 128, False, True,
+               ["ee%d" % (4 + b)] + cand + ["#f%d" % (b - 1)] * (b > 0), ["#f%d" % b])
         for b in range(4):
             tt(xw[:, b:512:4], T["pd%d" % b][:, 0:128], xw[:, 512 + b:1024:4], ADD,
                ["Ppd%d" % b] + ["xr%d%s" % (t, s) for s in "abc"], ["xc%d" % b], W1)
@@ -570,12 +593,12 @@ def rank_program(g, core, T, topo):
         if not last:
             tt(ET, XN, T.bt[:], ADD, xk + ["bt"], ["et"], gat(128))
             quant("qe%d" % (t + 1), 0, 128, T.et[:], ["et"], ["qe%d" % (t + 1)])
-            send_e(t + 1)
+            send_e(t + 1, [])
             av(T["xw%d" % (t + 1)][:, 512:640], XN, ID, 1.0, 0.0, xk, ["xr%da" % (t + 1)], gat(128))
             copies(t + 1)
         else:
             af(T.pxs[:], XN, -1.0, 0.0, xk, ["pxs"], gat(128))
-            dma("s", T.px[:], T.pxs[:], ["pxs"], [], "st")
+            dma("s", T.px[:], T.pxs[:], ["pxs"], [], "st", 1.9)
         w2 = "win%d" % (t + 1)
         ts(T.zs0[:], T.nmb[:], T.vv[:, 65:66], HN, ADD, SUB, ["nmb", "vv", "hn"], ["zs0"], W1)
         tr(T.zs1[:], T.zs0[:], ["zs0"], ["zs1"], W1)
@@ -592,17 +615,17 @@ def rank_program(g, core, T, topo):
         else:
             tt(T.nn0[:, 0:4], ae, c_("dd", 4), ADD, [aek, "dd"], ["nn0"])
             tr(T.nn1[:], T.nn0[:], ["nn0"], ["nn1"])
-            dma("s", T.an[:], T.nn1[ka:ka + 4, :], ["nn1"], [], "st")
-            dma("s", T.oc[:], bytes_of(w2, 128, 256), [w2 + ".sc"], [], "st", 1.8)
+            dma("s", T.an[:], T.nn1[ka:ka + 4, :], ["nn1"], [], "st", 2.2)
+            dma("s", T.oc[:], bytes_of(w2, 128, 256), [w2 + ".sc"], [], "st", 2.0)
             for a in range(4):
                 dma("sa"[a // 2], T.osc[4 * a:4 * a + 4, :], T[w2 + "s"][32 * a:32 * a + 4, 128:256], [w2 + ".ss"], [], "st")
             y_mm(w, 0, cand)
             for o, bank in enumerate(("py", "pa")):
-                av(T.yw[:, 256 * o:256 * o + 128], T[bank][:, 0:128], ID, 1.0, 0.0, ["P" + bank], ["yc%d" % o], W1)
-            af(T.yo[:, 0:128], T.yw[:, 0:256].indirect(T.so[:]), 1.0, 0.0, four("so") + ["yc0", "yw0"], ["yo0"], gat(128))
-            av(T.yo[:, 128:256], T.yw[:, 256:512].indirect(T.so[:]), ID, 1.0, 0.0, four("so") + ["yc1", "yw1"], ["yo1"],
-               gat(128))
-            dma("a", T.y[:, 512:768], T.yo[:], ["yo0", "yo1"], [], "st", 2.0)
+                move(T.yw[:, 256 * o:256 * o + 128], T[bank][:, 0:128], ["P" + bank], ["yc%d" % o], W1)
+                af(T.yo[:, 128 * o:128 * o + 128], T.yw[:, 256 * o:256 * o + 256].indirect(T.so[:]), 1.0, 0.0,
+                   four("so") + ["yc%d" % o, "yw%d" % o], ["yo%d" % o], gat(128))
+                dma("a", T.y[:, 512 + 128 * o:640 + 128 * o], T.yo[:, 128 * o:128 * o + 128], ["yo%d" % o], [], "st",
+                    2.3 - 0.2 * o)
     assert sum(v[1] for v in cols.values()) <= 128
 
     for j, q in arrange(nodes):

from concourse.bass import DstId, RemoteDMATransfer
from concourse.mybir import dt, AluOpType, AxisListType, ActivationFunctionType

N, A, M, CAPP, R, O = 8, 384, 32, 4, 3, 2
G = N // 2
HI = A
AW = 2 * A
NP = 3
PW = A // NP
C8, U8, F32, BF, U16, I32 = "float8_e4m3fn_x4", "uint8", "float32", "bfloat16", "uint16", "int32"

SCRATCH = {}


def _sb(name, cols, dtype):
    SCRATCH[name] = ("sbuf", [128, cols], dtype)


def _mx(name, cols):
    _sb(name + "c", cols, C8)
    _sb(name + "s", cols, U8)


_mx("at", AW)
_mx("ee", 1024)
_mx("wq", 256)
for _t in range(R):
    _mx("qe%d" % _t, 128)
    _mx("eg%d" % _t, 128)
    _mx("pk%d" % _t, 96)
    _mx("fa%d" % _t, 128)
    _sb("ml%d" % _t, 16, F32)
    _sb("xw%d" % _t, 1024, BF)
for _t in range(R + 1):
    _mx("win%d" % _t, 256)
for _n, _c, _d in (
        ("dtile", 4 * A, BF), ("wt", 1024, BF), ("bt", 128, BF), ("xs", 128, BF), ("et", 512, BF), ("pxs", 128, F32),
        ("ua", 516, BF), ("ub", 516, BF), ("na", 516, BF), ("nb", 516, BF), ("zb", A, BF), ("junk", 2 * A, BF),
        ("jd", 128, F32), ("ad", 128, F32), ("j2", 128, F32), ("aj", 128, F32), ("d4", 128, F32), ("kp4", 128, F32),
        ("am", 128, F32), ("asc", 128, F32), ("r21", 2 * A, F32), ("ci", 128, I32), ("cj", 128, I32), ("c4", 32, I32),
        ("cw", 128, F32), ("cu1", 128, F32), ("caps", 128, F32), ("cap4", 32, F32), ("u4", 64, F32),
        ("sbk", 128, F32), ("c32", 128, F32), ("n1", 128, F32), ("nmb", 128, F32),
        ("ab0", 128, F32), ("ab1", 128, F32), ("ab2", 128, F32), ("zs0", 128, F32), ("zs1", 128, F32), ("zs2", 128, F32),
        ("ys0", 256, F32), ("yw", 512, F32), ("yo", 256, F32),
        ("sm", 128, F32), ("si", 16, I32), ("acti", 8, I32), ("af", 8, F32), ("ae0", 16, F32),
        ("tm", 32, F32), ("kt", 32, F32), ("kp", 32, F32), ("qq", 66, F32), ("cpw", 66, F32), ("vv", 66, F32),
        ("nbw", 40, F32), ("khw", 40, F32), ("kho", 40, F32), ("gb", 64, F32), ("msel", 64, F32),
        ("z0", 64, F32), ("z1", 64, F32), ("zy", 64, F32), ("fb1", 32, F32), ("fb2", 32, F32),
        ("nn0", 32, F32), ("nn1", 32, F32), ("k8", 8, F32), ("p8", 8, F32),
        ("cu", 16, U16), ("ho", 8, U16), ("so", 8, U16), ("fo", 8, U16), ("ao", 8, U16), ("aoff", 8, U16)):
    _sb(_n, _c, _d)
for _n in ("pd0", "pd1", "pd2", "pd3", "ps1", "ps2", "pa", "py"):
    SCRATCH[_n] = ("psum", [128, 512], F32)

SEMAPHORES = ["sv", "sa", "sp", "sg", "ls", "lx", "lb", "lw", "la", "st", "aa"]
for _t in range(R):
    SEMAPHORES += ["ae%d" % _t, "am%d" % _t, "ac%d" % _t, "ld%d" % _t]

ADD, SUB, MUL, MAX, MIN = AluOpType.add, AluOpType.subtract, AluOpType.mult, AluOpType.max, AluOpType.min
EQ, NE, GT, LT, LE = AluOpType.is_equal, AluOpType.not_equal, AluOpType.is_gt, AluOpType.is_lt, AluOpType.is_le
AND, SHR = AluOpType.bitwise_and, AluOpType.logical_shift_right
X = AxisListType.X
ACT = ActivationFunctionType
BIG = float(2 ** 20)
PU = 1024.0
ZU = 2048.0
ISSUE, HOP, LOAD, SX, SLACK = 0.25, 1.3, 1.6, 0.03, 1.0
CASES = ((0.17, 0.0), (0.14, 0.3), (0.2, -0.15))
DONE, TURNS, MOVES, SHAKE = {}, 200, 8, 0.5


def places(k):
    return [s for s in range(G) if s // 2 != k // 2] + [k ^ 1, k]


def bits(es):
    m = 0
    for e in es:
        m |= 1 << e
    return m


def splits(es):
    q = len(es) // 4
    return ([es[:2 * q], es[2 * q:3 * q], es[3 * q:]], [es[:q], es[q:2 * q], es[2 * q:]])


def arrange(nodes):
    wr, rd, pred, soft = {}, {}, [], []
    for i, (q, _, reads, writes, _, _) in enumerate(nodes):
        ps = set()
        soft.append(set(wr[key] for key in reads if key[0] == "#" and q != "r"))
        for key in reads:
            ps.add(wr[key])
            if key[0] == "P":
                ps.update(j for j in rd.get(key, []) if nodes[j][0] != q or len(q) > 1)
        for key in writes:
            ps.update(rd.get(key, []))
            if key in wr:
                ps.add(wr[key])
        ps.discard(i)
        pred.append(sorted(ps))
        for key in reads:
            rd.setdefault(key, []).append(i)
        for key in writes:
            wr[key] = i
            rd[key] = []
    n = len(nodes)
    succ = [[] for _ in nodes]
    for j in range(n):
        for i in pred[j]:
            succ[i].append(j)

    def span(i, where, case):
        q = nodes[i][0]
        return nodes[i][4][where[i]] if len(q) > 1 else nodes[i][5] + (case[1] if q == "r" and nodes[i][5] else 0.0)

    def lat(i, j, where, case):
        if i in soft[j]:
            return nodes[i][4][where[i]]
        free = nodes[j][0] == "r" or nodes[i][0] == nodes[j][0] == "p"
        return span(i, where, case) + (0.0 if free else case[0])

    def forward(key, case):
        start, where, seq = {}, {}, []
        free = {q: 0.0 for q in "vapgsr"}
        left = [len(p) for p in pred]
        ready = {j: 0.0 for j in range(n) if not pred[j]}
        late = -min(key)
        while ready:
            t, q = min((max(free[q], r), q) for j, r in ready.items() for q in nodes[j][4])
            mine = [(key[j], j) for j in ready if q in nodes[j][4]]
            soon = [(ku, u) for ku, u in mine if ready[u] > t + 1e-9]
            j = None
            for kj, c in sorted(e for e in mine if ready[e[1]] <= t + 1e-9):
                end = t + nodes[c][4][q]
                if all(ready[u] >= end - 1e-9 or ku >= kj or end - ku <= late - SLACK
                       or end - ku <= ready[u] + nodes[u][4][q] - kj for ku, u in soon):
                    j = c
                    break
            if j is None:
                free[q] = min(ready[u] for _, u in soon)
                continue
            del ready[j]
            start[j], where[j] = t, q
            seq.append(j)
            late = max(late, t - key[j])
            if q != "r":
                free[q] = t + nodes[j][4][q]
            for s in succ[j]:
                left[s] -= 1
                if not left[s]:
                    ready[s] = max(start[i] + lat(i, s, where, case) for i in pred[s])
        return seq, where

    def length(seq, where, case):
        start, free, end = {}, {}, 0.0
        for j in seq:
            q = where[j]
            start[j] = max([start[i] + lat(i, j, where, case) for i in pred[j]] + [free.get(q, 0.0)])
            if q != "r":
                free[q] = start[j] + nodes[j][4][q]
            end = max(end, start[j] + span(j, where, case))
        return end

    shape = tuple(tuple(p) for p in pred)
    if shape not in DONE:
        first = {j: nodes[j][0][-1] for j in range(n)}
        case = CASES[0]
        key = [0.0] * n
        for i in range(n - 1, -1, -1):
            key[i] = min([key[j] - lat(i, j, first, case) for j in succ[i]] + [-span(i, first, case)])
        best, seed = None, 1
        for turn in range(TURNS):
            trial = list(best[3] if best else key)
            for _ in range(MOVES if turn else 0):
                seed = (seed * 1103515245 + 12345) % 2147483648
                j = (seed >> 8) % n
                seed = (seed * 1103515245 + 12345) % 2147483648
                trial[j] += SHAKE * (seed / 1073741824.0 - 1.0)
            seq, where = forward(trial, case)
            cost = sum(length(seq, where, c) for c in CASES)
            if best is None or cost <= best[0]:
                best = (cost, seq, where, trial)
        DONE[shape] = [(j, best[2][j]) for j in best[1]]
    return DONE[shape]


def rank_program(g, core, T, topo):
    rank = T.rank_of(core)
    if rank is None:
        return
    grp, k, mate = list(T.cores[rank % 2::2]), rank // 2, T.cores[rank ^ 1]
    own0 = 0 if rank == 2 * k else HI
    order = places(k)
    peers = [grp[s] for s in range(G) if s != k]
    Q0 = slice(32 * k, 32 * k + 32)
    ka, kb = 32 * k, 32 * k + 32

    queues = {"v": g.vector, "a": g.scalar, "p": g.tensor, "g": g, "s": g.sync}
    semof = {"v": "sv", "a": "sa", "p": "sp", "g": "sg"}
    count, nodes = {}, []
    clock = {q: {} for q in queues}
    wr, rd = {}, {}

    def need(q, toks):
        ck = clock[q]
        best = {}
        for tk in toks:
            if ck.get(tk[0], 0) < tk[1] and best.get(tk[0], (0, 0))[1] < tk[1]:
                best[tk[0]] = tk
        for tk in sorted(best.values(), key=lambda tk: -len(tk[2])):
            if ck.get(tk[0], 0) >= tk[1]:
                continue
            queues[q].wait_ge(T.sem[tk[0]], tk[1])
            for s, n in tk[2].items():
                if ck.get(s, 0) < n:
                    ck[s] = n

    def deps(q, reads, writes):
        toks = []
        for key in reads:
            if key[0] == "#":
                continue
            toks += wr[key]
            if key[0] == "P":
                toks += [tk for tk in rd.get(key, []) if tk[3] != q]
        for key in writes:
            if key[0] != "#":
                toks += wr.get(key, []) + rd.get(key, [])
        if q == "p":
            toks = [tk for tk in toks if tk[3] != "p"]
        need(q, toks)

    def note(tk, reads, writes):
        for key in reads:
            rd.setdefault(key, []).append(tk)
        for key in writes:
            wr[key] = [tk]
            rd[key] = []

    def op(qs, fn, reads, writes, hold, sem=None, n=1, last=None):
        if len(qs) == 1:
            fn, hold = {qs: fn}, {qs: hold}

        def emit(q):
            deps(q, reads, writes)
            s = sem or semof[q]
            fn[q]().then_inc(T.sem[s], n)
            count[s] = count.get(s, 0) + n
            ck = dict(clock[q])
            ck[s] = count[s]
            note((s, count[s], ck, q), reads, writes)
        nodes.append((qs, emit, reads, writes, hold, min(hold.values()) if last is None else last))

    def arrives(sem, n, after, keys, last):
        nodes.append(("r", lambda q: note((sem, n, {sem: n}, "r"), [], keys), after, keys, {"r": 0.0}, last))

    def send(transfers, reads, mark):
        def emit(q):
            deps("g", reads, [])
            g.remote_dma_fused([t[0] for t in transfers], local_sem=T.sem.ls)
            count["ls"] = count.get("ls", 0) + sum(t[1] for t in transfers)
        nodes.append(("g", emit, reads, [mark], {"g": ISSUE}, 0.01))

    def xfer(src, dsts, es, sem):
        ids = [DstId(rid=topo.addr(c)[0], pnc=topo.addr(c)[1]) for c, _ in dsts]
        return (RemoteDMATransfer(dst_ids=ids, dma_engine_mask=bits(es), remote_sem=T.sem[sem],
                                  srcs=[src], dsts=[v for _, v in dsts]), len(es))

    V, S, P = g.vector, g.scalar, g.tensor
    ID, W0, W1, W2 = ACT.Identity, 0.064, 0.128, 0.256

    def gat(n):
        return 0.05 + n * 1.3e-3

    def ts(out, in0, s1, s2, o0, o1, r, w, c=W0):
        if o1 is None:
            op("v", lambda: V.tensor_scalar(out, in0, s1, None, o0), r, w, c)
        else:
            op("v", lambda: V.tensor_scalar(out, in0, s1, s2, o0, o1), r, w, c)

    def tt(out, a, b, o, r, w, c=W0):
        op("v", lambda: V.tensor_tensor(out, a, b, o), r, w, c)

    def cp(out, a, r, w, c=W0):
        op("v", lambda: V.tensor_copy(out, a), r, w, c)

    def red(out, a, o, r, w):
        op("v", lambda: V.tensor_reduce(out, a, X, o), r, w, W0)

    def tr(out, a, r, w, c=W0):
        op("v", lambda: V.transpose(out, a), r, w, c)

    def ms(out, v, w, c=W0):
        op("v", lambda: V.memset(out, v), [], w, c)

    def scan(out, a, b, init, o0, o1, r, w, c=W0):
        op("v", lambda: V.tensor_tensor_scan(out, a, b, init, o0, o1), r, w, c)

    def av(out, a, func, scale, bias, r, w, c=W0, acc=None):
        op("a", lambda: S.activation(out, a, func, bias=bias, scale=scale, accum_out=acc), r, w, c)

    def af(out, a, scale, bias, r, w, c=W0):
        op("va", {"v": lambda: V.tensor_scalar(out, a, scale, bias, MUL, ADD),
                  "a": lambda: S.activation(out, a, ID, bias=bias, scale=scale)}, r, w, {"v": c, "a": c + SX})

    def move(out, a, r, w, c=W0):
        op("va", {"v": lambda: V.tensor_copy(out, a), "a": lambda: S.activation(out, a, ACT.Copy)}, r, w,
           {"v": c, "a": c + SX})

    def quant(name, a, b, src, r, w):
        op("v", lambda: V.quantize_mx(T[name + "c"][:, a:b], T[name + "s"][:, a:b], src), r, w, 0.015 + (b - a) * 1.05e-3)

    def pick(dn, a, b, sn, c, d, off, rc, rs, wc, ws):
        cp(T[dn + "c"][:, a:b].bitcast(dt.uint32), T[sn + "c"][:, c:d].bitcast(dt.uint32).indirect(off), rc, wc, gat(b - a))
        op("a", lambda: S.activation(T[dn + "s"][:, a:b], T[sn + "s"][:, c:d].indirect(off), ACT.Copy), rs, ws,
           gat(b - a) + 0.015)

    def mm(bank, ln, la, rn, ra, n, start, stop, r, w=()):
        op("p", lambda: P.matmul_mx(T[bank][:, 0:n], T[ln + "c"][:, la:la + 128], T[ln + "s"][:, la:la + 128],
                                    T[rn + "c"][:, ra:ra + n], T[rn + "s"][:, ra:ra + n], start, stop),
           r, ["P" + bank] + list(w), (n + 16) * 6e-4)

    def dma(q, out, src, r, w, sem, last=LOAD):
        op(q, lambda: queues[q].dma_start(out, src), r, w, 0.05, sem, 16, last)

    def bytes_of(name, a, b):
        return T[name + "c"][:, a:b].bitcast(dt.uint8)

    def iota(out, pat, base, cm, w, n, small=True):
        if small:
            op("g", lambda: g.iota(out, pat, base, cm, allow_small_or_imprecise_dtypes=True), [], w, 0.16 + 2e-3 * n)
        else:
            op("g", lambda: g.iota(out, pat, base, cm), [], w, 0.16 + 2e-3 * n)

    cols = {}

    def c_(name, w=1, rows=slice(0, 128), j=None):
        if name not in cols:
            cols[name] = (sum(v[1] for v in cols.values()), w)
        at, w = cols[name]
        return T.sm[rows, at:at + w] if j is None else T.sm[rows, at + j:at + j + 1]

    def quad(a):
        return slice(32 * a, 32 * a + 32)

    def four(w):
        return [w + str(a) for a in range(4)]

    EL, AL = T.cu[:, 2:4], T.cu[:, 4:5]

    for j, last in enumerate((1.75, 2.3, 3.0)):
        dma("a", T.dtile[:, 4 * PW * j:4 * PW * j + 4 * PW], T.d[:, 4 * PW * j:4 * PW * j + 4 * PW],
            ["#d%d" % (j - 1)] * (j > 0), ["dt%d" % j, "#d%d" % j], "ld%d" % j, last)
    dma("s", T.xs[:], T.x[:], [], ["xs", "#x"], "lx", 1.95)
    dma("s", T.bt[:], T.b[:], ["#x"], ["bt", "#b"], "lb", 2.5)
    dma("s", T.acti[ka:ka + 16, :], T.act[:], ["#b"], ["actia"], "la", 3.1)
    dma("s", T.acti[ka + 16:kb, :], T.act[:], ["#b"], ["actib"], "la", 3.1)
    arrives("la", 32, ["actia", "actib"], ["acti"], 0.0)

    iota(T.si[:, 0:1], [[1, 1]], 0, 1, ["pi"], 1, False)
    iota(T.jd[:], [[1, 128]], 0, -1, ["jd"], 128)
    iota(T.j2[:], [[0, 4], [1, 32]], ka, -1, ["j2"], 128)
    iota(T.ci[:], [[1, 128]], 0, 0, ["ci"], 128, False)
    iota(T.k8[:], [[-A, N]], A * (N - 1), 0, ["k8"], 8)
    iota(T.p8[:], [[-32, G], [0, 2]], 32 * (G - 1), 0, ["p8"], 8)
    ms(T.et[:], 0.0, ["et"], W2)
    ms(T.ua[:], 0.0, ["ua"], W2)
    ms(T.ub[:], 0.0, ["ub"], W2)
    ms(T.zb[:], 0.0, ["zb"], 0.19)
    ms(T.nn0[:], 0.0, ["nn0"])
    ms(T.nbw[:, 8:40], 1.0, ["nbc"])
    ms(T.khw[:, 8:40], 0.0, ["khc"])
    ms(T.qq[:, 34:66], 0.0, ["qqz"])
    ms(T.cpw[:, 0:34], -BIG, ["cpc"])
    ms(T.c32[:], -32.0 / PU, ["c32"], W1)
    for s in range(4):
        ms(T.sbk[:, 32 * s:32 * s + 32], float(s), ["sbk%d" % s])
    av(T.ad[:], T.jd[:], ACT.Abs, 1.0, 0.0, ["jd"], ["ad"], W1)
    av(T.ua[:, 2:514:4], T.ad[:], ACT.Relu, -1.0, 0.25, ["ad"], ["ua"], W1)
    av(T.ub[:, 3:515:4], T.ad[:], ACT.Relu, -1.0, 0.25, ["ad"], ["ub"], W1)
    av(T.na[:], T.ua[:], ID, -1.0, 0.0, ["ua"], ["na"], 0.52)
    av(T.nb[:], T.ub[:], ID, -1.0, 0.0, ["ub"], ["nb"], 0.52)
    av(T.aj[:], T.j2[:], ACT.Abs, 1.0, 0.0, ["j2"], ["aj"], W1)
    av(T.d4[:], T.aj[:], ACT.Relu, -1.0, 1.0, ["aj"], ["d4"], W1)
    av(T.kp4[:], T.aj[:], ACT.Sign, 1.0, 0.0, ["aj"], ["kp4"], W1)
    av(T.tm[:], T.j2[:, 0:32], ACT.Relu, BIG, BIG, ["j2"], ["tm"])
    for neg in range(2):
        for b in range(4):
            src = (("ua", "ub"), ("na", "nb"))[neg][b % 2]
            st, at = 2 if b < 2 else 0, 512 * neg + 128 * b
            quant("ee", at, at + 128, T[src][:, st:st + 512], [src], ["ee%d" % (4 * neg + b)])
    PI = T.si[:, 0:1]
    ts(T.si[:, 1:2], PI, 31, None, AND, None, ["pi"], ["p31"])
    ts(T.si[:, 2:3], PI, 15, None, AND, None, ["pi"], ["p15"])
    ts(T.si[:, 3:4], PI, 3, None, AND, None, ["pi"], ["p3"])
    ts(T.si[:, 4:5], PI, 4, 1, SHR, AND, ["pi"], ["pg"])
    ts(T.si[:, 5:6], PI, 2, 3, SHR, AND, ["pi"], ["pq"])
    cp(c_("pf", 5), T.si[:, 1:6], ["p31", "p15", "p3", "pg", "pq"], ["pf"])
    P31, P15, P3, PG, PQ = [c_("pf", j=j) for j in range(5)]
    P15Q = c_("pf", rows=Q0, j=1)
    cp(T.cu[:, 2:3], P15, ["pf"], ["ELa"])
    ts(T.cu[:, 3:4], P15, 16.0, None, ADD, None, ["pf", "ELa"], ["EL"])
    ts(AL, P3, 2.0, PG, MUL, ADD, ["pf"], ["AL"])
    av(c_("off2"), P15, ID, -ZU, 15 * ZU, ["pf"], ["off2"])
    av(c_("off3"), P15, ID, -ZU, 15 * ZU + HI - own0, ["pf"], ["off3"])
    av(c_("ic"), P31, ID, 1.0 / PU, P15, ["pf"], ["ic"])
    av(c_("ip"), P31, ID, 1.0 / PU, P3, ["pf"], ["ip"])
    av(c_("d153"), P3, ID, -1.0, P15, ["pf"], ["d153"])
    av(c_("thr"), P15, ID, 1.0, 0.25, ["pf"], ["thr"])
    av(c_("c4"), P3, ID, -0.25 / PU, PQ, ["pf"], ["c4c"])
    av(T.qq[:, 32:33], P3, ID, 1.0, -(CAPP - 0.5), ["pf"], ["qqc"])
    av(c_("plw", 8), T.p8[:], ID, 1.0 / PU, c_("ip"), ["p8", "ip"], ["plw"])
    ts(T.cj[:], T.ci[:], 15, None, AND, None, ["ci"], ["cj"], W1)
    ts(T.c4[:], T.ci[:, 0:32], 3, None, AND, None, ["ci"], ["c4"])
    ts(T.cw[:], T.ci[:], 128.0, 1.0 / PU, ADD, MUL, ["ci"], ["cw"], W1)
    ts(T.msel[:], T.cj[:, 0:64], P15, None, NE, None, ["cj", "pf"], ["msel"])
    ts(T.cu1[:], T.cj[:], P15, -BIG, NE, MUL, ["cj", "pf"], ["cu1"], W1)
    ts(T.u4[:, 0:32], T.c4[:], PQ, -BIG, NE, MUL, ["c4", "pf"], ["u4a"])
    av(T.u4[:, 32:64], T.cw[:, 0:32], ID, 1.0, PQ, ["cw", "pf"], ["u4b"])
    tt(T.cap4[:], T.u4[:, 0:32], T.u4[:, 32:64], ADD, ["u4a", "u4b"], ["cap4"])
    av(T.n1[:], T.cw[:], ID, 1.0, P15, ["cw", "pf"], ["n1"], W1)
    tt(T.caps[:], T.cu1[:], T.n1[:], ADD, ["cu1", "n1"], ["caps"], W2)

    def send_e(t, after):
        es = topo.engines(core, peers[0])
        n = "qe%d" % t
        calls = [xfer(bytes_of(n, ka, kb), [(c, bytes_of("eg%d" % t, ka, kb)) for c in peers], es, "ae%d" % t),
                 xfer(T[n + "s"][:, ka:kb], [(c, T["eg%ds" % t][:, ka:kb]) for c in peers], es, "ae%d" % t)]
        if t == 0:
            calls.reverse()
        send(calls[:1], [n] + after, "#ea%d" % t)
        send(calls[1:], [n, "#ea%d" % t], "#eb%d" % t)
        arrives("ae%d" % t, 2 * len(es) * len(peers), ["#eb%d" % t], ["eg%d.r" % t], HOP + (1.0 if t == 0 else 0))
        pick("eg%d" % t, ka, kb, n, ka, kb, EL, ["EL", n], ["EL", n], ["eg%d.c" % t], ["eg%d.s" % t])

    def copies(t):
        xw, key = T["xw%d" % t], "xr%d" % t
        av(xw[:, 640:768], xw[:, 512:640], ID, 1.0, 0.0, [key + "a"], [key + "b"], W1)
        av(xw[:, 768:1024], xw[:, 512:768], ID, 1.0, 0.0, [key + "a", key + "b"], [key + "c"], W2)

    ET = T.et[:, 128 * k:128 * k + 128]
    tt(ET, T.bt[:], T.xs[:], SUB, ["bt", "xs"], ["et"], W2)
    quant("qe0", 0, 128, T.et[:], ["et"], ["qe0"])
    av(T.xw0[:, 512:640], T.xs[:], ID, -1.0, 0.0, ["xs"], ["xr0a"], W1)
    copies(0)
    es = topo.engines(core, mate)
    half = len(es) // 2
    ato = ["at.%d" % j for j in range(NP)]

    def piece(j, engines, after):
        a, b = own0 + PW * j, own0 + PW * j + PW
        quant("at", a, b, T.dtile[:, 4 * PW * j:4 * PW * j + 4 * PW], ["dt%d" % j] + ato[j - 1:j], [ato[j]])
        send([xfer(bytes_of("at", a, b), [(mate, bytes_of("at", a, b))], engines, "aa")], [ato[j]] + after, "#a%d" % j)

    piece(0, es[:half], [])
    piece(1, es[half:], ["#a0"])
    send_e(0, ["#a1"])
    piece(2, es, ["#eb0"])
    send([xfer(T.ats[:, own0:own0 + A], [(mate, T.ats[:, own0:own0 + A])], es, "aa")], ato + ["#a2"], "#as")
    arrives("aa", 3 * len(es), ["#as"], ["at.r"], 1.7)

    for a in range(4):
        cp(T.af[quad(a), :], T.acti[Q0, :], ["acti"], ["af%d" % a])
    cp(T.aoff[:], T.af[:], four("af"), ["aoff"])
    ts(T.ae0[:], T.af[:].indirect(AL), float(A * rank), None, ADD, None, four("af") + ["AL"], ["ae0"], gat(16))
    pick("win0", 128, 256, "at", own0, own0 + A, T.aoff[:], ["aoff"] + ato, ["aoff"] + ato, ["win0.sc"], ["win0.ss"])
    dma("s", T.wt[:], T.w[:], ["at.r"], ["wt"], "lw", 2.5)
    quant("wq", 0, 256, T.wt[:], ["wt"], ["wq"])

    def y_mm(w, a, keys):
        for o, bank in enumerate(("py", "pa")):
            mm(bank, "wq", 128 * o, w, a, 128, True, True, ["wq"] + keys)

    AS = T.asc[:, 31:128:32]
    for t in range(R):
        last = t == R - 1
        ml, mk, eg, w, pk, fa, xw = (T["ml%d" % t], "ml%d" % t, "eg%d" % t, "win%d" % t, "pk%d" % t, "fa%d" % t,
                                     T["xw%d" % t])
        ae, aek = (T.ae0[:, 0:4], "ae0") if t == 0 else (c_("ae%d" % t, 4), "ae%d" % t)
        mm("pa", "qe%d" % t, 0, w, 128, 128, True, True, ["qe%d" % t, w + ".sc", w + ".ss"])
        tt(T.am[:], T.pa[:, 0:128], T.d4[:], MUL, ["Ppa", "d4"], ["am"], W1)
        scan(T.asc[:], T.kp4[:], T.am[:], 0.0, MUL, ADD, ["kp4", "am"], ["asc"], W1)
        scan(c_("rm", 4), AS, T.zb[:, 0:4], 1.0e29, MIN, ADD, ["asc", "zb"], ["rm"])
        NS = c_("nslot")
        av(c_("sj", 4), c_("rm", 4), ACT.Sign, -1.0, c_("rm", j=3), ["rm"], ["nslot"], 0.084, NS)
        av(T.ab0[:], T.c32[:], ID, NS, c_("ic"), ["c32", "nslot", "ic"], ["ab0"], W1)
        av(T.n1[:], T.sbk[:], ACT.Abs, 1.0, NS, four("sbk") + ["nslot"], ["n1"], W1)
        av(T.nmb[:], T.n1[:], ID, BIG, c_("d153"), ["n1", "d153"], ["nmb"], W1)
        tr(T.ab1[:], T.ab0[:], ["ab0"], ["ab1"], W1)
        scan(T.ab2[:], T.caps[:], T.ab1[:], 0.0, MAX, MIN, ["caps", "ab1"], ["ab2"], W1)
        for a in range(4):
            ts(T.ao[quad(a), :], T.ab2[Q0, 15:128:16], P15Q, PU, SUB, MUL, ["ab2", "pf"], ["ao%d" % a])
        pick(fa, 0, 128, w, 128, 256, T.ao[:], four("ao") + [w + ".sc"], four("ao") + [w + ".ss"], [fa + "c"], [fa + "s"])
        for b in range(4):
            mm("pd%d" % b, "ee", 128 * b, fa, 0, 128, True, False, ["ee%d" % b, fa + "c", fa + "s"])
        red(c_("amax"), AS, MAX, ["asc"], ["amax"])
        ts(c_("tb", 4), AS, c_("amax"), BIG, LT, MUL, ["asc", "amax"], ["tb"])
        tt(c_("ub", 4), c_("tb", 4), ae, ADD, ["tb", aek], ["ub4"])
        red(c_("amaxe"), c_("ub", 4), MIN, ["ub4"], ["amaxe"])
        av(c_("ak8", 8), T.k8[:], ID, -1.0, c_("amaxe"), ["k8", "amaxe"], ["ak8"])
        if t > 0:
            y_mm(w, 128, [w + ".sc", w + ".ss"])
            for o, bank in enumerate(("py", "pa")):
                if t == 1:
                    av(T.ys0[:, 128 * o:128 * o + 128], T[bank][:, 0:128], ID, 1.0, 0.0, ["P" + bank], ["ys%d" % o], W1)
                else:
                    ys = T.yw[:, 256 * o + 128:256 * o + 256]
                    av(ys, T[bank][:, 0:128], ID, 1.0, 0.0, ["P" + bank], ["yw%d" % o], W1)
                    dma("s", T.y[:, 256 + 128 * o:384 + 128 * o], ys, ["yw%d" % o], [], "st")
            if t == 1:
                dma("s", T.y[:, 0:256], T.ys0[:], ["ys0", "ys1"], [], "st")
        halves = [("ps1", 0, "r1", A), ("ps2", HI, "r2", 0)]
        if own0:
            halves.reverse()
        for (bank, a0, _, _), key in zip(halves, (ato, ["at.r"])):
            mm(bank, eg, 0, "at", a0, A, True, True, [eg + ".c", eg + ".s", eg + ".r"] + key)
        M2, M1 = T.r21[:, A - 1:A], T.r21[:, 2 * A - 1:2 * A]
        m0 = 4 * (G - 1 - k)
        C2, C1 = ml[:, m0 + 1:m0 + 2], ml[:, m0 + 3:m0 + 4]
        for bank, _, rk, r0 in halves:
            scan(T.r21[:, r0:r0 + A], T[bank][:, 0:A], T.zb[:], -1.0e29, MAX, ADD, ["P" + bank, "zb"], [rk], A * 1e-3)
        for _, _, rk, r0 in halves:
            av(T.junk[:, r0:r0 + A], T.r21[:, r0:r0 + A], ACT.Sign, -1.0, T.r21[:, r0 + A - 1:r0 + A], [rk],
               [mk + "." + rk, "junk" + rk], A * 1e-3 + 0.02, C1 if r0 else C2)
        c1k, c2k = mk + ".r1", mk + ".r2"
        cp(ml[:, m0:m0 + 4:2], T.r21[:, A - 1:2 * A:A], ["r1", "r2"], [mk + ".m"])
        mine = [mk + ".m", c1k, c2k]
        mv = ml[:, m0:m0 + 4]
        send([xfer(mv, [(c, mv) for c in peers], topo.engines(core, peers[0]), "am%d" % t)], mine, "#m%d" % t)
        arrives("am%d" % t, sum(len(topo.engines(c, core)) for c in peers), ["#m%d" % t], [mk + ".r"], HOP - 0.15)
        CF, cfk, CL, clk = (C2, c2k, C1, c1k) if own0 else (C1, c1k, C2, c2k)
        ts(T.gb[:], T.zb[:, 0:64], M2, M1, ADD, LE if own0 else GT, ["zb", "r1", "r2"], ["gb"])
        ts(c_("gh"), M2, M1, None, GT if own0 else LE, None, ["r1", "r2"], ["gh"])
        ts(c_("gu"), c_("gh"), float(HI if own0 else -HI), c_("off3"), MUL, ADD, ["gh", "off3"], ["gu"])
        ts(c_("rest"), CF, c_("gh"), c_("gu"), MUL, ADD, ["gh", "gu", cfk], ["rest"])
        ts(T.z0[:], T.gb[:], CL, c_("rest"), MUL, ADD, ["gb", clk, "rest"], ["z0"])
        tr(T.z1[:], T.z0[:], ["z0"], ["z1"])
        scan(T.zy[:], T.msel[:], T.z1[:], 0.0, MUL, MAX, ["msel", "z1"], ["zy"] + four("zc"))
        for h in range(2):
            f, s = order[2 * h], order[2 * h + 1]
            move(T.zy[quad(s), 15:32:16], T.zy[quad(f), 15:32:16], ["zy"], ["zc%d" % (2 * h)])
            move(T.zy[quad(f), 47:64:16], T.zy[quad(s), 47:64:16], ["zy"], ["zc%d" % (2 * h + 1)])
        for h, a, b, zk in ((0, 0, 4, ["zc0", "zc1"]), (1, 0, 2, ["zc2"]), (1, 2, 4, ["zc3"])):
            src = slice(64 * (order[2 * h] // 2), 64 * (order[2 * h] // 2) + 64)
            for d in range(2):
                ts(T.ho[64 * d:64 * d + 64, 4 * h + a:4 * h + b], T.zy[src, 15 + 16 * a:16 * b:16], c_("off2", 1, src), None,
                   SUB, None, ["zy", "off2"] + zk, ["ho%d%d%d" % (h, a, d)])
        hk = ["ho000", "ho001", "ho100", "ho101", "at.r"] + ato
        pick(pk, 0, 96, "at", 0, AW, T.ho[:, 0:6], hk, hk, [pk + ".c"], [pk + ".s"])
        ec, esc = splits(topo.engines(core, peers[0]))
        send([xfer(bytes_of(pk, 32 * i, 32 * i + 32), [(grp[order[i]], bytes_of(w, ka, kb))], ec[i], "ac%d" % t)
              for i in range(3)], [pk + ".c", "#m%d" % t], "#c%d" % t)
        send([xfer(T[pk + "s"][:, 32 * i:32 * i + 32], [(grp[order[i]], T[w + "s"][:, ka:kb])], esc[i], "ac%d" % t)
              for i in range(3)], [pk + ".s", "#c%d" % t], "#s%d" % t)
        arrives("ac%d" % t, sum(len(splits(topo.engines(grp[s], core))[j][places(s).index(k)])
                                for s in range(G) if s != k for j in range(2)), ["#s%d" % t], [w + ".r"], HOP)
        hk = ["ho120", "ho121", "at.r"] + ato
        pick(w, ka, kb, "at", 0, AW, T.ho[:, 6:8], hk, hk, [w + ".oc"], [w + ".os"])
        cand = [w + ".oc", w + ".os", w + ".r"]
        for b in range(4):
            mm("pd%d" % b, "ee", 512 + 128 * b, w, 0, 128, False, True,
               ["ee%d" % (4 + b)] + cand + ["#f%d" % (b - 1)] * (b > 0), ["#f%d" % b])
        for b in range(4):
            tt(xw[:, b:512:4], T["pd%d" % b][:, 0:128], xw[:, 512 + b:1024:4], ADD,
               ["Ppd%d" % b] + ["xr%d%s" % (t, s) for s in "abc"], ["xc%d" % b], W1)
        allm = mine + [mk + ".r"]
        SC, CC = ml[:, 0:16:2], ml[:, 1:16:2]
        HN = T.qq[:, 33:34]
        EMW, CPW = c_("emw", 8), c_("cpo", 8)
        EM, CPO = c_("emw", j=7), c_("cpo", j=7)
        red(c_("best"), SC, MAX, allm, ["best"])
        tt(c_("h8", 8), CC, c_("ak8", 8), EQ, allm + ["ak8"], ["h8"])
        tt(c_("e8", 8), CC, T.k8[:], ADD, allm + ["k8"], ["e8"])
        ts(T.nbw[:, 0:8], SC, c_("best"), None, LT, None, allm + ["best"], ["nbw"])
        tt(T.khw[:, 0:8], c_("h8", 8), T.k8[:], ADD, ["h8", "k8"], ["khw"])
        scan(T.kho[:], T.nbw[:], T.khw[:], BIG, MUL, MAX, ["nbw", "nbc", "khw", "khc"], ["kho"])
        scan(EMW, T.nbw[:, 0:8], c_("e8", 8), BIG, MUL, MAX, ["nbw", "e8"], ["em"])
        scan(CPW, T.nbw[:, 0:8], c_("plw", 8), BIG, MUL, MAX, ["nbw", "plw"], ["cpo"])
        tr(T.kt[:], T.kho[:, 8:40], ["kho"], ["kt"])
        av(T.kp[:], T.tm[:], ID, 1.0, T.kho[:, 39:40], ["kho", "tm"], ["kp"])
        av(T.cpw[:, 34:66], T.zb[:, 0:32], ID, 1.0, CPO, ["zb", "cpo"], ["cpw"])
        ts(HN, EM, c_("amaxe"), -64.0, EQ, MUL, ["em", "amaxe"], ["hn"])
        tt(T.qq[:, 0:32], T.kt[:], T.kp[:], EQ, ["kt", "kp"], ["qq"])
        scan(T.vv[:], T.qq[:], T.cpw[:], 0.0, ADD, MAX, ["qq", "qqc", "qqz", "hn", "cpc", "cpw"], ["vv"], 0.066)
        tr(T.fb1[:], T.vv[:, 34:66], ["vv"], ["fb1"])
        scan(T.fb2[:], T.cap4[:], T.fb1[:], 0.0, MAX, MIN, ["cap4", "fb1"], ["fb2"])
        for a in range(4):
            ts(T.fo[quad(a), :], T.fb2[Q0, 3:32:4], c_("c4", 1, Q0), 4 * PU, SUB, MUL, ["fb2", "c4c"], ["fo%d" % a])
        xk = four("fo") + four("xc") + ["xr%da" % t]
        XN = xw[:, 0:640].indirect(T.fo[:])
        if not last:
            tt(ET, XN, T.bt[:], ADD, xk + ["bt"], ["et"], gat(128))
            quant("qe%d" % (t + 1), 0, 128, T.et[:], ["et"], ["qe%d" % (t + 1)])
            send_e(t + 1, [])
            av(T["xw%d" % (t + 1)][:, 512:640], XN, ID, 1.0, 0.0, xk, ["xr%da" % (t + 1)], gat(128))
            copies(t + 1)
        else:
            af(T.pxs[:], XN, -1.0, 0.0, xk, ["pxs"], gat(128))
            dma("s", T.px[:], T.pxs[:], ["pxs"], [], "st", 1.9)
        w2 = "win%d" % (t + 1)
        ts(T.zs0[:], T.nmb[:], T.vv[:, 65:66], HN, ADD, SUB, ["nmb", "vv", "hn"], ["zs0"], W1)
        tr(T.zs1[:], T.zs0[:], ["zs0"], ["zs1"], W1)
        scan(T.zs2[:], T.caps[:], T.zs1[:], 0.0, MAX, MIN, ["caps", "zs1"], ["zs2"], W1)
        for a in range(4):
            ts(T.so[quad(a), :], T.zs2[Q0, 15:128:16], P15Q, PU, SUB, MUL, ["zs2", "pf"], ["so%d" % a])
        pick(w2, 128, 256, w, 0, 256, T.so[:], four("so") + [w + ".sc", w + ".oc", w + ".r"],
             four("so") + [w + ".ss", w + ".os", w + ".r"], [w2 + ".sc"], [w2 + ".ss"])
        av(c_("de", 4), ae, ID, -1.0, EM, [aek, "em"], ["de"])
        ts(c_("m2", 4), T.zs0[:, 0:128:32], c_("thr"), None, LT, None, ["zs0", "thr"], ["m2"])
        tt(c_("dd", 4), c_("m2", 4), c_("de", 4), MUL, ["m2", "de"], ["dd"])
        if not last:
            tt(c_("ae%d" % (t + 1), 4), ae, c_("dd", 4), ADD, [aek, "dd"], ["ae%d" % (t + 1)])
        else:
            tt(T.nn0[:, 0:4], ae, c_("dd", 4), ADD, [aek, "dd"], ["nn0"])
            tr(T.nn1[:], T.nn0[:], ["nn0"], ["nn1"])
            dma("s", T.an[:], T.nn1[ka:ka + 4, :], ["nn1"], [], "st", 2.2)
            dma("s", T.oc[:], bytes_of(w2, 128, 256), [w2 + ".sc"], [], "st", 2.0)
            for a in range(4):
                dma("sa"[a // 2], T.osc[4 * a:4 * a + 4, :], T[w2 + "s"][32 * a:32 * a + 4, 128:256], [w2 + ".ss"], [], "st")
            y_mm(w, 0, cand)
            for o, bank in enumerate(("py", "pa")):
                move(T.yw[:, 256 * o:256 * o + 128], T[bank][:, 0:128], ["P" + bank], ["yc%d" % o], W1)
                af(T.yo[:, 128 * o:128 * o + 128], T.yw[:, 256 * o:256 * o + 256].indirect(T.so[:]), 1.0, 0.0,
                   four("so") + ["yc%d" % o, "yw%d" % o], ["yo%d" % o], gat(128))
                dma("a", T.y[:, 512 + 128 * o:640 + 128 * o], T.yo[:, 128 * o:128 * o + 128], ["yo%d" % o], [], "st",
                    2.3 - 0.2 * o)
    assert sum(v[1] for v in cols.values()) <= 128

    for j, q in arrange(nodes):
        nodes[j][1](q)
    for s in ("sv", "sa", "sp", "sg", "ls"):
        g.wait_ge(T.sem[s], count[s])
    g.sync.wait_ge(T.sem.st, count["st"])
